import numpy as np
import ml_dtypes


def mxq(x, axis, fmt="e4m3"):
    dtype, down = {"e4m3": (ml_dtypes.float8_e4m3fn, 7), "e5m2": (ml_dtypes.float8_e5m2, 14)}[fmt]
    v = np.moveaxis(np.asarray(x, np.float32).astype(ml_dtypes.bfloat16).astype(np.float64), axis, -1)
    blocks = v.reshape(v.shape[:-1] + (-1, 32))
    amax = np.abs(blocks).max(-1, keepdims=True)
    byte = np.maximum(np.where(amax > 0, np.frexp(amax)[1] - 1 + 127, 0) - down, 1)
    scale = np.exp2(byte - 127.0)
    codes = (blocks / scale).astype(np.float32).astype(dtype).astype(np.float64)
    return np.moveaxis((codes * scale).reshape(v.shape), -1, axis)


WIDE = False


def mx_kscale(k):
    if not WIDE:
        return np.ones(k)
    levels = np.array([10, -10, 5, -5, 0])
    if k % 512:
        return np.exp2(np.random.permutation(np.resize(levels, k // 32))).repeat(32)
    a = np.empty((k // 512, 16))
    for p in range(k // 512):
        a[p, :8] = np.random.permutation(np.resize(levels, 8))
        for g in range(8):
            far = levels[np.abs(levels - a[p, g]) >= 10]
            a[p, g + 8] = far[np.random.randint(len(far))]
    return np.exp2(a.ravel()).repeat(32)


def f64(x):
    return np.asarray(x).astype(np.float64)


def striped(idx):
    return np.tile(idx.reshape(-1, 16).T, (8, 1)).astype(np.uint16)


def unstriped(offs):
    return offs[:16].T.reshape(-1).astype(np.int64)


E2M1 = np.array([0.0, 0.5, 1.0, 1.5, 2.0, 3.0, 4.0, 6.0, -0.0, -0.5, -1.0, -1.5, -2.0, -3.0, -4.0, -6.0])


def pack_weight(w, fmt):
    k, n = w.shape
    w = f64(np.asarray(w, np.float32).astype(ml_dtypes.bfloat16)).reshape(k // 32, 32, n)
    amax = np.abs(w).max(1)
    if fmt == "e4m3":
        byte = np.frexp(amax)[1] - 1 + 127 - 7
    else:
        mant, ex = np.frexp(amax / 6.0)
        byte = np.where(mant > 0.5, ex, ex - 1) + 127
    byte = np.clip(np.where(amax > 0, byte, 1), 1, 254)
    scaled = (w * np.exp2(127.0 - byte)[:, None, :]).reshape(k, n).astype(np.float32)
    by_word = np.ascontiguousarray(scaled.reshape(k // 512, 128, 4, n).transpose(0, 1, 3, 2))
    if fmt == "e4m3":
        words = by_word.astype(ml_dtypes.float8_e4m3fn).view(np.uint8)
    else:
        c = by_word.astype(ml_dtypes.float4_e2m1fn).view(np.uint8) & 0xF
        words = (c[..., 0::2] | (c[..., 1::2] << 4)).reshape(k // 512, 128, 2 * n)
    return np.ascontiguousarray(words), np.ascontiguousarray(byte.astype(np.uint8).reshape(k // 512, 16, n))


def unpack_weight(words, scales, fmt):
    g, _, n = scales.shape
    words = np.ascontiguousarray(words).reshape(g, 128, n, -1)
    if fmt == "e4m3":
        vals = words.view(ml_dtypes.float8_e4m3fn).astype(np.float64)
    else:
        nib = np.empty((g, 128, n, 4), np.uint8)
        nib[..., 0::2] = words & 0xF
        nib[..., 1::2] = words >> 4
        vals = E2M1[nib]
    vals = vals * np.repeat(np.exp2(scales.astype(np.float64) - 127.0), 8, axis=1)[..., None]
    return vals.transpose(0, 1, 3, 2).reshape(g * 512, n)


def gelu(v):
    return 0.5 * v * (1.0 + np.tanh(np.sqrt(2.0 / np.pi) * (v + 0.044715 * v**3)))


def often(T, S):
    return np.random.permutation(T)[(T * np.random.uniform(0, 1, S) ** 4).astype(np.int64)]


K, K2, T, S, H, N = 1024, 512, 4096, 1024, 1024, 512


def setup_inputs():
    n = np.random.standard_normal
    s = mx_kscale(K)[:, None]
    s2 = mx_kscale(K2)[:, None]
    u = mx_kscale(H)[:, None]
    tab_words, tab_scales = pack_weight(n((K, T)) * s, "e4m3")
    tab2_words, tab2_scales = pack_weight(n((K2, T)) * s2, "e2m1")
    wa_words, wa_scales = pack_weight(n((K, N)) / np.sqrt(K) / s, "e2m1")
    wr_words, wr_scales = pack_weight(n((K2, H)) / np.sqrt(K2) / s2 * u.T, "e4m3")
    return {
        "tab_words": tab_words, "tab_scales": tab_scales,
        "tab2_words": tab2_words, "tab2_scales": tab2_scales,
        "offs": striped(often(T, S)),
        "offs2": striped(often(T, S)),
        "wa_words": wa_words, "wa_scales": wa_scales,
        "wr_words": wr_words, "wr_scales": wr_scales,
        "wm": (0.45 * n((K, H)) / np.sqrt(K) / s).astype(np.float32),
        "wn": (0.7 * n((H, N)) / np.sqrt(H) / u).astype(np.float32),
        "gain": (np.random.uniform(1.0, 2.0, H) * u[:, 0]).astype(np.float32),
        "drift": (0.5 * n(N)).astype(np.float32),
    }


def reference(tab_words, tab_scales, tab2_words, tab2_scales, offs, offs2,
              wa_words, wa_scales, wr_words, wr_scales, wm, wn, gain, drift):
    v = unpack_weight(tab_words, tab_scales, "e4m3")[:, unstriped(offs)]
    v2 = unpack_weight(tab2_words, tab2_scales, "e2m1")[:, unstriped(offs2)]
    wa = unpack_weight(wa_words, wa_scales, "e2m1")
    wr = unpack_weight(wr_words, wr_scales, "e4m3")
    phase = mxq(f64(wm), 0, "e4m3").T @ v
    rate = wr.T @ v2
    h = rate - f64(gain)[:, None] * np.sin(phase)
    hq = mxq(h, 0, "e4m3")
    angle = wa.T @ v + mxq(f64(wn), 0, "e4m3").T @ hq
    return angle + f64(drift)[:, None]

@@ -1,0 +1,307 @@
+from contextlib import ExitStack
+
+import concourse.mybir as mybir
+
+K, K2, T, S, H, N = 1024, 512, 4096, 1024, 1024, 512
+FLOPS = 2 * S * (K * H + K2 * H + K * N + H * N)
+
+F32 = mybir.dt.float32
+BF16 = mybir.dt.bfloat16
+I32 = mybir.dt.int32
+U32 = mybir.dt.uint32
+U16 = mybir.dt.uint16
+U8 = mybir.dt.uint8
+FP8X4 = mybir.dt.float8_e4m3fn_x4
+FP4X4 = mybir.dt.float4_e2m1fn_x4
+ACT = mybir.ActivationFunctionType
+ALU = mybir.AluOpType
+
+P = 128
+PACK = 4
+KP = P * PACK
+NT = 512
+TAB1_AT = 4 * 4 * PACK * KP
+LATE_BYTES = 4 * 4 * PACK * KP + 4 * T + 2 * T + 2 * 4 * PACK * N + 2 * 4 * KP + 4 * N + 2 * 64
+
+
+def tile_list_attitude_propagation_kernel(
+    tc, tab_words, tab_scales, tab2_words, tab2_scales, offs, offs2,
+    wa_words, wa_scales, wr_words, wr_scales, wm, wn, gain, drift, out,
+):
+    nc = tc.nc
+    with ExitStack() as ctx:
+        keep = ctx.enter_context(tc.tile_pool(name="keep", bufs=1))
+        ring = ctx.enter_context(tc.tile_pool(name="ring", bufs=2))
+        psum = ctx.enter_context(tc.psum_pool(name="psum", bufs=1))
+
+        def held(shape, dtype, name):
+            return keep.tile(shape, dtype, name=name, align_bytes=64)
+
+        late = ctx.enter_context(tc.tile_pool(name="late", bufs=1))
+        used = [4 * PACK * KP]
+
+        def late_tile(shape, dtype, name, nbytes):
+            tile = late.tile(shape, dtype, name=name, align_bytes=64, offset=used[0])
+            used[0] = used[0] + nbytes
+            return tile
+
+        first = late.tile([P, LATE_BYTES // 4], F32, name="first", align_bytes=64, offset=0)
+        zero_in = late.tile([P, (64 + 5 * T) // 4], F32, name="zero_in", align_bytes=64, offset=LATE_BYTES)
+        idx = keep.tile([P, S // 16], U16, name="idx")
+        idx2 = keep.tile([P, S // 16], U16, name="idx2")
+        wm_raw = [
+            [first[:, 0 : PACK * KP].rearrange("p (j c) -> p j c", j=PACK) if (a, b) == (0, 0)
+             else late_tile([P, PACK, KP], F32, "wm_raw%d%d" % (b, a), 4 * PACK * KP) for a in range(2)]
+            for b in range(2)]
+        tab_w = [
+            late.tile([P, T], I32, name="tab_w0", align_bytes=64, offset=LATE_BYTES + 64),
+            late_tile([P, T], I32, "tab_w1", 4 * T)]
+        tab_s = held([P, T], U8, "tab_s")
+        tab2_w = late_tile([P, T // 2], I32, "tab2_w", 2 * T)
+        tab2_s = late.tile([P, T], U8, name="tab2_s", align_bytes=64, offset=LATE_BYTES + 64 + 4 * T)
+        wn_raw = [late_tile([P, PACK, N], F32, "wn_raw%d" % b, 4 * PACK * N) for b in range(2)]
+        wr_raw = [late_tile([P, KP], I32, "wr_raw%d" % b, 4 * KP) for b in range(2)]
+        wr_s_raw = held([P, H], U8, "wr_s_raw")
+        wa_w = late_tile([P, 2, 2 * N], U8, "wa_w", 4 * N)
+        wa_s = held([P, 2, N], U8, "wa_s")
+        gain_sb = late_tile([P, 2, PACK], F32, "gain_sb", 64)
+        drift_sb = late_tile([P, N // P], F32, "drift_sb", 64)
+        assert used[0] == LATE_BYTES
+        v_s1 = held([P, S], U8, "v_s1")
+        zero = held([P, 1], F32, "zero")
+
+        nc.vector.memset(tab_s[:].bitcast(I32), 0)
+        nc.gpsimd.memset(zero_in[:, 0:1], 0.0)
+        nc.scalar.activation(zero[:], zero_in[:, 0:1], ACT.Sin)
+        nc.vector.memset(tab2_s[:].bitcast(I32), 0)
+        nc.gpsimd.memset(wr_s_raw[:].bitcast(I32), 0)
+        nc.gpsimd.memset(wa_s[:].rearrange("p a n -> p (a n)").bitcast(I32), 0)
+        nc.gpsimd.memset(v_s1[:].bitcast(I32), 0)
+
+        def load_wm(b, a):
+            rows = wm[KP * a : KP * (a + 1), KP * b : KP * (b + 1)]
+            nc.sync.dma_start(wm_raw[b][a][:], rows.rearrange("(p j) c -> p j c", j=PACK))
+
+        def load_wn(b):
+            rows = wn[KP * b : KP * (b + 1), :]
+            nc.sync.dma_start(wn_raw[b][:], rows.rearrange("(p t) n -> p t n", t=PACK))
+
+        def load_tab(a):
+            nc.sync.dma_start(tab_w[a][:], tab_words[a].rearrange("p t i -> p (t i)").bitcast(I32))
+
+        def load_wr(b):
+            words = wr_words[0].rearrange("p c i -> p (c i)").bitcast(I32)
+            nc.sync.dma_start(wr_raw[b][:], words[:, KP * b : KP * (b + 1)])
+
+        nc.sync.dma_start(idx[:], offs)
+        nc.sync.dma_start(idx2[:], offs2)
+        load_wm(0, 0)
+        for q in range(4):
+            nc.sync.dma_start(
+                tab_s[32 * q : 32 * q + 8, :].bitcast(I32), tab_scales[:, 4 * q : 4 * q + 4, :].bitcast(I32))
+        load_tab(0)
+        for q in range(4):
+            nc.sync.dma_start(
+                tab2_s[32 * q : 32 * q + 4, :].bitcast(I32), tab2_scales[0, 4 * q : 4 * q + 4, :].bitcast(I32))
+        load_wm(0, 1)
+        load_tab(1)
+        nc.sync.dma_start(gain_sb[:], gain.rearrange("(b p t) -> p b t", b=2, t=PACK))
+        nc.sync.dma_start(tab2_w[:], tab2_words[0].bitcast(I32))
+        load_wr(0)
+        load_wm(1, 0)
+        load_wm(1, 1)
+        load_wr(1)
+        load_wn(0)
+        nc.sync.dma_start(wa_w[:].bitcast(I32), wa_words.bitcast(I32).rearrange("a p c -> p a c"))
+        load_wn(1)
+        with nc.allow_non_contiguous_dma(reason="one drift value a partition"):
+            nc.sync.dma_start(drift_sb[:], drift.rearrange("(c p) -> p c", p=P))
+
+        for q in range(4):
+            nc.gpsimd.dma_start(
+                wr_s_raw[32 * q : 32 * q + 4, :].bitcast(I32), wr_scales[0, 4 * q : 4 * q + 4, :].bitcast(I32))
+        for q in range(4):
+            nc.gpsimd.dma_start(
+                wa_s[32 * q : 32 * q + 4, :, :].bitcast(I32),
+                wa_scales[:, 4 * q : 4 * q + 4, :].bitcast(I32).rearrange("a r n -> r a n"))
+
+        v_s = held([P, S], U8, "v_s")
+        v_w0 = held([P, S], U32, "v_w0")
+        v_w1 = [held([P, NT], U32, "v_w1%d" % j) for j in range(2)]
+        v2_s = held([P, S], U8, "v2_s")
+        v2_w = [late.tile([P, 2 * NT], U8, name="v2_w%d" % j, align_bytes=64, offset=TAB1_AT + 2 * NT * j)
+                for j in range(2)]
+        half = NT // 16
+
+        wm_bf = [[held([P, KP * PACK], BF16, "wm_bf%d%d" % (b, a)) for a in range(2)] for b in range(2)]
+        wm_c = [[held([P, KP], U32, "wm_c%d%d" % (b, a)) for a in range(2)] for b in range(2)]
+        wm_s = [[held([P, KP], U8, "wm_s%d%d" % (b, a)) for a in range(2)] for b in range(2)]
+        wn_bf = [held([P, N * PACK], BF16, "wn_bf%d" % b) for b in range(2)]
+        wn_c = [held([P, N], U32, "wn_c%d" % b) for b in range(2)]
+        wn_s = [held([P, N], U8, "wn_s%d" % b) for b in range(2)]
+        wr_c = [late.tile([P, KP], I32, name="wr_c%d" % b, align_bytes=64, offset=TAB1_AT + 4 * NT + 4 * KP * b)
+                for b in range(2)]
+        wr_s = late.tile([P, H], U8, name="wr_s", align_bytes=64, offset=LATE_BYTES + 64)
+        h_c = [[held([P, NT], U32, "h_c%d%d" % (b, j)) for j in range(2)] for b in range(2)]
+        h_s = [[held([P, NT], U8, "h_s%d%d" % (b, j)) for j in range(2)] for b in range(2)]
+
+        def cast_wm(b, a):
+            nc.scalar.copy(
+                wm_bf[b][a][:].rearrange("p (t m j) -> p m t j", t=PACK, j=PACK),
+                wm_raw[b][a][:].rearrange("p j (m t) -> p m t j", t=PACK))
+
+        def quant_wm(b, a):
+            nc.vector.quantize_mx(wm_c[b][a][:].bitcast(FP8X4), wm_s[b][a][:], wm_bf[b][a][:])
+
+        def cast_wn(b):
+            nc.scalar.copy(
+                wn_bf[b][:].rearrange("p (c i t) -> p c t i", i=4, t=PACK),
+                wn_raw[b][:].rearrange("p t (c i) -> p c t i", i=4))
+
+        def quant_wn(b):
+            nc.vector.quantize_mx(wn_c[b][:].bitcast(FP8X4), wn_s[b][:], wn_bf[b][:])
+
+        def order_wr(b):
+            nc.vector.tensor_copy(
+                wr_c[b][:].rearrange("p (t u i) -> p u t i", t=PACK, i=4),
+                wr_raw[b][:].rearrange("p (u i t) -> p u t i", t=PACK, i=4))
+
+        def gather_v2(j):
+            nc.vector.tensor_copy(
+                v2_w[j][:].bitcast(U16), tab2_w[:].bitcast(U16).indirect(idx2[:, half * j : half * (j + 1)]))
+
+        def v_words(a, j):
+            return (v_w0[:, NT * j : NT * (j + 1)] if a == 0 else v_w1[j][:]).bitcast(FP8X4)
+
+        sines = {}
+        planes = {}
+        woven = {}
+        acc = {}
+
+        def kick(b, j, t):
+            cols = slice(P * t, P * (t + 1))
+            toks = slice(NT * j, NT * (j + 1))
+            phase = psum.tile([P, NT], F32, name="phase", tag="phase", bufs=2)
+            for a in range(2):
+                nc.tensor.matmul_mx(
+                    phase[:], lhsT=wm_c[b][a][:, cols].bitcast(FP8X4), lhsT_scale=wm_s[b][a][:, cols],
+                    rhs=v_words(a, j), rhs_scale=v_s[4 * a :, toks], start=(a == 0), stop=(a == 1))
+            sine = ring.tile([P, NT], F32, name="sine", tag="sine", bufs=8)
+            nc.scalar.activation(sine[:], phase[:], ACT.Sin, bias=zero[:], scale=-1.0)
+            sines[b, j, t] = sine
+
+        def new_rate(b, j, t):
+            toks = slice(NT * j, NT * (j + 1))
+            rate = psum.tile([P, NT], F32, name="rate", tag="rate", bufs=2)
+            nc.tensor.matmul_mx(
+                rate[:], lhsT=wr_c[b][:, P * t : P * (t + 1)].bitcast(FP8X4),
+                lhsT_scale=wr_s[:, KP * b + P * t : KP * b + P * (t + 1)],
+                rhs=v2_w[j][:].bitcast(FP4X4), rhs_scale=v2_s[:, toks], start=True, stop=True)
+            if t == 0:
+                planes[b, j] = ring.tile([P, PACK, NT], BF16, name="h_planes", tag="h_planes", align_bytes=64)
+            nc.vector.scalar_tensor_tensor(
+                planes[b, j][:, t, :], sines[b, j, t][:], gain_sb[:, b, t : t + 1], rate[:], ALU.mult, ALU.add)
+
+        def weave(b, j):
+            woven[b, j] = ring.tile([P, NT * PACK], BF16, name="h_bf", tag="h_bf", align_bytes=64)
+            nc.vector.tensor_copy(
+                woven[b, j][:].rearrange("p (c i t) -> p c t i", i=4, t=PACK),
+                planes[b, j][:].rearrange("p t (c i) -> p c t i", i=4))
+
+        def quant_h(b, j):
+            nc.vector.quantize_mx(h_c[b][j][:].bitcast(FP8X4), h_s[b][j][:], woven[b, j][:])
+
+        def open_angle(j, c, tag, bufs):
+            toks = slice(NT * j, NT * (j + 1))
+            acc[j, c] = psum.tile([P, NT], F32, name="angle", tag=tag, bufs=bufs)
+            for a in range(2):
+                nc.tensor.matmul_mx(
+                    acc[j, c][:], lhsT=wa_w[:, a, 2 * P * c : 2 * P * (c + 1)].bitcast(FP4X4),
+                    lhsT_scale=wa_s[:, a, P * c : P * (c + 1)],
+                    rhs=v_words(a, j), rhs_scale=(v_s if a == 0 else v_s1)[:, toks],
+                    start=(a == 0), stop=False)
+
+        def add_h(b, j, c):
+            cols = slice(P * c, P * (c + 1))
+            nc.tensor.matmul_mx(
+                acc[j, c][:], lhsT=wn_c[b][:, cols].bitcast(FP8X4), lhsT_scale=wn_s[b][:, cols],
+                rhs=h_c[b][j][:].bitcast(FP8X4), rhs_scale=h_s[b][j][:], start=False, stop=(b == 1))
+
+        def finish(j, c, on_vector):
+            res = ring.tile([P, NT], F32, name="res", tag="res", bufs=8)
+            if on_vector:
+                nc.vector.tensor_scalar(res[:], acc[j, c][:], drift_sb[:, c : c + 1], None, ALU.add)
+            else:
+                nc.scalar.activation(res[:], acc[j, c][:], ACT.Identity, bias=drift_sb[:, c : c + 1])
+            nc.sync.dma_start(out[P * c : P * (c + 1), NT * j : NT * (j + 1)], res[:])
+
+        cast_wm(0, 0)
+        nc.vector.tensor_copy(v_s[:], tab_s[:].indirect(idx[:]))
+        nc.gpsimd.dma_start(v_s1[0:100, :].bitcast(I32), v_s[4:104, :].bitcast(I32))
+        nc.vector.tensor_copy(v_w0[:], tab_w[0][:].bitcast(U32).indirect(idx[:]))
+        quant_wm(0, 0)
+        nc.vector.tensor_copy(v2_s[:], tab2_s[:].indirect(idx2[:]))
+        cast_wm(0, 1)
+        nc.vector.tensor_copy(
+            wr_s[:].rearrange("p (b t m) -> p b t m", b=2, t=PACK),
+            wr_s_raw[:].rearrange("p (b m t) -> p b t m", b=2, t=PACK))
+        quant_wm(0, 1)
+        for j in range(2):
+            nc.vector.tensor_copy(
+                v_w1[j][:], tab_w[1][:].bitcast(U32).indirect(idx[:, half * j : half * (j + 1)]))
+        gather_v2(0)
+        order_wr(0)
+
+        for t in range(PACK):
+            kick(0, 0, t)
+        for t in range(PACK):
+            kick(0, 1, t)
+            new_rate(0, 0, t)
+        gather_v2(1)
+        cast_wm(1, 0)
+        cast_wm(1, 1)
+        weave(0, 0)
+        new_rate(0, 1, 0)
+        quant_h(0, 0)
+        new_rate(0, 1, 1)
+        quant_wm(1, 0)
+        new_rate(0, 1, 2)
+        new_rate(0, 1, 3)
+        order_wr(1)
+        quant_wm(1, 1)
+        weave(0, 1)
+        for t in range(PACK):
+            kick(1, 0, t)
+        cast_wn(0)
+        for c in range(4):
+            open_angle(0, c, "angle", 4)
+        new_rate(1, 0, 0)
+        quant_h(0, 1)
+        for t in range(1, PACK):
+            new_rate(1, 0, t)
+        for t in range(PACK):
+            kick(1, 1, t)
+        cast_wn(1)
+        quant_wn(0)
+        for c in range(4):
+            add_h(0, 0, c)
+        weave(1, 0)
+        new_rate(1, 1, 0)
+        quant_h(1, 0)
+        quant_wn(1)
+        for c in range(4):
+            add_h(1, 0, c)
+            finish(0, c, False)
+        for t in range(1, PACK):
+            new_rate(1, 1, t)
+        for c in range(4):
+            if c < 2:
+                open_angle(1, c, "phase", 2)
+            else:
+                open_angle(1, c, "angle", 4)
+            add_h(0, 1, c)
+        weave(1, 1)
+        quant_h(1, 1)
+        for c in range(4):
+            add_h(1, 1, c)
+            finish(1, c, c % 2 == 1)

@@ -20,8 +20,9 @@ P = 128
 PACK = 4
 KP = P * PACK
 NT = 512
+LAST_SPLIT = 352
 TAB1_AT = 4 * 4 * PACK * KP
-LATE_BYTES = 4 * 4 * PACK * KP + 4 * T + 2 * T + 2 * 4 * PACK * N + 2 * 4 * KP + 4 * N + 2 * 64
+LATE_BYTES = 4 * 4 * PACK * KP + 4 * T + 2 * T + 2 * 4 * PACK * N + 2 * 4 * KP + 6 * N + 2 * 64
 
 
 def tile_list_attitude_propagation_kernel(
@@ -63,7 +64,7 @@ def tile_list_attitude_propagation_kernel(
         wr_raw = [late_tile([P, KP], I32, "wr_raw%d" % b, 4 * KP) for b in range(2)]
         wr_s_raw = held([P, H], U8, "wr_s_raw")
         wa_w = late_tile([P, 2, 2 * N], U8, "wa_w", 4 * N)
-        wa_s = held([P, 2, N], U8, "wa_s")
+        wa_s = late_tile([P, 2, N], U8, "wa_s", 2 * N)
         gain_sb = late_tile([P, 2, PACK], F32, "gain_sb", 64)
         drift_sb = late_tile([P, N // P], F32, "drift_sb", 64)
         assert used[0] == LATE_BYTES
@@ -75,7 +76,6 @@ def tile_list_attitude_propagation_kernel(
         nc.scalar.activation(zero[:], zero_in[:, 0:1], ACT.Sin)
         nc.vector.memset(tab2_s[:].bitcast(I32), 0)
         nc.gpsimd.memset(wr_s_raw[:].bitcast(I32), 0)
-        nc.gpsimd.memset(wa_s[:].rearrange("p a n -> p (a n)").bitcast(I32), 0)
         nc.gpsimd.memset(v_s1[:].bitcast(I32), 0)
 
         def load_wm(b, a):
@@ -111,8 +111,13 @@ def tile_list_attitude_propagation_kernel(
         load_wm(1, 0)
         load_wm(1, 1)
         load_wr(1)
-        load_wn(0)
         nc.sync.dma_start(wa_w[:].bitcast(I32), wa_words.bitcast(I32).rearrange("a p c -> p a c"))
+        nc.vector.memset(wa_s[:].rearrange("p a n -> p (a n)").bitcast(I32), 0)
+        for q in range(4):
+            nc.sync.dma_start(
+                wa_s[32 * q : 32 * q + 4, :, :].bitcast(I32),
+                wa_scales[:, 4 * q : 4 * q + 4, :].bitcast(I32).rearrange("a r n -> r a n"))
+        load_wn(0)
         load_wn(1)
         with nc.allow_non_contiguous_dma(reason="one drift value a partition"):
             nc.sync.dma_start(drift_sb[:], drift.rearrange("(c p) -> p c", p=P))
@@ -120,10 +125,6 @@ def tile_list_attitude_propagation_kernel(
         for q in range(4):
             nc.gpsimd.dma_start(
                 wr_s_raw[32 * q : 32 * q + 4, :].bitcast(I32), wr_scales[0, 4 * q : 4 * q + 4, :].bitcast(I32))
-        for q in range(4):
-            nc.gpsimd.dma_start(
-                wa_s[32 * q : 32 * q + 4, :, :].bitcast(I32),
-                wa_scales[:, 4 * q : 4 * q + 4, :].bitcast(I32).rearrange("a r n -> r a n"))
 
         v_s = held([P, S], U8, "v_s")
         v_w0 = held([P, S], U32, "v_w0")
@@ -133,30 +134,38 @@ def tile_list_attitude_propagation_kernel(
                 for j in range(2)]
         half = NT // 16
 
-        wm_bf = [[held([P, KP * PACK], BF16, "wm_bf%d%d" % (b, a)) for a in range(2)] for b in range(2)]
+        mid = ctx.enter_context(tc.tile_pool(name="mid", bufs=1))
+
+        def mid_tile(shape, dtype, name, slot):
+            return mid.tile(shape, dtype, name=name, align_bytes=64, offset=4 * NT * slot)
+
+        sine_slot = {(0, 0): 1, (1, 0): 7, (0, 1): 12, (1, 1): 16}
+        wm_bf = [[held([P, KP * PACK], BF16, "wm_bf0%d" % a) for a in range(2)],
+                 [mid_tile([P, KP * PACK], BF16, "wm_bf1%d" % a, 4 * a) for a in range(2)]]
         wm_c = [[held([P, KP], U32, "wm_c%d%d" % (b, a)) for a in range(2)] for b in range(2)]
         wm_s = [[held([P, KP], U8, "wm_s%d%d" % (b, a)) for a in range(2)] for b in range(2)]
-        wn_bf = [held([P, N * PACK], BF16, "wn_bf%d" % b) for b in range(2)]
+        wn_bf = [mid_tile([P, N * PACK], BF16, "wn_bf%d" % b, 6 + 2 * b) for b in range(2)]
         wn_c = [held([P, N], U32, "wn_c%d" % b) for b in range(2)]
         wn_s = [held([P, N], U8, "wn_s%d" % b) for b in range(2)]
-        wr_c = [late.tile([P, KP], I32, name="wr_c%d" % b, align_bytes=64, offset=TAB1_AT + 4 * NT + 4 * KP * b)
-                for b in range(2)]
+        wr_c = [late.tile([P, KP], I32, name="wr_c0", align_bytes=64, offset=TAB1_AT + 4 * NT),
+                mid_tile([P, KP], I32, "wr_c1", 15)]
         wr_s = late.tile([P, H], U8, name="wr_s", align_bytes=64, offset=LATE_BYTES + 64)
         h_c = [[held([P, NT], U32, "h_c%d%d" % (b, j)) for j in range(2)] for b in range(2)]
         h_s = [[held([P, NT], U8, "h_s%d%d" % (b, j)) for j in range(2)] for b in range(2)]
 
-        def cast_wm(b, a):
-            nc.scalar.copy(
-                wm_bf[b][a][:].rearrange("p (t m j) -> p m t j", t=PACK, j=PACK),
-                wm_raw[b][a][:].rearrange("p j (m t) -> p m t j", t=PACK))
+        def cast_wm(b, a, copy):
+            copy(
+                wm_bf[b][a][:].rearrange("p (t m j) -> p m j t", t=PACK, j=PACK),
+                wm_raw[b][a][:].rearrange("p j (m t) -> p m j t", t=PACK))
 
         def quant_wm(b, a):
             nc.vector.quantize_mx(wm_c[b][a][:].bitcast(FP8X4), wm_s[b][a][:], wm_bf[b][a][:])
 
         def cast_wn(b):
-            nc.scalar.copy(
-                wn_bf[b][:].rearrange("p (c i t) -> p c t i", i=4, t=PACK),
-                wn_raw[b][:].rearrange("p t (c i) -> p c t i", i=4))
+            for c in range(N // P):
+                nc.scalar.copy(
+                    wn_bf[b][:, PACK * P * c : PACK * P * (c + 1)].rearrange("p (u i t) -> p u t i", i=4, t=PACK),
+                    wn_raw[b][:, :, P * c : P * (c + 1)].rearrange("p t (u i) -> p u t i", i=4))
 
         def quant_wn(b):
             nc.vector.quantize_mx(wn_c[b][:].bitcast(FP8X4), wn_s[b][:], wn_bf[b][:])
@@ -181,39 +190,40 @@ def tile_list_attitude_propagation_kernel(
         def kick(b, j, t):
             cols = slice(P * t, P * (t + 1))
             toks = slice(NT * j, NT * (j + 1))
-            phase = psum.tile([P, NT], F32, name="phase", tag="phase", bufs=2)
+            phase = psum.tile([P, NT], F32, name="phase", tag=("sum%d" if (b, j) == (0, 1) else "work%d") % t)
             for a in range(2):
                 nc.tensor.matmul_mx(
                     phase[:], lhsT=wm_c[b][a][:, cols].bitcast(FP8X4), lhsT_scale=wm_s[b][a][:, cols],
                     rhs=v_words(a, j), rhs_scale=v_s[4 * a :, toks], start=(a == 0), stop=(a == 1))
-            sine = ring.tile([P, NT], F32, name="sine", tag="sine", bufs=8)
+            sine = mid_tile([P, NT], F32, "sine%d%d%d" % (b, j, t), sine_slot[b, j] + t)
             nc.scalar.activation(sine[:], phase[:], ACT.Sin, bias=zero[:], scale=-1.0)
             sines[b, j, t] = sine
 
         def new_rate(b, j, t):
             toks = slice(NT * j, NT * (j + 1))
-            rate = psum.tile([P, NT], F32, name="rate", tag="rate", bufs=2)
+            rate = psum.tile([P, NT], F32, name="rate", tag=("sum%d" if (b, j) == (0, 1) else "work%d") % t)
             nc.tensor.matmul_mx(
                 rate[:], lhsT=wr_c[b][:, P * t : P * (t + 1)].bitcast(FP8X4),
                 lhsT_scale=wr_s[:, KP * b + P * t : KP * b + P * (t + 1)],
                 rhs=v2_w[j][:].bitcast(FP4X4), rhs_scale=v2_s[:, toks], start=True, stop=True)
             if t == 0:
-                planes[b, j] = ring.tile([P, PACK, NT], BF16, name="h_planes", tag="h_planes", align_bytes=64)
+                planes[b, j] = ring.tile([P, PACK, NT], BF16, name="h_planes", tag="h_planes", bufs=3, align_bytes=64)
             nc.vector.scalar_tensor_tensor(
                 planes[b, j][:, t, :], sines[b, j, t][:], gain_sb[:, b, t : t + 1], rate[:], ALU.mult, ALU.add)
 
-        def weave(b, j):
+        def weave(b, j, shares):
             woven[b, j] = ring.tile([P, NT * PACK], BF16, name="h_bf", tag="h_bf", align_bytes=64)
-            nc.vector.tensor_copy(
-                woven[b, j][:].rearrange("p (c i t) -> p c t i", i=4, t=PACK),
-                planes[b, j][:].rearrange("p t (c i) -> p c t i", i=4))
+            for copy, lo, hi in shares:
+                copy(
+                    woven[b, j][:, PACK * lo : PACK * hi].rearrange("p (u i t) -> p u t i", i=4, t=PACK),
+                    planes[b, j][:, :, lo:hi].rearrange("p t (u i) -> p u t i", i=4))
 
         def quant_h(b, j):
             nc.vector.quantize_mx(h_c[b][j][:].bitcast(FP8X4), h_s[b][j][:], woven[b, j][:])
 
-        def open_angle(j, c, tag, bufs):
+        def open_angle(j, c):
             toks = slice(NT * j, NT * (j + 1))
-            acc[j, c] = psum.tile([P, NT], F32, name="angle", tag=tag, bufs=bufs)
+            acc[j, c] = psum.tile([P, NT], F32, name="angle", tag="sum%d" % c)
             for a in range(2):
                 nc.tensor.matmul_mx(
                     acc[j, c][:], lhsT=wa_w[:, a, 2 * P * c : 2 * P * (c + 1)].bitcast(FP4X4),
@@ -235,13 +245,13 @@ def tile_list_attitude_propagation_kernel(
                 nc.scalar.activation(res[:], acc[j, c][:], ACT.Identity, bias=drift_sb[:, c : c + 1])
             nc.sync.dma_start(out[P * c : P * (c + 1), NT * j : NT * (j + 1)], res[:])
 
-        cast_wm(0, 0)
+        cast_wm(0, 0, nc.scalar.copy)
         nc.vector.tensor_copy(v_s[:], tab_s[:].indirect(idx[:]))
         nc.gpsimd.dma_start(v_s1[0:100, :].bitcast(I32), v_s[4:104, :].bitcast(I32))
         nc.vector.tensor_copy(v_w0[:], tab_w[0][:].bitcast(U32).indirect(idx[:]))
         quant_wm(0, 0)
         nc.vector.tensor_copy(v2_s[:], tab2_s[:].indirect(idx2[:]))
-        cast_wm(0, 1)
+        cast_wm(0, 1, nc.scalar.copy)
         nc.vector.tensor_copy(
             wr_s[:].rearrange("p (b t m) -> p b t m", b=2, t=PACK),
             wr_s_raw[:].rearrange("p (b m t) -> p b t m", b=2, t=PACK))
@@ -252,55 +262,53 @@ def tile_list_attitude_propagation_kernel(
         gather_v2(0)
         order_wr(0)
 
+        on_vector = [(nc.vector.tensor_copy, 0, NT)]
+        shared = [(nc.vector.tensor_copy, 0, LAST_SPLIT), (nc.scalar.copy, LAST_SPLIT, NT)]
+
         for t in range(PACK):
             kick(0, 0, t)
-        for t in range(PACK):
-            kick(0, 1, t)
-            new_rate(0, 0, t)
         gather_v2(1)
-        cast_wm(1, 0)
-        cast_wm(1, 1)
-        weave(0, 0)
-        new_rate(0, 1, 0)
-        quant_h(0, 0)
-        new_rate(0, 1, 1)
+        kick(0, 1, 0)
+        for t in range(PACK):
+            if t + 1 < PACK:
+                kick(0, 1, t + 1)
+            new_rate(0, 0, t)
+        cast_wm(1, 0, nc.scalar.copy)
+        cast_wm(1, 1, nc.scalar.copy)
+        for t in range(PACK):
+            new_rate(0, 1, t)
         quant_wm(1, 0)
-        new_rate(0, 1, 2)
-        new_rate(0, 1, 3)
         order_wr(1)
         quant_wm(1, 1)
-        weave(0, 1)
         for t in range(PACK):
             kick(1, 0, t)
-        cast_wn(0)
         for c in range(4):
-            open_angle(0, c, "angle", 4)
+            open_angle(0, c)
+        weave(0, 0, on_vector)
         new_rate(1, 0, 0)
-        quant_h(0, 1)
+        quant_h(0, 0)
         for t in range(1, PACK):
             new_rate(1, 0, t)
+        cast_wn(0)
+        cast_wn(1)
         for t in range(PACK):
             kick(1, 1, t)
-        cast_wn(1)
+        weave(1, 0, on_vector)
         quant_wn(0)
+        quant_h(1, 0)
+        weave(0, 1, on_vector)
+        quant_wn(1)
+        quant_h(0, 1)
         for c in range(4):
             add_h(0, 0, c)
-        weave(1, 0)
-        new_rate(1, 1, 0)
-        quant_h(1, 0)
-        quant_wn(1)
         for c in range(4):
+            new_rate(1, 1, c)
             add_h(1, 0, c)
             finish(0, c, False)
-        for t in range(1, PACK):
-            new_rate(1, 1, t)
         for c in range(4):
-            if c < 2:
-                open_angle(1, c, "phase", 2)
-            else:
-                open_angle(1, c, "angle", 4)
+            open_angle(1, c)
             add_h(0, 1, c)
-        weave(1, 1)
+        weave(1, 1, shared)
         quant_h(1, 1)
         for c in range(4):
             add_h(1, 1, c)

@@ -20,6 +20,7 @@ P = 128
 PACK = 4
 KP = P * PACK
 NT = 512
+WM11_AT = 3 * 4 * PACK * KP
 LAST_SPLIT = 352
 TAB1_AT = 4 * 4 * PACK * KP
 LATE_BYTES = 4 * 4 * PACK * KP + 4 * T + 2 * T + 2 * 4 * PACK * N + 2 * 4 * KP + 6 * N + 2 * 64
@@ -111,13 +112,13 @@ def tile_list_attitude_propagation_kernel(
         load_wm(1, 0)
         load_wm(1, 1)
         load_wr(1)
+        load_wn(0)
         nc.sync.dma_start(wa_w[:].bitcast(I32), wa_words.bitcast(I32).rearrange("a p c -> p a c"))
         nc.vector.memset(wa_s[:].rearrange("p a n -> p (a n)").bitcast(I32), 0)
         for q in range(4):
             nc.sync.dma_start(
                 wa_s[32 * q : 32 * q + 4, :, :].bitcast(I32),
                 wa_scales[:, 4 * q : 4 * q + 4, :].bitcast(I32).rearrange("a r n -> r a n"))
-        load_wn(0)
         load_wn(1)
         with nc.allow_non_contiguous_dma(reason="one drift value a partition"):
             nc.sync.dma_start(drift_sb[:], drift.rearrange("(c p) -> p c", p=P))
@@ -141,14 +142,16 @@ def tile_list_attitude_propagation_kernel(
 
         sine_slot = {(0, 0): 1, (1, 0): 7, (0, 1): 12, (1, 1): 16}
         wm_bf = [[held([P, KP * PACK], BF16, "wm_bf0%d" % a) for a in range(2)],
-                 [mid_tile([P, KP * PACK], BF16, "wm_bf1%d" % a, 4 * a) for a in range(2)]]
-        wm_c = [[held([P, KP], U32, "wm_c%d%d" % (b, a)) for a in range(2)] for b in range(2)]
+                 [mid_tile([P, KP * PACK], BF16, "wm_bf10", 20), mid_tile([P, KP * PACK], BF16, "wm_bf11", 4)]]
+        wm_c = [[mid_tile([P, KP], U32, "wm_c01", 20) if (b, a) == (0, 1)
+                 else held([P, KP], U32, "wm_c%d%d" % (b, a)) for a in range(2)] for b in range(2)]
         wm_s = [[held([P, KP], U8, "wm_s%d%d" % (b, a)) for a in range(2)] for b in range(2)]
-        wn_bf = [mid_tile([P, N * PACK], BF16, "wn_bf%d" % b, 6 + 2 * b) for b in range(2)]
+        wn_bf = [late.tile([P, N * PACK], BF16, name="wn_bf0", align_bytes=64, offset=WM11_AT),
+                 mid_tile([P, N * PACK], BF16, "wn_bf1", 13)]
         wn_c = [held([P, N], U32, "wn_c%d" % b) for b in range(2)]
         wn_s = [held([P, N], U8, "wn_s%d" % b) for b in range(2)]
         wr_c = [late.tile([P, KP], I32, name="wr_c0", align_bytes=64, offset=TAB1_AT + 4 * NT),
-                mid_tile([P, KP], I32, "wr_c1", 15)]
+                late.tile([P, KP], I32, name="wr_c1", align_bytes=64, offset=WM11_AT + 2 * N * PACK)]
         wr_s = late.tile([P, H], U8, name="wr_s", align_bytes=64, offset=LATE_BYTES + 64)
         h_c = [[held([P, NT], U32, "h_c%d%d" % (b, j)) for j in range(2)] for b in range(2)]
         h_s = [[held([P, NT], U8, "h_s%d%d" % (b, j)) for j in range(2)] for b in range(2)]
@@ -182,21 +185,27 @@ def tile_list_attitude_propagation_kernel(
         def v_words(a, j):
             return (v_w0[:, NT * j : NT * (j + 1)] if a == 0 else v_w1[j][:]).bitcast(FP8X4)
 
+        phases = {}
         sines = {}
         planes = {}
         woven = {}
         acc = {}
 
-        def kick(b, j, t):
+        def phase_pass(b, j, t, a):
             cols = slice(P * t, P * (t + 1))
-            toks = slice(NT * j, NT * (j + 1))
+            nc.tensor.matmul_mx(
+                phases[b, j, t][:], lhsT=wm_c[b][a][:, cols].bitcast(FP8X4), lhsT_scale=wm_s[b][a][:, cols],
+                rhs=v_words(a, j), rhs_scale=v_s[4 * a :, NT * j : NT * (j + 1)], start=(a == 0), stop=(a == 1))
+
+        def open_phase(b, j, t):
             phase = psum.tile([P, NT], F32, name="phase", tag=("sum%d" if (b, j) == (0, 1) else "work%d") % t)
-            for a in range(2):
-                nc.tensor.matmul_mx(
-                    phase[:], lhsT=wm_c[b][a][:, cols].bitcast(FP8X4), lhsT_scale=wm_s[b][a][:, cols],
-                    rhs=v_words(a, j), rhs_scale=v_s[4 * a :, toks], start=(a == 0), stop=(a == 1))
+            phases[b, j, t] = phase
+            phase_pass(b, j, t, 0)
+
+        def kick(b, j, t):
+            phase_pass(b, j, t, 1)
             sine = mid_tile([P, NT], F32, "sine%d%d%d" % (b, j, t), sine_slot[b, j] + t)
-            nc.scalar.activation(sine[:], phase[:], ACT.Sin, bias=zero[:], scale=-1.0)
+            nc.scalar.activation(sine[:], phases[b, j, t][:], ACT.Sin, bias=zero[:], scale=-1.0)
             sines[b, j, t] = sine
 
         def new_rate(b, j, t):
@@ -212,7 +221,7 @@ def tile_list_attitude_propagation_kernel(
                 planes[b, j][:, t, :], sines[b, j, t][:], gain_sb[:, b, t : t + 1], rate[:], ALU.mult, ALU.add)
 
         def weave(b, j, shares):
-            woven[b, j] = ring.tile([P, NT * PACK], BF16, name="h_bf", tag="h_bf", align_bytes=64)
+            woven[b, j] = ring.tile([P, NT * PACK], BF16, name="h_bf", tag="h_bf", bufs=3, align_bytes=64)
             for copy, lo, hi in shares:
                 copy(
                     woven[b, j][:, PACK * lo : PACK * hi].rearrange("p (u i t) -> p u t i", i=4, t=PACK),
@@ -223,7 +232,7 @@ def tile_list_attitude_propagation_kernel(
 
         def open_angle(j, c):
             toks = slice(NT * j, NT * (j + 1))
-            acc[j, c] = psum.tile([P, NT], F32, name="angle", tag="sum%d" % c)
+            acc[j, c] = psum.tile([P, NT], F32, name="angle", tag=("sum%d" if j == 0 else "work%d") % c)
             for a in range(2):
                 nc.tensor.matmul_mx(
                     acc[j, c][:], lhsT=wa_w[:, a, 2 * P * c : 2 * P * (c + 1)].bitcast(FP4X4),
@@ -262,26 +271,31 @@ def tile_list_attitude_propagation_kernel(
         gather_v2(0)
         order_wr(0)
 
+        on_scalar = [(nc.scalar.copy, lo, lo + P) for lo in range(0, NT, P)]
         on_vector = [(nc.vector.tensor_copy, 0, NT)]
         shared = [(nc.vector.tensor_copy, 0, LAST_SPLIT), (nc.scalar.copy, LAST_SPLIT, NT)]
 
+        for j in range(2):
+            for t in range(PACK):
+                open_phase(0, j, t)
         for t in range(PACK):
             kick(0, 0, t)
         gather_v2(1)
-        kick(0, 1, 0)
         for t in range(PACK):
-            if t + 1 < PACK:
-                kick(0, 1, t + 1)
-            new_rate(0, 0, t)
+            kick(0, 1, t)
         cast_wm(1, 0, nc.scalar.copy)
-        cast_wm(1, 1, nc.scalar.copy)
         for t in range(PACK):
-            new_rate(0, 1, t)
+            new_rate(0, 0, t)
+        cast_wm(1, 1, nc.vector.tensor_copy)
         quant_wm(1, 0)
-        order_wr(1)
+        for t in range(PACK):
+            open_phase(1, 0, t)
         quant_wm(1, 1)
+        order_wr(1)
         for t in range(PACK):
             kick(1, 0, t)
+        for t in range(PACK):
+            new_rate(0, 1, t)
         for c in range(4):
             open_angle(0, c)
         weave(0, 0, on_vector)
@@ -292,19 +306,21 @@ def tile_list_attitude_propagation_kernel(
         cast_wn(0)
         cast_wn(1)
         for t in range(PACK):
+            open_phase(1, 1, t)
             kick(1, 1, t)
-        weave(1, 0, on_vector)
         quant_wn(0)
-        quant_h(1, 0)
-        weave(0, 1, on_vector)
+        weave(1, 0, on_vector)
         quant_wn(1)
-        quant_h(0, 1)
+        quant_h(1, 0)
+        weave(0, 1, on_scalar)
         for c in range(4):
             add_h(0, 0, c)
         for c in range(4):
             new_rate(1, 1, c)
+        for c in range(4):
             add_h(1, 0, c)
             finish(0, c, False)
+        quant_h(0, 1)
         for c in range(4):
             open_angle(1, c)
             add_h(0, 1, c)

@@ -221,11 +221,17 @@ def tile_list_attitude_propagation_kernel(
                 planes[b, j][:, t, :], sines[b, j, t][:], gain_sb[:, b, t : t + 1], rate[:], ALU.mult, ALU.add)
 
         def weave(b, j, shares):
-            woven[b, j] = ring.tile([P, NT * PACK], BF16, name="h_bf", tag="h_bf", bufs=3, align_bytes=64)
+            woven[b, j] = ring.tile([P, NT * PACK], BF16, name="h_bf", tag="h_bf", align_bytes=64)
             for copy, lo, hi in shares:
                 copy(
                     woven[b, j][:, PACK * lo : PACK * hi].rearrange("p (u i t) -> p u t i", i=4, t=PACK),
                     planes[b, j][:, :, lo:hi].rearrange("p t (u i) -> p u t i", i=4))
+
+        def weave_on_gpsimd(b, j):
+            woven[b, j] = mid_tile([P, NT * PACK], BF16, "h_bf%d%d" % (b, j), 4)
+            nc.gpsimd.tensor_scalar(
+                woven[b, j][:].rearrange("p (n t) -> p n t", t=PACK),
+                planes[b, j][:].rearrange("p t n -> p n t"), 1.0, 0.0, ALU.mult, ALU.add)
 
         def quant_h(b, j):
             nc.vector.quantize_mx(h_c[b][j][:].bitcast(FP8X4), h_s[b][j][:], woven[b, j][:])
@@ -272,7 +278,6 @@ def tile_list_attitude_propagation_kernel(
         order_wr(0)
 
         on_scalar = [(nc.scalar.copy, lo, lo + P) for lo in range(0, NT, P)]
-        on_vector = [(nc.vector.tensor_copy, 0, NT)]
         shared = [(nc.vector.tensor_copy, 0, LAST_SPLIT), (nc.scalar.copy, LAST_SPLIT, NT)]
 
         for j in range(2):
@@ -298,9 +303,10 @@ def tile_list_attitude_propagation_kernel(
             new_rate(0, 1, t)
         for c in range(4):
             open_angle(0, c)
-        weave(0, 0, on_vector)
+        weave_on_gpsimd(0, 0)
         new_rate(1, 0, 0)
         quant_h(0, 0)
+        weave_on_gpsimd(0, 1)
         for t in range(1, PACK):
             new_rate(1, 0, t)
         cast_wn(0)
@@ -309,10 +315,9 @@ def tile_list_attitude_propagation_kernel(
             open_phase(1, 1, t)
             kick(1, 1, t)
         quant_wn(0)
-        weave(1, 0, on_vector)
+        weave(1, 0, on_scalar)
         quant_wn(1)
         quant_h(1, 0)
-        weave(0, 1, on_scalar)
         for c in range(4):
             add_h(0, 0, c)
         for c in range(4):

@@ -23,7 +23,7 @@ NT = 512
 WM11_AT = 3 * 4 * PACK * KP
 LAST_SPLIT = 352
 TAB1_AT = 4 * 4 * PACK * KP
-LATE_BYTES = 4 * 4 * PACK * KP + 4 * T + 2 * T + 2 * 4 * PACK * N + 2 * 4 * KP + 6 * N + 2 * 64
+LATE_BYTES = 4 * 4 * PACK * KP + 4 * T + 2 * T + 2 * 4 * PACK * N + 2 * 4 * KP + 4 * N + 2 * 64
 
 
 def tile_list_attitude_propagation_kernel(
@@ -65,7 +65,7 @@ def tile_list_attitude_propagation_kernel(
         wr_raw = [late_tile([P, KP], I32, "wr_raw%d" % b, 4 * KP) for b in range(2)]
         wr_s_raw = held([P, H], U8, "wr_s_raw")
         wa_w = late_tile([P, 2, 2 * N], U8, "wa_w", 4 * N)
-        wa_s = late_tile([P, 2, N], U8, "wa_s", 2 * N)
+        wa_s = held([P, 2, N], U8, "wa_s")
         gain_sb = late_tile([P, 2, PACK], F32, "gain_sb", 64)
         drift_sb = late_tile([P, N // P], F32, "drift_sb", 64)
         assert used[0] == LATE_BYTES
@@ -77,6 +77,7 @@ def tile_list_attitude_propagation_kernel(
         nc.scalar.activation(zero[:], zero_in[:, 0:1], ACT.Sin)
         nc.vector.memset(tab2_s[:].bitcast(I32), 0)
         nc.gpsimd.memset(wr_s_raw[:].bitcast(I32), 0)
+        nc.gpsimd.memset(wa_s[:].rearrange("p a n -> p (a n)").bitcast(I32), 0)
         nc.gpsimd.memset(v_s1[:].bitcast(I32), 0)
 
         def load_wm(b, a):
@@ -110,15 +111,10 @@ def tile_list_attitude_propagation_kernel(
         nc.sync.dma_start(tab2_w[:], tab2_words[0].bitcast(I32))
         load_wr(0)
         load_wm(1, 0)
+        nc.sync.dma_start(wa_w[:].bitcast(I32), wa_words.bitcast(I32).rearrange("a p c -> p a c"))
         load_wm(1, 1)
         load_wr(1)
         load_wn(0)
-        nc.sync.dma_start(wa_w[:].bitcast(I32), wa_words.bitcast(I32).rearrange("a p c -> p a c"))
-        nc.vector.memset(wa_s[:].rearrange("p a n -> p (a n)").bitcast(I32), 0)
-        for q in range(4):
-            nc.sync.dma_start(
-                wa_s[32 * q : 32 * q + 4, :, :].bitcast(I32),
-                wa_scales[:, 4 * q : 4 * q + 4, :].bitcast(I32).rearrange("a r n -> r a n"))
         load_wn(1)
         with nc.allow_non_contiguous_dma(reason="one drift value a partition"):
             nc.sync.dma_start(drift_sb[:], drift.rearrange("(c p) -> p c", p=P))
@@ -126,6 +122,10 @@ def tile_list_attitude_propagation_kernel(
         for q in range(4):
             nc.gpsimd.dma_start(
                 wr_s_raw[32 * q : 32 * q + 4, :].bitcast(I32), wr_scales[0, 4 * q : 4 * q + 4, :].bitcast(I32))
+        for q in range(4):
+            nc.gpsimd.dma_start(
+                wa_s[32 * q : 32 * q + 4, :, :].bitcast(I32),
+                wa_scales[:, 4 * q : 4 * q + 4, :].bitcast(I32).rearrange("a r n -> r a n"))
 
         v_s = held([P, S], U8, "v_s")
         v_w0 = held([P, S], U32, "v_w0")
@@ -141,11 +141,13 @@ def tile_list_attitude_propagation_kernel(
             return mid.tile(shape, dtype, name=name, align_bytes=64, offset=4 * NT * slot)
 
         sine_slot = {(0, 0): 1, (1, 0): 7, (0, 1): 12, (1, 1): 16}
+        woven_slot = {(0, 0): 24, (0, 1): 24, (1, 0): 26, (1, 1): 28}
         wm_bf = [[held([P, KP * PACK], BF16, "wm_bf0%d" % a) for a in range(2)],
-                 [mid_tile([P, KP * PACK], BF16, "wm_bf10", 20), mid_tile([P, KP * PACK], BF16, "wm_bf11", 4)]]
+                 [mid_tile([P, KP * PACK], BF16, "wm_bf10", 20), mid_tile([P, KP * PACK], BF16, "wm_bf11", 22)]]
         wm_c = [[mid_tile([P, KP], U32, "wm_c01", 20) if (b, a) == (0, 1)
                  else held([P, KP], U32, "wm_c%d%d" % (b, a)) for a in range(2)] for b in range(2)]
-        wm_s = [[held([P, KP], U8, "wm_s%d%d" % (b, a)) for a in range(2)] for b in range(2)]
+        wm_s = [[mid_tile([P, KP], U8, "wm_s01", 22) if (b, a) == (0, 1)
+                 else held([P, KP], U8, "wm_s%d%d" % (b, a)) for a in range(2)] for b in range(2)]
         wn_bf = [late.tile([P, N * PACK], BF16, name="wn_bf0", align_bytes=64, offset=WM11_AT),
                  mid_tile([P, N * PACK], BF16, "wn_bf1", 13)]
         wn_c = [held([P, N], U32, "wn_c%d" % b) for b in range(2)]
@@ -210,7 +212,7 @@ def tile_list_attitude_propagation_kernel(
 
         def new_rate(b, j, t):
             toks = slice(NT * j, NT * (j + 1))
-            rate = psum.tile([P, NT], F32, name="rate", tag=("sum%d" if (b, j) == (0, 1) else "work%d") % t)
+            rate = psum.tile([P, NT], F32, name="rate", tag=("sum%d" if (b, j) == (0, 0) else "work%d") % t)
             nc.tensor.matmul_mx(
                 rate[:], lhsT=wr_c[b][:, P * t : P * (t + 1)].bitcast(FP8X4),
                 lhsT_scale=wr_s[:, KP * b + P * t : KP * b + P * (t + 1)],
@@ -221,14 +223,14 @@ def tile_list_attitude_propagation_kernel(
                 planes[b, j][:, t, :], sines[b, j, t][:], gain_sb[:, b, t : t + 1], rate[:], ALU.mult, ALU.add)
 
         def weave(b, j, shares):
-            woven[b, j] = ring.tile([P, NT * PACK], BF16, name="h_bf", tag="h_bf", align_bytes=64)
+            woven[b, j] = mid_tile([P, NT * PACK], BF16, "h_bf%d%d" % (b, j), woven_slot[b, j])
             for copy, lo, hi in shares:
                 copy(
                     woven[b, j][:, PACK * lo : PACK * hi].rearrange("p (u i t) -> p u t i", i=4, t=PACK),
                     planes[b, j][:, :, lo:hi].rearrange("p t (u i) -> p u t i", i=4))
 
         def weave_on_gpsimd(b, j):
-            woven[b, j] = mid_tile([P, NT * PACK], BF16, "h_bf%d%d" % (b, j), 4)
+            woven[b, j] = mid_tile([P, NT * PACK], BF16, "h_bf%d%d" % (b, j), woven_slot[b, j])
             nc.gpsimd.tensor_scalar(
                 woven[b, j][:].rearrange("p (n t) -> p n t", t=PACK),
                 planes[b, j][:].rearrange("p t n -> p n t"), 1.0, 0.0, ALU.mult, ALU.add)
@@ -277,7 +279,7 @@ def tile_list_attitude_propagation_kernel(
         gather_v2(0)
         order_wr(0)
 
-        on_scalar = [(nc.scalar.copy, lo, lo + P) for lo in range(0, NT, P)]
+        on_vector = [(nc.vector.tensor_copy, 0, NT)]
         shared = [(nc.vector.tensor_copy, 0, LAST_SPLIT), (nc.scalar.copy, LAST_SPLIT, NT)]
 
         for j in range(2):
@@ -289,21 +291,21 @@ def tile_list_attitude_propagation_kernel(
         for t in range(PACK):
             kick(0, 1, t)
         cast_wm(1, 0, nc.scalar.copy)
+        cast_wm(1, 1, nc.scalar.copy)
         for t in range(PACK):
             new_rate(0, 0, t)
-        cast_wm(1, 1, nc.vector.tensor_copy)
         quant_wm(1, 0)
-        for t in range(PACK):
-            open_phase(1, 0, t)
         quant_wm(1, 1)
         order_wr(1)
-        for t in range(PACK):
-            kick(1, 0, t)
         for t in range(PACK):
             new_rate(0, 1, t)
         for c in range(4):
             open_angle(0, c)
-        weave_on_gpsimd(0, 0)
+        for t in range(PACK):
+            open_phase(1, 0, t)
+        for t in range(PACK):
+            kick(1, 0, t)
+        weave(0, 0, on_vector)
         new_rate(1, 0, 0)
         quant_h(0, 0)
         weave_on_gpsimd(0, 1)
@@ -315,7 +317,7 @@ def tile_list_attitude_propagation_kernel(
             open_phase(1, 1, t)
             kick(1, 1, t)
         quant_wn(0)
-        weave(1, 0, on_scalar)
+        weave(1, 0, on_vector)
         quant_wn(1)
         quant_h(1, 0)
         for c in range(4):

@@ -20,10 +20,7 @@ P = 128
 PACK = 4
 KP = P * PACK
 NT = 512
-WM11_AT = 3 * 4 * PACK * KP
-LAST_SPLIT = 352
-TAB1_AT = 4 * 4 * PACK * KP
-LATE_BYTES = 4 * 4 * PACK * KP + 4 * T + 2 * T + 2 * 4 * PACK * N + 2 * 4 * KP + 4 * N + 2 * 64
+KB = 1024
 
 
 def tile_list_attitude_propagation_kernel(
@@ -33,52 +30,55 @@ def tile_list_attitude_propagation_kernel(
     nc = tc.nc
     with ExitStack() as ctx:
         keep = ctx.enter_context(tc.tile_pool(name="keep", bufs=1))
-        ring = ctx.enter_context(tc.tile_pool(name="ring", bufs=2))
+        ring = ctx.enter_context(tc.tile_pool(name="ring", bufs=1))
+        arena = ctx.enter_context(tc.tile_pool(name="arena", bufs=1))
         psum = ctx.enter_context(tc.psum_pool(name="psum", bufs=1))
 
         def held(shape, dtype, name):
             return keep.tile(shape, dtype, name=name, align_bytes=64)
 
-        late = ctx.enter_context(tc.tile_pool(name="late", bufs=1))
-        used = [4 * PACK * KP]
+        def placed(shape, dtype, name, at):
+            return arena.tile(shape, dtype, name=name, align_bytes=64, offset=at)
 
-        def late_tile(shape, dtype, name, nbytes):
-            tile = late.tile(shape, dtype, name=name, align_bytes=64, offset=used[0])
-            used[0] = used[0] + nbytes
-            return tile
-
-        first = late.tile([P, LATE_BYTES // 4], F32, name="first", align_bytes=64, offset=0)
-        zero_in = late.tile([P, (64 + 5 * T) // 4], F32, name="zero_in", align_bytes=64, offset=LATE_BYTES)
         idx = keep.tile([P, S // 16], U16, name="idx")
         idx2 = keep.tile([P, S // 16], U16, name="idx2")
+
+        at = {}
+        end = 0
+        for name, size in (
+            ("wm00", 8 * KB), ("wm01", 8 * KB), ("tab1", 16 * KB), ("tab2", 8 * KB), ("wr0", 2 * KB),
+            ("gain", 64), ("wm10", 8 * KB), ("wr1", 2 * KB), ("wm11", 8 * KB), ("wn0", 8 * KB),
+            ("wa", 2 * KB), ("wn1", 8 * KB), ("wa_s", KB), ("late_end", 0),
+            ("tab0", 16 * KB), ("tab_s", 4 * KB), ("v_w11", 2 * KB - 64), ("tab2_s", 4 * KB + 64),
+        ):
+            at[name] = end
+            end = end + size
+
+        first = placed([P, at["late_end"] // 4], F32, "first", 0)
         wm_raw = [
             [first[:, 0 : PACK * KP].rearrange("p (j c) -> p j c", j=PACK) if (a, b) == (0, 0)
-             else late_tile([P, PACK, KP], F32, "wm_raw%d%d" % (b, a), 4 * PACK * KP) for a in range(2)]
+             else placed([P, PACK, KP], F32, "wm_raw%d%d" % (b, a), at["wm%d%d" % (b, a)]) for a in range(2)]
             for b in range(2)]
-        tab_w = [
-            late.tile([P, T], I32, name="tab_w0", align_bytes=64, offset=LATE_BYTES + 64),
-            late_tile([P, T], I32, "tab_w1", 4 * T)]
-        tab_s = held([P, T], U8, "tab_s")
-        tab2_w = late_tile([P, T // 2], I32, "tab2_w", 2 * T)
-        tab2_s = late.tile([P, T], U8, name="tab2_s", align_bytes=64, offset=LATE_BYTES + 64 + 4 * T)
-        wn_raw = [late_tile([P, PACK, N], F32, "wn_raw%d" % b, 4 * PACK * N) for b in range(2)]
-        wr_raw = [late_tile([P, KP], I32, "wr_raw%d" % b, 4 * KP) for b in range(2)]
+        tab_w = [placed([P, T], I32, "tab_w%d" % a, at["tab%d" % a]) for a in range(2)]
+        tab_s = placed([P, T], U8, "tab_s", at["tab_s"])
+        tab2_w = placed([P, T // 2], I32, "tab2_w", at["tab2"])
+        tab2_s = placed([P, T], U8, "tab2_s", at["tab2_s"])
+        wn_raw = [placed([P, PACK, N], F32, "wn_raw%d" % b, at["wn%d" % b]) for b in range(2)]
+        wr_raw = [placed([P, KP], I32, "wr_raw%d" % b, at["wr%d" % b]) for b in range(2)]
         wr_s_raw = held([P, H], U8, "wr_s_raw")
-        wa_w = late_tile([P, 2, 2 * N], U8, "wa_w", 4 * N)
-        wa_s = held([P, 2, N], U8, "wa_s")
-        gain_sb = late_tile([P, 2, PACK], F32, "gain_sb", 64)
-        drift_sb = late_tile([P, N // P], F32, "drift_sb", 64)
-        assert used[0] == LATE_BYTES
-        v_s1 = held([P, S], U8, "v_s1")
+        wa_w = placed([P, 2, 2 * N], U8, "wa_w", at["wa"])
+        wa_s = placed([P, 2, N], U8, "wa_s", at["wa_s"])
+        gain_sb = placed([P, 2, PACK], F32, "gain_sb", at["gain"])
+        drift_sb = placed([P, N // P], F32, "drift_sb", at["tab1"])
+        v_plane = [held([P, S], U8, "v_plane%d" % a) for a in range(2)]
+        zero_in = held([P, 1], F32, "zero_in")
         zero = held([P, 1], F32, "zero")
 
+        nc.gpsimd.memset(zero_in[:], 0.0)
+        nc.scalar.activation(zero[:], zero_in[:], ACT.Sin)
+        nc.vector.memset(wr_s_raw[:].bitcast(I32), 0)
         nc.vector.memset(tab_s[:].bitcast(I32), 0)
-        nc.gpsimd.memset(zero_in[:, 0:1], 0.0)
-        nc.scalar.activation(zero[:], zero_in[:, 0:1], ACT.Sin)
         nc.vector.memset(tab2_s[:].bitcast(I32), 0)
-        nc.gpsimd.memset(wr_s_raw[:].bitcast(I32), 0)
-        nc.gpsimd.memset(wa_s[:].rearrange("p a n -> p (a n)").bitcast(I32), 0)
-        nc.gpsimd.memset(v_s1[:].bitcast(I32), 0)
 
         def load_wm(b, a):
             rows = wm[KP * a : KP * (a + 1), KP * b : KP * (b + 1)]
@@ -95,76 +95,72 @@ def tile_list_attitude_propagation_kernel(
             words = wr_words[0].rearrange("p c i -> p (c i)").bitcast(I32)
             nc.sync.dma_start(wr_raw[b][:], words[:, KP * b : KP * (b + 1)])
 
-        nc.sync.dma_start(idx[:], offs)
-        nc.sync.dma_start(idx2[:], offs2)
         load_wm(0, 0)
-        for q in range(4):
-            nc.sync.dma_start(
-                tab_s[32 * q : 32 * q + 8, :].bitcast(I32), tab_scales[:, 4 * q : 4 * q + 4, :].bitcast(I32))
+        nc.sync.dma_start(idx[:], offs)
         load_tab(0)
+        nc.sync.dma_start(idx2[:], offs2)
         for q in range(4):
             nc.sync.dma_start(
-                tab2_s[32 * q : 32 * q + 4, :].bitcast(I32), tab2_scales[0, 4 * q : 4 * q + 4, :].bitcast(I32))
-        load_wm(0, 1)
-        load_tab(1)
-        nc.sync.dma_start(gain_sb[:], gain.rearrange("(b p t) -> p b t", b=2, t=PACK))
-        nc.sync.dma_start(tab2_w[:], tab2_words[0].bitcast(I32))
-        load_wr(0)
-        load_wm(1, 0)
-        nc.sync.dma_start(wa_w[:].bitcast(I32), wa_words.bitcast(I32).rearrange("a p c -> p a c"))
-        load_wm(1, 1)
-        load_wr(1)
-        load_wn(0)
-        load_wn(1)
-        with nc.allow_non_contiguous_dma(reason="one drift value a partition"):
-            nc.sync.dma_start(drift_sb[:], drift.rearrange("(c p) -> p c", p=P))
-
-        for q in range(4):
-            nc.gpsimd.dma_start(
                 wr_s_raw[32 * q : 32 * q + 4, :].bitcast(I32), wr_scales[0, 4 * q : 4 * q + 4, :].bitcast(I32))
         for q in range(4):
             nc.gpsimd.dma_start(
+                tab_s[32 * q + 4 : 32 * q + 12, :].bitcast(I32), tab_scales[:, 4 * q : 4 * q + 4, :].bitcast(I32))
+        for q in range(4):
+            nc.gpsimd.dma_start(
+                tab2_s[32 * q : 32 * q + 4, :].bitcast(I32), tab2_scales[0, 4 * q : 4 * q + 4, :].bitcast(I32))
+
+        wm_bf = [[held([P, KP * PACK], BF16, "wm_bf%d%d" % (b, a)) for a in range(2)] for b in range(2)]
+
+        def cast_wm(b, a, copy, lo, hi):
+            copy(
+                wm_bf[b][a][:].rearrange("p (t m j) -> p m j t", t=PACK, j=PACK)[:, :, :, lo:hi],
+                wm_raw[b][a][:].rearrange("p j (m t) -> p m j t", t=PACK)[:, :, :, lo:hi])
+
+        cast_wm(0, 0, nc.scalar.copy, 0, PACK)
+
+        load_wm(0, 1)
+        load_tab(1)
+        nc.sync.dma_start(tab2_w[:], tab2_words[0].bitcast(I32))
+        load_wr(0)
+        nc.sync.dma_start(gain_sb[:], gain.rearrange("(b p t) -> p b t", b=2, t=PACK))
+        load_wm(1, 0)
+        load_wr(1)
+        load_wm(1, 1)
+        load_wn(0)
+        nc.sync.dma_start(wa_w[:].bitcast(I32), wa_words.bitcast(I32).rearrange("a p c -> p a c"))
+        load_wn(1)
+        nc.gpsimd.memset(wa_s[:].rearrange("p a n -> p (a n)").bitcast(I32), 0)
+        for q in range(4):
+            nc.sync.dma_start(
                 wa_s[32 * q : 32 * q + 4, :, :].bitcast(I32),
                 wa_scales[:, 4 * q : 4 * q + 4, :].bitcast(I32).rearrange("a r n -> r a n"))
+        for a in range(2):
+            nc.gpsimd.memset(v_plane[a][:].bitcast(I32), 0)
 
         v_s = held([P, S], U8, "v_s")
-        v_w0 = held([P, S], U32, "v_w0")
-        v_w1 = [held([P, NT], U32, "v_w1%d" % j) for j in range(2)]
+        v_w0 = placed([P, S], U32, "v_w0", at["tab_s"])
+        v_w1 = [placed([P, NT], U32, "v_w10", at["tab2_s"] + 64), placed([P, NT], U32, "v_w11", at["v_w11"])]
         v2_s = held([P, S], U8, "v2_s")
-        v2_w = [late.tile([P, 2 * NT], U8, name="v2_w%d" % j, align_bytes=64, offset=TAB1_AT + 2 * NT * j)
-                for j in range(2)]
+        v2_w = [held([P, 2 * NT], U8, "v2_w%d" % j) for j in range(2)]
         half = NT // 16
 
-        mid = ctx.enter_context(tc.tile_pool(name="mid", bufs=1))
-
-        def mid_tile(shape, dtype, name, slot):
-            return mid.tile(shape, dtype, name=name, align_bytes=64, offset=4 * NT * slot)
-
-        sine_slot = {(0, 0): 1, (1, 0): 7, (0, 1): 12, (1, 1): 16}
-        woven_slot = {(0, 0): 24, (0, 1): 24, (1, 0): 26, (1, 1): 28}
-        wm_bf = [[held([P, KP * PACK], BF16, "wm_bf0%d" % a) for a in range(2)],
-                 [mid_tile([P, KP * PACK], BF16, "wm_bf10", 20), mid_tile([P, KP * PACK], BF16, "wm_bf11", 22)]]
-        wm_c = [[mid_tile([P, KP], U32, "wm_c01", 20) if (b, a) == (0, 1)
+        wm_c = [[placed([P, KP], U32, "wm_c01", at["tab2_s"] + 64 + 2 * KB) if (b, a) == (0, 1)
                  else held([P, KP], U32, "wm_c%d%d" % (b, a)) for a in range(2)] for b in range(2)]
-        wm_s = [[mid_tile([P, KP], U8, "wm_s01", 22) if (b, a) == (0, 1)
-                 else held([P, KP], U8, "wm_s%d%d" % (b, a)) for a in range(2)] for b in range(2)]
-        wn_bf = [late.tile([P, N * PACK], BF16, name="wn_bf0", align_bytes=64, offset=WM11_AT),
-                 mid_tile([P, N * PACK], BF16, "wn_bf1", 13)]
+        wm_s = [[held([P, KP], U8, "wm_s%d%d" % (b, a)) for a in range(2)] for b in range(2)]
+        wn_bf = [held([P, N * PACK], BF16, "wn_bf%d" % b) for b in range(2)]
         wn_c = [held([P, N], U32, "wn_c%d" % b) for b in range(2)]
         wn_s = [held([P, N], U8, "wn_s%d" % b) for b in range(2)]
-        wr_c = [late.tile([P, KP], I32, name="wr_c0", align_bytes=64, offset=TAB1_AT + 4 * NT),
-                late.tile([P, KP], I32, name="wr_c1", align_bytes=64, offset=WM11_AT + 2 * N * PACK)]
-        wr_s = late.tile([P, H], U8, name="wr_s", align_bytes=64, offset=LATE_BYTES + 64)
+        wr_c = [held([P, KP], I32, "wr_c%d" % b) for b in range(2)]
+        wr_s = held([P, H], U8, "wr_s")
         h_c = [[held([P, NT], U32, "h_c%d%d" % (b, j)) for j in range(2)] for b in range(2)]
         h_s = [[held([P, NT], U8, "h_s%d%d" % (b, j)) for j in range(2)] for b in range(2)]
+        planes = [[held([P, PACK, NT], BF16, "h_planes%d%d" % (b, j)) for j in range(2)] for b in range(2)]
+        woven = [[held([P, NT * PACK], BF16, "h_bf%d%d" % (b, j)) for j in range(2)] for b in range(2)]
 
-        def cast_wm(b, a, copy):
-            copy(
-                wm_bf[b][a][:].rearrange("p (t m j) -> p m j t", t=PACK, j=PACK),
-                wm_raw[b][a][:].rearrange("p j (m t) -> p m j t", t=PACK))
-
-        def quant_wm(b, a):
-            nc.vector.quantize_mx(wm_c[b][a][:].bitcast(FP8X4), wm_s[b][a][:], wm_bf[b][a][:])
+        def quant_wm(b, a, lo, hi):
+            nc.vector.quantize_mx(
+                wm_c[b][a][:, P * lo : P * hi].bitcast(FP8X4), wm_s[b][a][:, P * lo : P * hi],
+                wm_bf[b][a][:, KP * lo : KP * hi])
 
         def cast_wn(b):
             for c in range(N // P):
@@ -187,65 +183,58 @@ def tile_list_attitude_propagation_kernel(
         def v_words(a, j):
             return (v_w0[:, NT * j : NT * (j + 1)] if a == 0 else v_w1[j][:]).bitcast(FP8X4)
 
+        def bank(n, name):
+            return psum.tile([P, NT], F32, name=name, tag="bank%d" % n)
+
         phases = {}
         sines = {}
-        planes = {}
-        woven = {}
+        rates = {}
         acc = {}
 
         def phase_pass(b, j, t, a):
             cols = slice(P * t, P * (t + 1))
             nc.tensor.matmul_mx(
                 phases[b, j, t][:], lhsT=wm_c[b][a][:, cols].bitcast(FP8X4), lhsT_scale=wm_s[b][a][:, cols],
-                rhs=v_words(a, j), rhs_scale=v_s[4 * a :, NT * j : NT * (j + 1)], start=(a == 0), stop=(a == 1))
+                rhs=v_words(a, j), rhs_scale=v_s[4 * (a + 1) :, NT * j : NT * (j + 1)],
+                start=(a == 0), stop=(a == 1))
 
-        def open_phase(b, j, t):
-            phase = psum.tile([P, NT], F32, name="phase", tag=("sum%d" if (b, j) == (0, 1) else "work%d") % t)
-            phases[b, j, t] = phase
+        def open_phase(b, j, t, n):
+            phases[b, j, t] = bank(n, "phase")
             phase_pass(b, j, t, 0)
 
         def kick(b, j, t):
             phase_pass(b, j, t, 1)
-            sine = mid_tile([P, NT], F32, "sine%d%d%d" % (b, j, t), sine_slot[b, j] + t)
+            sine = ring.tile([P, NT], F32, name="sine", tag="sine%d%d" % (j, t), align_bytes=64)
             nc.scalar.activation(sine[:], phases[b, j, t][:], ACT.Sin, bias=zero[:], scale=-1.0)
             sines[b, j, t] = sine
 
-        def new_rate(b, j, t):
-            toks = slice(NT * j, NT * (j + 1))
-            rate = psum.tile([P, NT], F32, name="rate", tag=("sum%d" if (b, j) == (0, 0) else "work%d") % t)
+        def old_rate(b, j, t, n):
+            rates[b, j, t] = bank(n, "rate")
             nc.tensor.matmul_mx(
-                rate[:], lhsT=wr_c[b][:, P * t : P * (t + 1)].bitcast(FP8X4),
+                rates[b, j, t][:], lhsT=wr_c[b][:, P * t : P * (t + 1)].bitcast(FP8X4),
                 lhsT_scale=wr_s[:, KP * b + P * t : KP * b + P * (t + 1)],
-                rhs=v2_w[j][:].bitcast(FP4X4), rhs_scale=v2_s[:, toks], start=True, stop=True)
-            if t == 0:
-                planes[b, j] = ring.tile([P, PACK, NT], BF16, name="h_planes", tag="h_planes", bufs=3, align_bytes=64)
+                rhs=v2_w[j][:].bitcast(FP4X4), rhs_scale=v2_s[:, NT * j : NT * (j + 1)], start=True, stop=True)
+
+        def new_rate(b, j, t):
             nc.vector.scalar_tensor_tensor(
-                planes[b, j][:, t, :], sines[b, j, t][:], gain_sb[:, b, t : t + 1], rate[:], ALU.mult, ALU.add)
+                planes[b][j][:, t, :], sines[b, j, t][:], gain_sb[:, b, t : t + 1], rates[b, j, t][:],
+                ALU.mult, ALU.add)
 
-        def weave(b, j, shares):
-            woven[b, j] = mid_tile([P, NT * PACK], BF16, "h_bf%d%d" % (b, j), woven_slot[b, j])
-            for copy, lo, hi in shares:
-                copy(
-                    woven[b, j][:, PACK * lo : PACK * hi].rearrange("p (u i t) -> p u t i", i=4, t=PACK),
-                    planes[b, j][:, :, lo:hi].rearrange("p t (u i) -> p u t i", i=4))
-
-        def weave_on_gpsimd(b, j):
-            woven[b, j] = mid_tile([P, NT * PACK], BF16, "h_bf%d%d" % (b, j), woven_slot[b, j])
-            nc.gpsimd.tensor_scalar(
-                woven[b, j][:].rearrange("p (n t) -> p n t", t=PACK),
-                planes[b, j][:].rearrange("p t n -> p n t"), 1.0, 0.0, ALU.mult, ALU.add)
+        def weave(b, j, copy, lo, hi):
+            copy(
+                woven[b][j][:, PACK * lo : PACK * hi].rearrange("p (u i t) -> p u t i", i=4, t=PACK),
+                planes[b][j][:, :, lo:hi].rearrange("p t (u i) -> p u t i", i=4))
 
         def quant_h(b, j):
-            nc.vector.quantize_mx(h_c[b][j][:].bitcast(FP8X4), h_s[b][j][:], woven[b, j][:])
+            nc.vector.quantize_mx(h_c[b][j][:].bitcast(FP8X4), h_s[b][j][:], woven[b][j][:])
 
-        def open_angle(j, c):
-            toks = slice(NT * j, NT * (j + 1))
-            acc[j, c] = psum.tile([P, NT], F32, name="angle", tag=("sum%d" if j == 0 else "work%d") % c)
+        def open_angle(j, c, n):
+            acc[j, c] = bank(n, "angle")
             for a in range(2):
                 nc.tensor.matmul_mx(
                     acc[j, c][:], lhsT=wa_w[:, a, 2 * P * c : 2 * P * (c + 1)].bitcast(FP4X4),
                     lhsT_scale=wa_s[:, a, P * c : P * (c + 1)],
-                    rhs=v_words(a, j), rhs_scale=(v_s if a == 0 else v_s1)[:, toks],
+                    rhs=v_words(a, j), rhs_scale=v_plane[a][:, NT * j : NT * (j + 1)],
                     start=(a == 0), stop=False)
 
         def add_h(b, j, c):
@@ -255,84 +244,91 @@ def tile_list_attitude_propagation_kernel(
                 rhs=h_c[b][j][:].bitcast(FP8X4), rhs_scale=h_s[b][j][:], start=False, stop=(b == 1))
 
         def finish(j, c, on_vector):
-            res = ring.tile([P, NT], F32, name="res", tag="res", bufs=8)
+            res = placed([P, NT], F32, "res%d%d" % (j, c), at["tab0"] + 2 * KB * (4 * j + c))
             if on_vector:
                 nc.vector.tensor_scalar(res[:], acc[j, c][:], drift_sb[:, c : c + 1], None, ALU.add)
             else:
                 nc.scalar.activation(res[:], acc[j, c][:], ACT.Identity, bias=drift_sb[:, c : c + 1])
             nc.sync.dma_start(out[P * c : P * (c + 1), NT * j : NT * (j + 1)], res[:])
 
-        cast_wm(0, 0, nc.scalar.copy)
-        nc.vector.tensor_copy(v_s[:], tab_s[:].indirect(idx[:]))
-        nc.gpsimd.dma_start(v_s1[0:100, :].bitcast(I32), v_s[4:104, :].bitcast(I32))
-        nc.vector.tensor_copy(v_w0[:], tab_w[0][:].bitcast(U32).indirect(idx[:]))
-        quant_wm(0, 0)
-        nc.vector.tensor_copy(v2_s[:], tab2_s[:].indirect(idx2[:]))
-        cast_wm(0, 1, nc.scalar.copy)
         nc.vector.tensor_copy(
             wr_s[:].rearrange("p (b t m) -> p b t m", b=2, t=PACK),
             wr_s_raw[:].rearrange("p (b m t) -> p b t m", b=2, t=PACK))
-        quant_wm(0, 1)
+        quant_wm(0, 0, 0, PACK)
+        nc.vector.tensor_copy(v_s[:], tab_s[:].indirect(idx[:]))
+        for a in range(2):
+            nc.sync.dma_start(v_plane[a][0:100, :].bitcast(I32), v_s[4 * (a + 1) : 4 * (a + 1) + 100, :].bitcast(I32))
+        nc.vector.tensor_copy(v_w0[:], tab_w[0][:].bitcast(U32).indirect(idx[:]))
+        nc.vector.tensor_copy(v2_s[:], tab2_s[:].indirect(idx2[:]))
+        cast_wm(0, 1, nc.scalar.copy, 0, PACK)
+        quant_wm(0, 1, 0, PACK)
         for j in range(2):
             nc.vector.tensor_copy(
                 v_w1[j][:], tab_w[1][:].bitcast(U32).indirect(idx[:, half * j : half * (j + 1)]))
+        with nc.allow_non_contiguous_dma(reason="one drift value a partition"):
+            nc.sync.dma_start(drift_sb[:], drift.rearrange("(c p) -> p c", p=P))
         gather_v2(0)
         order_wr(0)
-
-        on_vector = [(nc.vector.tensor_copy, 0, NT)]
-        shared = [(nc.vector.tensor_copy, 0, LAST_SPLIT), (nc.scalar.copy, LAST_SPLIT, NT)]
+        gather_v2(1)
 
         for j in range(2):
             for t in range(PACK):
-                open_phase(0, j, t)
+                open_phase(0, j, t, 4 * j + t)
+        for j in range(2):
+            for t in range(PACK):
+                kick(0, j, t)
         for t in range(PACK):
-            kick(0, 0, t)
-        gather_v2(1)
-        for t in range(PACK):
-            kick(0, 1, t)
-        cast_wm(1, 0, nc.scalar.copy)
-        cast_wm(1, 1, nc.scalar.copy)
-        for t in range(PACK):
+            old_rate(0, 0, t, t)
             new_rate(0, 0, t)
-        quant_wm(1, 0)
-        quant_wm(1, 1)
         order_wr(1)
         for t in range(PACK):
+            old_rate(0, 1, t, 4 + t)
             new_rate(0, 1, t)
-        for c in range(4):
-            open_angle(0, c)
+        cast_wm(1, 0, nc.scalar.copy, 0, PACK)
+        quant_wm(1, 0, 0, PACK)
+        cast_wm(1, 1, nc.scalar.copy, 0, 2)
+        cast_wm(1, 1, nc.vector.tensor_copy, 2, PACK)
         for t in range(PACK):
-            open_phase(1, 0, t)
+            old_rate(1, 0, t, 4 + t)
+        for t in range(PACK):
+            open_phase(1, 0, t, t)
+        quant_wm(1, 1, 0, 2)
+        quant_wm(1, 1, 2, PACK)
+        cast_wn(0)
+        weave(0, 0, nc.vector.tensor_copy, 0, NT)
         for t in range(PACK):
             kick(1, 0, t)
-        weave(0, 0, on_vector)
-        new_rate(1, 0, 0)
         quant_h(0, 0)
-        weave_on_gpsimd(0, 1)
-        for t in range(1, PACK):
-            new_rate(1, 0, t)
-        cast_wn(0)
-        cast_wn(1)
-        for t in range(PACK):
-            open_phase(1, 1, t)
-            kick(1, 1, t)
         quant_wn(0)
-        weave(1, 0, on_vector)
-        quant_wn(1)
-        quant_h(1, 0)
+        for t in range(PACK):
+            new_rate(1, 0, t)
+        for t in range(PACK):
+            open_phase(1, 1, t, t)
+            kick(1, 1, t)
+        cast_wn(1)
+        weave(1, 0, nc.vector.tensor_copy, 0, NT)
         for c in range(4):
+            old_rate(1, 1, c, c)
+            open_angle(0, c, 4 + c)
             add_h(0, 0, c)
-        for c in range(4):
-            new_rate(1, 1, c)
+        new_rate(1, 1, 0)
+        quant_h(1, 0)
+        new_rate(1, 1, 1)
+        new_rate(1, 1, 2)
+        quant_wn(1)
+        new_rate(1, 1, 3)
+        weave(0, 1, nc.scalar.copy, 0, NT // 2)
         for c in range(4):
             add_h(1, 0, c)
             finish(0, c, False)
+        weave(0, 1, nc.vector.tensor_copy, NT // 2, NT)
+        weave(1, 1, nc.vector.tensor_copy, 0, NT)
         quant_h(0, 1)
-        for c in range(4):
-            open_angle(1, c)
-            add_h(0, 1, c)
-        weave(1, 1, shared)
         quant_h(1, 1)
         for c in range(4):
+            open_angle(1, c, c)
+        for c in range(4):
+            add_h(0, 1, c)
+        for c in range(4):
             add_h(1, 1, c)
-            finish(1, c, c % 2 == 1)
+            finish(1, c, c % 2 == 0)

@@ -30,7 +30,6 @@ def tile_list_attitude_propagation_kernel(
     nc = tc.nc
     with ExitStack() as ctx:
         keep = ctx.enter_context(tc.tile_pool(name="keep", bufs=1))
-        ring = ctx.enter_context(tc.tile_pool(name="ring", bufs=1))
         arena = ctx.enter_context(tc.tile_pool(name="arena", bufs=1))
         psum = ctx.enter_context(tc.psum_pool(name="psum", bufs=1))
 
@@ -46,39 +45,40 @@ def tile_list_attitude_propagation_kernel(
         at = {}
         end = 0
         for name, size in (
-            ("wm00", 8 * KB), ("wm01", 8 * KB), ("tab1", 16 * KB), ("tab2", 8 * KB), ("wr0", 2 * KB),
-            ("gain", 64), ("wm10", 8 * KB), ("wr1", 2 * KB), ("wm11", 8 * KB), ("wn0", 8 * KB),
-            ("wa", 2 * KB), ("wn1", 8 * KB), ("wa_s", KB), ("late_end", 0),
-            ("tab0", 16 * KB), ("tab_s", 4 * KB), ("v_w11", 2 * KB - 64), ("tab2_s", 4 * KB + 64),
+            ("tab_s", 4 * KB), ("planes", 2 * KB), ("tab1", 16 * KB), ("first_end", 0),
+            ("tab2_s", 4 * KB), ("v2_plane", KB), ("wa_s", KB),
+            ("tab2", 8 * KB), ("wr", 4 * KB), ("gain", 64), ("wm10", 8 * KB), ("wm11", 8 * KB),
+            ("wn0", 8 * KB), ("wa", 2 * KB), ("wn1", 8 * KB), ("drift", 64), ("late_end", 0),
+            ("wm00", 8 * KB), ("wm01", 8 * KB), ("early", 64), ("wr_s", KB), ("tab0", 16 * KB), ("early_end", 0),
+            ("sine0", 8 * KB), ("sine1", 8 * KB), ("wm_bf10", 4 * KB), ("wn_bf1", 4 * KB),
         ):
             at[name] = end
             end = end + size
 
-        first = placed([P, at["late_end"] // 4], F32, "first", 0)
-        wm_raw = [
-            [first[:, 0 : PACK * KP].rearrange("p (j c) -> p j c", j=PACK) if (a, b) == (0, 0)
-             else placed([P, PACK, KP], F32, "wm_raw%d%d" % (b, a), at["wm%d%d" % (b, a)]) for a in range(2)]
-            for b in range(2)]
+        first = placed([P, at["first_end"]], U8, "first", 0)
+        second = placed([P, at["late_end"] - at["tab2_s"]], U8, "second", at["tab2_s"])
+        tab2_s = second[:, 0:T]
+        tab_s = first[:, 0:T]
+        wm_raw = [[placed([P, PACK, KP], F32, "wm_raw%d%d" % (b, a), at["wm%d%d" % (b, a)]) for a in range(2)]
+                  for b in range(2)]
         tab_w = [placed([P, T], I32, "tab_w%d" % a, at["tab%d" % a]) for a in range(2)]
-        tab_s = placed([P, T], U8, "tab_s", at["tab_s"])
         tab2_w = placed([P, T // 2], I32, "tab2_w", at["tab2"])
-        tab2_s = placed([P, T], U8, "tab2_s", at["tab2_s"])
         wn_raw = [placed([P, PACK, N], F32, "wn_raw%d" % b, at["wn%d" % b]) for b in range(2)]
-        wr_raw = [placed([P, KP], I32, "wr_raw%d" % b, at["wr%d" % b]) for b in range(2)]
-        wr_s_raw = held([P, H], U8, "wr_s_raw")
+        wr_raw = placed([P, H], I32, "wr_raw", at["wr"])
+        early = placed([P, (at["early_end"] - at["early"]) // 4], F32, "early", at["early"])
         wa_w = placed([P, 2, 2 * N], U8, "wa_w", at["wa"])
         wa_s = placed([P, 2, N], U8, "wa_s", at["wa_s"])
         gain_sb = placed([P, 2, PACK], F32, "gain_sb", at["gain"])
-        drift_sb = placed([P, N // P], F32, "drift_sb", at["tab1"])
-        v_plane = [held([P, S], U8, "v_plane%d" % a) for a in range(2)]
-        zero_in = held([P, 1], F32, "zero_in")
-        zero = held([P, 1], F32, "zero")
+        drift_sb = placed([P, N // P], F32, "drift_sb", at["drift"])
+        v_plane = [placed([P, S], U8, "v_plane%d" % a, at["planes"] + KB * a) for a in range(2)]
+        v2_plane = placed([P, S], U8, "v2_plane", at["v2_plane"])
+        zero_in = placed([P, 1], F32, "zero_in", at["wn_bf1"])
+        zero = placed([P, 1], F32, "zero", at["wm_bf10"])
 
-        nc.gpsimd.memset(zero_in[:], 0.0)
-        nc.scalar.activation(zero[:], zero_in[:], ACT.Sin)
-        nc.vector.memset(wr_s_raw[:].bitcast(I32), 0)
-        nc.vector.memset(tab_s[:].bitcast(I32), 0)
-        nc.vector.memset(tab2_s[:].bitcast(I32), 0)
+        nc.vector.memset(first[:, 0 : at["tab1"]].bitcast(I32), 0)
+        nc.vector.memset(second[:, 0 : at["tab2"] - at["tab2_s"]].bitcast(I32), 0)
+        nc.vector.memset(early[:, 0:1], 0.0)
+        nc.vector.tensor_copy(zero_in[:], early[:, 0:1])
 
         def load_wm(b, a):
             rows = wm[KP * a : KP * (a + 1), KP * b : KP * (b + 1)]
@@ -88,28 +88,42 @@ def tile_list_attitude_propagation_kernel(
             rows = wn[KP * b : KP * (b + 1), :]
             nc.sync.dma_start(wn_raw[b][:], rows.rearrange("(p t) n -> p t n", t=PACK))
 
-        def load_tab(a):
-            nc.sync.dma_start(tab_w[a][:], tab_words[a].rearrange("p t i -> p (t i)").bitcast(I32))
+        def load_tab(a, lo=0, hi=T):
+            words = tab_words[a].rearrange("p t i -> p (t i)").bitcast(I32)
+            nc.sync.dma_start(tab_w[a][:, lo:hi], words[:, lo:hi])
 
-        def load_wr(b):
-            words = wr_words[0].rearrange("p c i -> p (c i)").bitcast(I32)
-            nc.sync.dma_start(wr_raw[b][:], words[:, KP * b : KP * (b + 1)])
-
-        load_wm(0, 0)
-        nc.sync.dma_start(idx[:], offs)
-        load_tab(0)
-        nc.sync.dma_start(idx2[:], offs2)
-        for q in range(4):
+        def load_wr_scales(q):
             nc.sync.dma_start(
                 wr_s_raw[32 * q : 32 * q + 4, :].bitcast(I32), wr_scales[0, 4 * q : 4 * q + 4, :].bitcast(I32))
-        for q in range(4):
-            nc.gpsimd.dma_start(
-                tab_s[32 * q + 4 : 32 * q + 12, :].bitcast(I32), tab_scales[:, 4 * q : 4 * q + 4, :].bitcast(I32))
-        for q in range(4):
-            nc.gpsimd.dma_start(
-                tab2_s[32 * q : 32 * q + 4, :].bitcast(I32), tab2_scales[0, 4 * q : 4 * q + 4, :].bitcast(I32))
 
-        wm_bf = [[held([P, KP * PACK], BF16, "wm_bf%d%d" % (b, a)) for a in range(2)] for b in range(2)]
+        nc.sync.dma_start(idx[:], offs)
+        nc.sync.dma_start(idx2[:], offs2)
+        load_wm(0, 0)
+        load_wm(0, 1)
+        nc.scalar.dma_start(
+            tab_s[0:P:4, :].bitcast(I32), tab_scales.rearrange("a q t -> (a q) t").bitcast(I32))
+        nc.scalar.dma_start(tab2_s[0:P:8, :].bitcast(I32), tab2_scales[0].bitcast(I32))
+        nc.scalar.activation(zero[:], zero_in[:], ACT.Sin)
+        load_tab(0)
+        wr_s_raw = placed([P, H], U8, "wr_s_raw", at["wr_s"])
+        nc.vector.memset(wr_s_raw[:].bitcast(I32), 0)
+        for q in range(4):
+            load_wr_scales(q)
+
+        v_s = held([P, S], U8, "v_s")
+        v2_s = held([P, S], U8, "v2_s")
+        nc.vector.tensor_copy(v_s[:], tab_s.indirect(idx[:]))
+        nc.vector.tensor_copy(v2_s[:], tab2_s.indirect(idx2[:]))
+
+        def move_rows(plane, gathered, start, step_r, step_q):
+            for r in range(4):
+                lo = start + step_r * r
+                nc.sync.dma_start(
+                    plane[r:P:32, :].bitcast(I32), gathered[lo : lo + 3 * step_q + 1 : step_q, :].bitcast(I32))
+
+        wm_bf = [[held([P, KP * PACK], BF16, "wm_bf0%d" % a) for a in range(2)],
+                 [placed([P, KP * PACK], BF16, "wm_bf10", at["wm_bf10"]),
+                  placed([P, KP * PACK], BF16, "wm_bf11", at["sine0"] + 2 * KB)]]
 
         def cast_wm(b, a, copy, lo, hi):
             copy(
@@ -118,39 +132,37 @@ def tile_list_attitude_propagation_kernel(
 
         cast_wm(0, 0, nc.scalar.copy, 0, PACK)
 
-        load_wm(0, 1)
-        load_tab(1)
+        load_tab(1, 0, T // 2)
+        move_rows(v_plane[0], v_s, 0, 4, 16)
+        load_tab(1, T // 2, T)
+        move_rows(v_plane[1], v_s, 64, 4, 16)
+        nc.sync.dma_start(wr_raw[:], wr_words[0].rearrange("p c i -> p (c i)").bitcast(I32))
         nc.sync.dma_start(tab2_w[:], tab2_words[0].bitcast(I32))
-        load_wr(0)
+        move_rows(v2_plane, v2_s, 0, 8, 32)
         nc.sync.dma_start(gain_sb[:], gain.rearrange("(b p t) -> p b t", b=2, t=PACK))
         load_wm(1, 0)
-        load_wr(1)
         load_wm(1, 1)
         load_wn(0)
         nc.sync.dma_start(wa_w[:].bitcast(I32), wa_words.bitcast(I32).rearrange("a p c -> p a c"))
         load_wn(1)
-        nc.gpsimd.memset(wa_s[:].rearrange("p a n -> p (a n)").bitcast(I32), 0)
         for q in range(4):
             nc.sync.dma_start(
                 wa_s[32 * q : 32 * q + 4, :, :].bitcast(I32),
                 wa_scales[:, 4 * q : 4 * q + 4, :].bitcast(I32).rearrange("a r n -> r a n"))
-        for a in range(2):
-            nc.gpsimd.memset(v_plane[a][:].bitcast(I32), 0)
+        with nc.allow_non_contiguous_dma(reason="one drift value a partition"):
+            nc.sync.dma_start(drift_sb[:], drift.rearrange("(c p) -> p c", p=P))
 
-        v_s = held([P, S], U8, "v_s")
-        v_w0 = placed([P, S], U32, "v_w0", at["tab_s"])
-        v_w1 = [placed([P, NT], U32, "v_w10", at["tab2_s"] + 64), placed([P, NT], U32, "v_w11", at["v_w11"])]
-        v2_s = held([P, S], U8, "v2_s")
+        v_w0 = held([P, S], U32, "v_w0")
+        v_w1 = [held([P, NT], U32, "v_w1%d" % j) for j in range(2)]
         v2_w = [held([P, 2 * NT], U8, "v2_w%d" % j) for j in range(2)]
         half = NT // 16
 
-        wm_c = [[placed([P, KP], U32, "wm_c01", at["tab2_s"] + 64 + 2 * KB) if (b, a) == (0, 1)
-                 else held([P, KP], U32, "wm_c%d%d" % (b, a)) for a in range(2)] for b in range(2)]
+        wm_c = [[held([P, KP], U32, "wm_c%d%d" % (b, a)) for a in range(2)] for b in range(2)]
         wm_s = [[held([P, KP], U8, "wm_s%d%d" % (b, a)) for a in range(2)] for b in range(2)]
-        wn_bf = [held([P, N * PACK], BF16, "wn_bf%d" % b) for b in range(2)]
+        wn_bf = [held([P, N * PACK], BF16, "wn_bf0"), placed([P, N * PACK], BF16, "wn_bf1", at["wn_bf1"])]
         wn_c = [held([P, N], U32, "wn_c%d" % b) for b in range(2)]
         wn_s = [held([P, N], U8, "wn_s%d" % b) for b in range(2)]
-        wr_c = [held([P, KP], I32, "wr_c%d" % b) for b in range(2)]
+        wr_c = held([P, H], I32, "wr_c")
         wr_s = held([P, H], U8, "wr_s")
         h_c = [[held([P, NT], U32, "h_c%d%d" % (b, j)) for j in range(2)] for b in range(2)]
         h_s = [[held([P, NT], U8, "h_s%d%d" % (b, j)) for j in range(2)] for b in range(2)]
@@ -171,11 +183,6 @@ def tile_list_attitude_propagation_kernel(
         def quant_wn(b):
             nc.vector.quantize_mx(wn_c[b][:].bitcast(FP8X4), wn_s[b][:], wn_bf[b][:])
 
-        def order_wr(b):
-            nc.vector.tensor_copy(
-                wr_c[b][:].rearrange("p (t u i) -> p u t i", t=PACK, i=4),
-                wr_raw[b][:].rearrange("p (u i t) -> p u t i", t=PACK, i=4))
-
         def gather_v2(j):
             nc.vector.tensor_copy(
                 v2_w[j][:].bitcast(U16), tab2_w[:].bitcast(U16).indirect(idx2[:, half * j : half * (j + 1)]))
@@ -195,7 +202,7 @@ def tile_list_attitude_propagation_kernel(
             cols = slice(P * t, P * (t + 1))
             nc.tensor.matmul_mx(
                 phases[b, j, t][:], lhsT=wm_c[b][a][:, cols].bitcast(FP8X4), lhsT_scale=wm_s[b][a][:, cols],
-                rhs=v_words(a, j), rhs_scale=v_s[4 * (a + 1) :, NT * j : NT * (j + 1)],
+                rhs=v_words(a, j), rhs_scale=v_plane[a][:, NT * j : NT * (j + 1)],
                 start=(a == 0), stop=(a == 1))
 
         def open_phase(b, j, t, n):
@@ -204,16 +211,16 @@ def tile_list_attitude_propagation_kernel(
 
         def kick(b, j, t):
             phase_pass(b, j, t, 1)
-            sine = ring.tile([P, NT], F32, name="sine", tag="sine%d%d" % (j, t), align_bytes=64)
-            nc.scalar.activation(sine[:], phases[b, j, t][:], ACT.Sin, bias=zero[:], scale=-1.0)
+            sine = placed([P, NT], F32, "sine%d%d%d" % (b, j, t), at["sine%d" % j] + 2 * KB * t)
+            nc.scalar.activation(sine[:], phases[b, j, t][:], ACT.Sin, bias=(zero, zero_in)[b][:], scale=-1.0)
             sines[b, j, t] = sine
 
         def old_rate(b, j, t, n):
             rates[b, j, t] = bank(n, "rate")
             nc.tensor.matmul_mx(
-                rates[b, j, t][:], lhsT=wr_c[b][:, P * t : P * (t + 1)].bitcast(FP8X4),
+                rates[b, j, t][:], lhsT=wr_c[:, KP * b + P * t : KP * b + P * (t + 1)].bitcast(FP8X4),
                 lhsT_scale=wr_s[:, KP * b + P * t : KP * b + P * (t + 1)],
-                rhs=v2_w[j][:].bitcast(FP4X4), rhs_scale=v2_s[:, NT * j : NT * (j + 1)], start=True, stop=True)
+                rhs=v2_w[j][:].bitcast(FP4X4), rhs_scale=v2_plane[:, NT * j : NT * (j + 1)], start=True, stop=True)
 
         def new_rate(b, j, t):
             nc.vector.scalar_tensor_tensor(
@@ -251,36 +258,32 @@ def tile_list_attitude_propagation_kernel(
                 nc.scalar.activation(res[:], acc[j, c][:], ACT.Identity, bias=drift_sb[:, c : c + 1])
             nc.sync.dma_start(out[P * c : P * (c + 1), NT * j : NT * (j + 1)], res[:])
 
+        quant_wm(0, 0, 0, PACK)
+        cast_wm(0, 1, nc.scalar.copy, 0, PACK)
+        quant_wm(0, 1, 0, PACK)
         nc.vector.tensor_copy(
             wr_s[:].rearrange("p (b t m) -> p b t m", b=2, t=PACK),
             wr_s_raw[:].rearrange("p (b m t) -> p b t m", b=2, t=PACK))
-        quant_wm(0, 0, 0, PACK)
-        nc.vector.tensor_copy(v_s[:], tab_s[:].indirect(idx[:]))
-        for a in range(2):
-            nc.sync.dma_start(v_plane[a][0:100, :].bitcast(I32), v_s[4 * (a + 1) : 4 * (a + 1) + 100, :].bitcast(I32))
         nc.vector.tensor_copy(v_w0[:], tab_w[0][:].bitcast(U32).indirect(idx[:]))
-        nc.vector.tensor_copy(v2_s[:], tab2_s[:].indirect(idx2[:]))
-        cast_wm(0, 1, nc.scalar.copy, 0, PACK)
-        quant_wm(0, 1, 0, PACK)
         for j in range(2):
             nc.vector.tensor_copy(
                 v_w1[j][:], tab_w[1][:].bitcast(U32).indirect(idx[:, half * j : half * (j + 1)]))
-        with nc.allow_non_contiguous_dma(reason="one drift value a partition"):
-            nc.sync.dma_start(drift_sb[:], drift.rearrange("(c p) -> p c", p=P))
+        nc.vector.tensor_copy(
+            wr_c[:].rearrange("p (b t u i) -> p b u t i", b=2, t=PACK, i=4),
+            wr_raw[:].rearrange("p (b u i t) -> p b u t i", b=2, t=PACK, i=4))
         gather_v2(0)
-        order_wr(0)
         gather_v2(1)
 
         for j in range(2):
             for t in range(PACK):
                 open_phase(0, j, t, 4 * j + t)
-        for j in range(2):
-            for t in range(PACK):
-                kick(0, j, t)
+        for t in range(PACK):
+            kick(0, 0, t)
+        for t in range(PACK):
+            kick(0, 1, t)
         for t in range(PACK):
             old_rate(0, 0, t, t)
             new_rate(0, 0, t)
-        order_wr(1)
         for t in range(PACK):
             old_rate(0, 1, t, 4 + t)
             new_rate(0, 1, t)

@@ -21,6 +21,7 @@ PACK = 4
 KP = P * PACK
 NT = 512
 KB = 1024
+SPLIT = 416
 
 
 def tile_list_attitude_propagation_kernel(
@@ -50,7 +51,7 @@ def tile_list_attitude_propagation_kernel(
             ("tab2", 8 * KB), ("wr", 4 * KB), ("gain", 64), ("wm10", 8 * KB), ("wm11", 8 * KB),
             ("wn0", 8 * KB), ("wa", 2 * KB), ("wn1", 8 * KB), ("drift", 64), ("late_end", 0),
             ("wm00", 8 * KB), ("wm01", 8 * KB), ("early", 64), ("wr_s", KB), ("tab0", 16 * KB), ("early_end", 0),
-            ("sine0", 8 * KB), ("sine1", 8 * KB), ("wm_bf10", 4 * KB), ("wn_bf1", 4 * KB),
+            ("sine0", 8 * KB), ("sine1", 8 * KB), ("wm_bf10", 4 * KB), ("wn_bf", 4 * KB), ("h_bf01", 4 * KB), ("h_bf1", 4 * KB),
         ):
             at[name] = end
             end = end + size
@@ -72,11 +73,11 @@ def tile_list_attitude_propagation_kernel(
         drift_sb = placed([P, N // P], F32, "drift_sb", at["drift"])
         v_plane = [placed([P, S], U8, "v_plane%d" % a, at["planes"] + KB * a) for a in range(2)]
         v2_plane = placed([P, S], U8, "v2_plane", at["v2_plane"])
-        zero_in = placed([P, 1], F32, "zero_in", at["wn_bf1"])
+        zero_in = placed([P, 1], F32, "zero_in", at["h_bf01"])
         zero = placed([P, 1], F32, "zero", at["wm_bf10"])
 
-        nc.vector.memset(first[:, 0 : at["tab1"]].bitcast(I32), 0)
-        nc.vector.memset(second[:, 0 : at["tab2"] - at["tab2_s"]].bitcast(I32), 0)
+        nc.vector.memset(first[:, 0:T].bitcast(I32), 0)
+        nc.vector.memset(second[:, 0:T].bitcast(I32), 0)
         nc.vector.memset(early[:, 0:1], 0.0)
         nc.vector.tensor_copy(zero_in[:], early[:, 0:1])
 
@@ -143,8 +144,8 @@ def tile_list_attitude_propagation_kernel(
         load_wm(1, 0)
         load_wm(1, 1)
         load_wn(0)
-        nc.sync.dma_start(wa_w[:].bitcast(I32), wa_words.bitcast(I32).rearrange("a p c -> p a c"))
         load_wn(1)
+        nc.sync.dma_start(wa_w[:].bitcast(I32), wa_words.bitcast(I32).rearrange("a p c -> p a c"))
         for q in range(4):
             nc.sync.dma_start(
                 wa_s[32 * q : 32 * q + 4, :, :].bitcast(I32),
@@ -159,24 +160,25 @@ def tile_list_attitude_propagation_kernel(
 
         wm_c = [[held([P, KP], U32, "wm_c%d%d" % (b, a)) for a in range(2)] for b in range(2)]
         wm_s = [[held([P, KP], U8, "wm_s%d%d" % (b, a)) for a in range(2)] for b in range(2)]
-        wn_bf = [held([P, N * PACK], BF16, "wn_bf0"), placed([P, N * PACK], BF16, "wn_bf1", at["wn_bf1"])]
-        wn_c = [held([P, N], U32, "wn_c%d" % b) for b in range(2)]
+        wn_bf = [placed([P, N * PACK], BF16, "wn_bf%d" % b, at["wn_bf"]) for b in range(2)]
+        wn_c = [held([P, N], U32, "wn_c0"), placed([P, N], U32, "wn_c1", at["sine1"] + 6 * KB)]
         wn_s = [held([P, N], U8, "wn_s%d" % b) for b in range(2)]
         wr_c = held([P, H], I32, "wr_c")
         wr_s = held([P, H], U8, "wr_s")
         h_c = [[held([P, NT], U32, "h_c%d%d" % (b, j)) for j in range(2)] for b in range(2)]
         h_s = [[held([P, NT], U8, "h_s%d%d" % (b, j)) for j in range(2)] for b in range(2)]
         planes = [[held([P, PACK, NT], BF16, "h_planes%d%d" % (b, j)) for j in range(2)] for b in range(2)]
-        woven = [[held([P, NT * PACK], BF16, "h_bf%d%d" % (b, j)) for j in range(2)] for b in range(2)]
+        woven = [[held([P, NT * PACK], BF16, "h_bf00"), placed([P, NT * PACK], BF16, "h_bf01", at["h_bf01"])],
+                 [placed([P, NT * PACK], BF16, "h_bf1%d" % j, at["h_bf1"]) for j in range(2)]]
 
         def quant_wm(b, a, lo, hi):
             nc.vector.quantize_mx(
                 wm_c[b][a][:, P * lo : P * hi].bitcast(FP8X4), wm_s[b][a][:, P * lo : P * hi],
                 wm_bf[b][a][:, KP * lo : KP * hi])
 
-        def cast_wn(b):
-            for c in range(N // P):
-                nc.scalar.copy(
+        def cast_wn(b, copy, lo, hi):
+            for c in range(lo, hi):
+                copy(
                     wn_bf[b][:, PACK * P * c : PACK * P * (c + 1)].rearrange("p (u i t) -> p u t i", i=4, t=PACK),
                     wn_raw[b][:, :, P * c : P * (c + 1)].rearrange("p t (u i) -> p u t i", i=4))
 
@@ -232,6 +234,11 @@ def tile_list_attitude_propagation_kernel(
                 woven[b][j][:, PACK * lo : PACK * hi].rearrange("p (u i t) -> p u t i", i=4, t=PACK),
                 planes[b][j][:, :, lo:hi].rearrange("p t (u i) -> p u t i", i=4))
 
+        def interleave_on_gpsimd(dst, src, lo, hi):
+            nc.gpsimd.tensor_scalar(
+                dst[:, PACK * lo : PACK * hi].rearrange("p (n t) -> p n t", t=PACK),
+                src[:, :, lo:hi].rearrange("p t n -> p n t"), 1.0, 0.0, ALU.mult, ALU.add)
+
         def quant_h(b, j):
             nc.vector.quantize_mx(h_c[b][j][:].bitcast(FP8X4), h_s[b][j][:], woven[b][j][:])
 
@@ -277,61 +284,70 @@ def tile_list_attitude_propagation_kernel(
         for j in range(2):
             for t in range(PACK):
                 open_phase(0, j, t, 4 * j + t)
-        for t in range(PACK):
-            kick(0, 0, t)
-        for t in range(PACK):
-            kick(0, 1, t)
+        for j in range(2):
+            for t in range(PACK):
+                kick(0, j, t)
         for t in range(PACK):
             old_rate(0, 0, t, t)
             new_rate(0, 0, t)
         for t in range(PACK):
             old_rate(0, 1, t, 4 + t)
-            new_rate(0, 1, t)
+        new_rate(0, 1, 0)
+        new_rate(0, 1, 1)
         cast_wm(1, 0, nc.scalar.copy, 0, PACK)
+        cast_wm(1, 1, nc.vector.tensor_copy, 0, 2)
         quant_wm(1, 0, 0, PACK)
-        cast_wm(1, 1, nc.scalar.copy, 0, 2)
-        cast_wm(1, 1, nc.vector.tensor_copy, 2, PACK)
-        for t in range(PACK):
+        cast_wm(1, 1, nc.scalar.copy, 2, PACK)
+        quant_wm(1, 1, 0, 2)
+        new_rate(0, 1, 2)
+        quant_wm(1, 1, 2, PACK)
+        new_rate(0, 1, 3)
+        for t in range(2):
             old_rate(1, 0, t, 4 + t)
         for t in range(PACK):
             open_phase(1, 0, t, t)
-        quant_wm(1, 1, 0, 2)
-        quant_wm(1, 1, 2, PACK)
-        cast_wn(0)
+        cast_wn(0, nc.scalar.copy, 0, 3)
         weave(0, 0, nc.vector.tensor_copy, 0, NT)
         for t in range(PACK):
             kick(1, 0, t)
+        for t in range(2, PACK):
+            old_rate(1, 0, t, 4 + t)
+        cast_wn(0, nc.vector.tensor_copy, 3, 4)
         quant_h(0, 0)
         quant_wn(0)
+        interleave_on_gpsimd(wn_bf[1], wn_raw[1], 0, N)
         for t in range(PACK):
             new_rate(1, 0, t)
         for t in range(PACK):
             open_phase(1, 1, t, t)
             kick(1, 1, t)
-        cast_wn(1)
-        weave(1, 0, nc.vector.tensor_copy, 0, NT)
+        interleave_on_gpsimd(woven[1][0], planes[1][0], 0, SPLIT)
+        weave(1, 0, nc.scalar.copy, SPLIT, NT)
+        weave(0, 1, nc.scalar.copy, 0, NT)
+        for t in range(PACK):
+            old_rate(1, 1, t, t)
+            new_rate(1, 1, t)
         for c in range(4):
-            old_rate(1, 1, c, c)
             open_angle(0, c, 4 + c)
-            add_h(0, 0, c)
-        new_rate(1, 1, 0)
-        quant_h(1, 0)
-        new_rate(1, 1, 1)
-        new_rate(1, 1, 2)
-        quant_wn(1)
-        new_rate(1, 1, 3)
-        weave(0, 1, nc.scalar.copy, 0, NT // 2)
         for c in range(4):
-            add_h(1, 0, c)
-            finish(0, c, False)
-        weave(0, 1, nc.vector.tensor_copy, NT // 2, NT)
+            add_h(0, 0, c)
+        quant_wn(1)
+        quant_h(1, 0)
         weave(1, 1, nc.vector.tensor_copy, 0, NT)
         quant_h(0, 1)
         quant_h(1, 1)
+        open_angle(1, 0, 0)
         for c in range(4):
-            open_angle(1, c, c)
-        for c in range(4):
+            add_h(1, 0, c)
+            finish(0, c, False)
+        open_angle(1, 1, 1)
+        for c in range(2):
             add_h(0, 1, c)
-        for c in range(4):
+        for c in range(2):
             add_h(1, 1, c)
-            finish(1, c, c % 2 == 0)
+            finish(1, c, True)
+        for c in range(2, 4):
+            open_angle(1, c, c)
+            add_h(0, 1, c)
+            add_h(1, 1, c)
+            finish(1, c, True)

@@ -48,9 +48,9 @@ def tile_list_attitude_propagation_kernel(
         for name, size in (
             ("tab_s", 4 * KB), ("planes", 2 * KB), ("tab1", 16 * KB), ("first_end", 0),
             ("tab2_s", 4 * KB), ("v2_plane", KB), ("wa_s", KB),
-            ("tab2", 8 * KB), ("wr", 4 * KB), ("gain", 64), ("wm10", 8 * KB), ("wm11", 8 * KB),
+            ("tab2", 8 * KB), ("wr", 4 * KB), ("wm10", 8 * KB), ("wm11", 8 * KB),
             ("wn0", 8 * KB), ("wa", 2 * KB), ("wn1", 8 * KB), ("drift", 64), ("late_end", 0),
-            ("wm00", 8 * KB), ("wm01", 8 * KB), ("early", 64), ("wr_s", KB), ("tab0", 16 * KB), ("early_end", 0),
+            ("wm00", 8 * KB), ("wm01", 8 * KB), ("early", 64), ("tab0", 16 * KB), ("early_end", 0),
             ("sine0", 8 * KB), ("sine1", 8 * KB), ("wm_bf10", 4 * KB), ("wn_bf", 4 * KB), ("h_bf01", 4 * KB), ("h_bf1", 4 * KB),
         ):
             at[name] = end
@@ -69,13 +69,15 @@ def tile_list_attitude_propagation_kernel(
         early = placed([P, (at["early_end"] - at["early"]) // 4], F32, "early", at["early"])
         wa_w = placed([P, 2, 2 * N], U8, "wa_w", at["wa"])
         wa_s = placed([P, 2, N], U8, "wa_s", at["wa_s"])
-        gain_sb = placed([P, 2, PACK], F32, "gain_sb", at["gain"])
+        gain_sb = held([P, 2, PACK], F32, "gain_sb")
         drift_sb = placed([P, N // P], F32, "drift_sb", at["drift"])
         v_plane = [placed([P, S], U8, "v_plane%d" % a, at["planes"] + KB * a) for a in range(2)]
         v2_plane = placed([P, S], U8, "v2_plane", at["v2_plane"])
         zero_in = placed([P, 1], F32, "zero_in", at["h_bf01"])
         zero = placed([P, 1], F32, "zero", at["wm_bf10"])
 
+        wr_s_raw = held([P, H], U8, "wr_s_raw")
+        nc.gpsimd.memset(wr_s_raw[:].bitcast(I32), 0)
         nc.vector.memset(first[:, 0:T].bitcast(I32), 0)
         nc.vector.memset(second[:, 0:T].bitcast(I32), 0)
         nc.vector.memset(early[:, 0:1], 0.0)
@@ -94,32 +96,31 @@ def tile_list_attitude_propagation_kernel(
             nc.sync.dma_start(tab_w[a][:, lo:hi], words[:, lo:hi])
 
         def load_wr_scales(q):
-            nc.sync.dma_start(
+            nc.gpsimd.dma_start(
                 wr_s_raw[32 * q : 32 * q + 4, :].bitcast(I32), wr_scales[0, 4 * q : 4 * q + 4, :].bitcast(I32))
 
-        nc.sync.dma_start(idx[:], offs)
-        nc.sync.dma_start(idx2[:], offs2)
         load_wm(0, 0)
         load_wm(0, 1)
+        nc.sync.dma_start(idx[:], offs)
+        nc.sync.dma_start(idx2[:], offs2)
         nc.scalar.dma_start(
             tab_s[0:P:4, :].bitcast(I32), tab_scales.rearrange("a q t -> (a q) t").bitcast(I32))
         nc.scalar.dma_start(tab2_s[0:P:8, :].bitcast(I32), tab2_scales[0].bitcast(I32))
         nc.scalar.activation(zero[:], zero_in[:], ACT.Sin)
         load_tab(0)
-        wr_s_raw = placed([P, H], U8, "wr_s_raw", at["wr_s"])
-        nc.vector.memset(wr_s_raw[:].bitcast(I32), 0)
         for q in range(4):
             load_wr_scales(q)
+        nc.gpsimd.dma_start(gain_sb[:], gain.rearrange("(b p t) -> p b t", b=2, t=PACK))
 
         v_s = held([P, S], U8, "v_s")
         v2_s = held([P, S], U8, "v2_s")
         nc.vector.tensor_copy(v_s[:], tab_s.indirect(idx[:]))
         nc.vector.tensor_copy(v2_s[:], tab2_s.indirect(idx2[:]))
 
-        def move_rows(plane, gathered, start, step_r, step_q):
+        def move_rows(queue, plane, gathered, start, step_r, step_q):
             for r in range(4):
                 lo = start + step_r * r
-                nc.sync.dma_start(
+                queue.dma_start(
                     plane[r:P:32, :].bitcast(I32), gathered[lo : lo + 3 * step_q + 1 : step_q, :].bitcast(I32))
 
         wm_bf = [[held([P, KP * PACK], BF16, "wm_bf0%d" % a) for a in range(2)],
@@ -133,14 +134,12 @@ def tile_list_attitude_propagation_kernel(
 
         cast_wm(0, 0, nc.scalar.copy, 0, PACK)
 
-        load_tab(1, 0, T // 2)
-        move_rows(v_plane[0], v_s, 0, 4, 16)
-        load_tab(1, T // 2, T)
-        move_rows(v_plane[1], v_s, 64, 4, 16)
+        move_rows(nc.sync, v_plane[0], v_s, 0, 4, 16)
+        load_tab(1)
+        move_rows(nc.sync, v_plane[1], v_s, 64, 4, 16)
         nc.sync.dma_start(wr_raw[:], wr_words[0].rearrange("p c i -> p (c i)").bitcast(I32))
         nc.sync.dma_start(tab2_w[:], tab2_words[0].bitcast(I32))
-        move_rows(v2_plane, v2_s, 0, 8, 32)
-        nc.sync.dma_start(gain_sb[:], gain.rearrange("(b p t) -> p b t", b=2, t=PACK))
+        move_rows(nc.gpsimd, v2_plane, v2_s, 0, 8, 32)
         load_wm(1, 0)
         load_wm(1, 1)
         load_wn(0)
@@ -164,7 +163,7 @@ def tile_list_attitude_propagation_kernel(
         wn_c = [held([P, N], U32, "wn_c0"), placed([P, N], U32, "wn_c1", at["sine1"] + 6 * KB)]
         wn_s = [held([P, N], U8, "wn_s%d" % b) for b in range(2)]
         wr_c = held([P, H], I32, "wr_c")
-        wr_s = held([P, H], U8, "wr_s")
+        wr_s = placed([P, H], U8, "wr_s", at["tab2_s"])
         h_c = [[held([P, NT], U32, "h_c%d%d" % (b, j)) for j in range(2)] for b in range(2)]
         h_s = [[held([P, NT], U8, "h_s%d%d" % (b, j)) for j in range(2)] for b in range(2)]
         planes = [[held([P, PACK, NT], BF16, "h_planes%d%d" % (b, j)) for j in range(2)] for b in range(2)]

@@ -21,7 +21,9 @@ PACK = 4
 KP = P * PACK
 NT = 512
 KB = 1024
-SPLIT = 416
+SPLIT = 304
+TURNING = (0, 1, 6, 7)
+WAITING = (4, 5, 2, 3)
 
 
 def tile_list_attitude_propagation_kernel(
@@ -291,6 +293,8 @@ def tile_list_attitude_propagation_kernel(
             new_rate(0, 0, t)
         for t in range(PACK):
             old_rate(0, 1, t, 4 + t)
+        for t in range(2, PACK):
+            old_rate(1, 0, t, t)
         new_rate(0, 1, 0)
         new_rate(0, 1, 1)
         cast_wm(1, 0, nc.scalar.copy, 0, PACK)
@@ -303,14 +307,14 @@ def tile_list_attitude_propagation_kernel(
         new_rate(0, 1, 3)
         for t in range(2):
             old_rate(1, 0, t, 4 + t)
-        for t in range(PACK):
-            open_phase(1, 0, t, t)
+        for t in range(PACK - 1):
+            open_phase(1, 0, t, TURNING[t])
         cast_wn(0, nc.scalar.copy, 0, 3)
         weave(0, 0, nc.vector.tensor_copy, 0, NT)
-        for t in range(PACK):
+        for t in range(PACK - 1):
             kick(1, 0, t)
-        for t in range(2, PACK):
-            old_rate(1, 0, t, 4 + t)
+        open_phase(1, 0, PACK - 1, TURNING[PACK - 1])
+        kick(1, 0, PACK - 1)
         cast_wn(0, nc.vector.tensor_copy, 3, 4)
         quant_h(0, 0)
         quant_wn(0)
@@ -318,16 +322,16 @@ def tile_list_attitude_propagation_kernel(
         for t in range(PACK):
             new_rate(1, 0, t)
         for t in range(PACK):
-            open_phase(1, 1, t, t)
+            open_phase(1, 1, t, TURNING[t])
             kick(1, 1, t)
         interleave_on_gpsimd(woven[1][0], planes[1][0], 0, SPLIT)
         weave(1, 0, nc.scalar.copy, SPLIT, NT)
         weave(0, 1, nc.scalar.copy, 0, NT)
         for t in range(PACK):
-            old_rate(1, 1, t, t)
+            old_rate(1, 1, t, TURNING[t])
             new_rate(1, 1, t)
         for c in range(4):
-            open_angle(0, c, 4 + c)
+            open_angle(0, c, WAITING[c])
         for c in range(4):
             add_h(0, 0, c)
         quant_wn(1)
@@ -346,7 +350,7 @@ def tile_list_attitude_propagation_kernel(
             add_h(1, 1, c)
             finish(1, c, True)
         for c in range(2, 4):
-            open_angle(1, c, c)
+            open_angle(1, c, TURNING[c])
             add_h(0, 1, c)
             add_h(1, 1, c)
             finish(1, c, True)

@@ -52,7 +52,7 @@ def tile_list_attitude_propagation_kernel(
             ("tab2_s", 4 * KB), ("v2_plane", KB), ("wa_s", KB),
             ("tab2", 8 * KB), ("wr", 4 * KB), ("wm10", 8 * KB), ("wm11", 8 * KB),
             ("wn0", 8 * KB), ("wa", 2 * KB), ("wn1", 8 * KB), ("drift", 64), ("late_end", 0),
-            ("wm00", 8 * KB), ("wm01", 8 * KB), ("early", 64), ("tab0", 16 * KB), ("early_end", 0),
+            ("wm00", 8 * KB), ("wm01", 8 * KB), ("tab0", 16 * KB),
             ("sine0", 8 * KB), ("sine1", 8 * KB), ("wm_bf10", 4 * KB), ("wn_bf", 4 * KB), ("h_bf01", 4 * KB), ("h_bf1", 4 * KB),
         ):
             at[name] = end
@@ -68,7 +68,6 @@ def tile_list_attitude_propagation_kernel(
         tab2_w = placed([P, T // 2], I32, "tab2_w", at["tab2"])
         wn_raw = [placed([P, PACK, N], F32, "wn_raw%d" % b, at["wn%d" % b]) for b in range(2)]
         wr_raw = placed([P, H], I32, "wr_raw", at["wr"])
-        early = placed([P, (at["early_end"] - at["early"]) // 4], F32, "early", at["early"])
         wa_w = placed([P, 2, 2 * N], U8, "wa_w", at["wa"])
         wa_s = placed([P, 2, N], U8, "wa_s", at["wa_s"])
         gain_sb = held([P, 2, PACK], F32, "gain_sb")
@@ -82,8 +81,7 @@ def tile_list_attitude_propagation_kernel(
         nc.gpsimd.memset(wr_s_raw[:].bitcast(I32), 0)
         nc.vector.memset(first[:, 0:T].bitcast(I32), 0)
         nc.vector.memset(second[:, 0:T].bitcast(I32), 0)
-        nc.vector.memset(early[:, 0:1], 0.0)
-        nc.vector.tensor_copy(zero_in[:], early[:, 0:1])
+        nc.vector.memset(zero_in[:], 0.0)
 
         def load_wm(b, a):
             rows = wm[KP * a : KP * (a + 1), KP * b : KP * (b + 1)]
@@ -101,10 +99,10 @@ def tile_list_attitude_propagation_kernel(
             nc.gpsimd.dma_start(
                 wr_s_raw[32 * q : 32 * q + 4, :].bitcast(I32), wr_scales[0, 4 * q : 4 * q + 4, :].bitcast(I32))
 
-        load_wm(0, 0)
-        load_wm(0, 1)
         nc.sync.dma_start(idx[:], offs)
+        load_wm(0, 0)
         nc.sync.dma_start(idx2[:], offs2)
+        load_wm(0, 1)
         nc.scalar.dma_start(
             tab_s[0:P:4, :].bitcast(I32), tab_scales.rearrange("a q t -> (a q) t").bitcast(I32))
         nc.scalar.dma_start(tab2_s[0:P:8, :].bitcast(I32), tab2_scales[0].bitcast(I32))
@@ -258,6 +256,28 @@ def tile_list_attitude_propagation_kernel(
                 acc[j, c][:], lhsT=wn_c[b][:, cols].bitcast(FP8X4), lhsT_scale=wn_s[b][:, cols],
                 rhs=h_c[b][j][:].bitcast(FP8X4), rhs_scale=h_s[b][j][:], start=False, stop=(b == 1))
 
+        def close_in_halves(j, c, banks):
+            cols = slice(P * c, P * (c + 1))
+            for side, n in enumerate(banks):
+                total = bank(n, "angle")
+                for g in range(2):
+                    lo = P * (2 * side + g)
+                    part = total[:, P * g : P * (g + 1)]
+                    for a in range(2):
+                        nc.tensor.matmul_mx(
+                            part, lhsT=wa_w[:, a, 2 * P * c : 2 * P * (c + 1)].bitcast(FP4X4),
+                            lhsT_scale=wa_s[:, a, cols], rhs=v_words(a, j)[:, lo : lo + P],
+                            rhs_scale=v_plane[a][:, NT * j + lo : NT * j + lo + P], start=(a == 0), stop=False)
+                    for b in range(2):
+                        nc.tensor.matmul_mx(
+                            part, lhsT=wn_c[b][:, cols].bitcast(FP8X4), lhsT_scale=wn_s[b][:, cols],
+                            rhs=h_c[b][j][:, lo : lo + P].bitcast(FP8X4), rhs_scale=h_s[b][j][:, lo : lo + P],
+                            start=False, stop=(b == 1))
+                res = placed([P, 2 * P], F32, "res_half%d" % side, at["tab0"] + 2 * KB * (4 * j + c) + KB * side)
+                nc.vector.tensor_scalar(res[:], total[:, 0 : 2 * P], drift_sb[:, c : c + 1], None, ALU.add)
+                lo = NT * j + 2 * P * side
+                nc.sync.dma_start(out[cols, lo : lo + 2 * P], res[:])
+
         def finish(j, c, on_vector):
             res = placed([P, NT], F32, "res%d%d" % (j, c), at["tab0"] + 2 * KB * (4 * j + c))
             if on_vector:
@@ -349,8 +369,8 @@ def tile_list_attitude_propagation_kernel(
         for c in range(2):
             add_h(1, 1, c)
             finish(1, c, True)
-        for c in range(2, 4):
-            open_angle(1, c, TURNING[c])
-            add_h(0, 1, c)
-            add_h(1, 1, c)
-            finish(1, c, True)
+        open_angle(1, 2, TURNING[2])
+        add_h(0, 1, 2)
+        add_h(1, 1, 2)
+        finish(1, 2, True)
+        close_in_halves(1, 3, (TURNING[3], WAITING[0]))

@@ -163,7 +163,8 @@ def tile_list_attitude_propagation_kernel(
         wn_c = [held([P, N], U32, "wn_c0"), placed([P, N], U32, "wn_c1", at["sine1"] + 6 * KB)]
         wn_s = [held([P, N], U8, "wn_s%d" % b) for b in range(2)]
         wr_c = held([P, H], I32, "wr_c")
-        wr_s = placed([P, H], U8, "wr_s", at["tab2_s"])
+        wr_s = placed([P, KP + 2 * P], U8, "wr_s", at["tab2_s"])
+        wr_s_late = placed([P, 2 * P], U8, "wr_s_late", at["sine1"] + 2 * KB)
         h_c = [[held([P, NT], U32, "h_c%d%d" % (b, j)) for j in range(2)] for b in range(2)]
         h_s = [[held([P, NT], U8, "h_s%d%d" % (b, j)) for j in range(2)] for b in range(2)]
         planes = [[held([P, PACK, NT], BF16, "h_planes%d%d" % (b, j)) for j in range(2)] for b in range(2)]
@@ -183,6 +184,11 @@ def tile_list_attitude_propagation_kernel(
 
         def quant_wn(b):
             nc.vector.quantize_mx(wn_c[b][:].bitcast(FP8X4), wn_s[b][:], wn_bf[b][:])
+
+        def order_wr_scales(dst, b, lo, hi):
+            nc.vector.tensor_copy(
+                dst.rearrange("p (t m) -> p t m", m=P),
+                wr_s_raw[:, KP * b : KP * (b + 1)].rearrange("p (m t) -> p t m", t=PACK)[:, lo:hi, :])
 
         def gather_v2(j):
             nc.vector.tensor_copy(
@@ -220,7 +226,8 @@ def tile_list_attitude_propagation_kernel(
             rates[b, j, t] = bank(n, "rate")
             nc.tensor.matmul_mx(
                 rates[b, j, t][:], lhsT=wr_c[:, KP * b + P * t : KP * b + P * (t + 1)].bitcast(FP8X4),
-                lhsT_scale=wr_s[:, KP * b + P * t : KP * b + P * (t + 1)],
+                lhsT_scale=(wr_s_late[:, P * (t - 2) : P * (t - 1)] if b == 1 and t >= 2
+                            else wr_s[:, KP * b + P * t : KP * b + P * (t + 1)]),
                 rhs=v2_w[j][:].bitcast(FP4X4), rhs_scale=v2_plane[:, NT * j : NT * (j + 1)], start=True, stop=True)
 
         def new_rate(b, j, t):
@@ -289,9 +296,8 @@ def tile_list_attitude_propagation_kernel(
         quant_wm(0, 0, 0, PACK)
         cast_wm(0, 1, nc.scalar.copy, 0, PACK)
         quant_wm(0, 1, 0, PACK)
-        nc.vector.tensor_copy(
-            wr_s[:].rearrange("p (b t m) -> p b t m", b=2, t=PACK),
-            wr_s_raw[:].rearrange("p (b m t) -> p b t m", b=2, t=PACK))
+        order_wr_scales(wr_s[:, 0:KP], 0, 0, PACK)
+        order_wr_scales(wr_s[:, KP : KP + 2 * P], 1, 0, 2)
         nc.vector.tensor_copy(v_w0[:], tab_w[0][:].bitcast(U32).indirect(idx[:]))
         for j in range(2):
             nc.vector.tensor_copy(
@@ -313,10 +319,9 @@ def tile_list_attitude_propagation_kernel(
             new_rate(0, 0, t)
         for t in range(PACK):
             old_rate(0, 1, t, 4 + t)
-        for t in range(2, PACK):
-            old_rate(1, 0, t, t)
         new_rate(0, 1, 0)
         new_rate(0, 1, 1)
+        order_wr_scales(wr_s_late[:], 1, 2, PACK)
         cast_wm(1, 0, nc.scalar.copy, 0, PACK)
         cast_wm(1, 1, nc.vector.tensor_copy, 0, 2)
         quant_wm(1, 0, 0, PACK)
@@ -325,8 +330,8 @@ def tile_list_attitude_propagation_kernel(
         new_rate(0, 1, 2)
         quant_wm(1, 1, 2, PACK)
         new_rate(0, 1, 3)
-        for t in range(2):
-            old_rate(1, 0, t, 4 + t)
+        for t in range(PACK):
+            old_rate(1, 0, t, WAITING[t])
         for t in range(PACK - 1):
             open_phase(1, 0, t, TURNING[t])
         cast_wn(0, nc.scalar.copy, 0, 3)

@@ -21,9 +21,8 @@ PACK = 4
 KP = P * PACK
 NT = 512
 KB = 1024
-SPLIT = 304
-TURNING = (0, 1, 6, 7)
-WAITING = (4, 5, 2, 3)
+WN1_GPSIMD = 256
+H_GPSIMD = 384
 
 
 def tile_list_attitude_propagation_kernel(
@@ -48,40 +47,47 @@ def tile_list_attitude_propagation_kernel(
         at = {}
         end = 0
         for name, size in (
-            ("tab_s", 4 * KB), ("planes", 2 * KB), ("tab1", 16 * KB), ("first_end", 0),
-            ("tab2_s", 4 * KB), ("v2_plane", KB), ("wa_s", KB),
-            ("tab2", 8 * KB), ("wr", 4 * KB), ("wm10", 8 * KB), ("wm11", 8 * KB),
-            ("wn0", 8 * KB), ("wa", 2 * KB), ("wn1", 8 * KB), ("drift", 64), ("late_end", 0),
-            ("wm00", 8 * KB), ("wm01", 8 * KB), ("tab0", 16 * KB),
-            ("sine0", 8 * KB), ("sine1", 8 * KB), ("wm_bf10", 4 * KB), ("wn_bf", 4 * KB), ("h_bf01", 4 * KB), ("h_bf1", 4 * KB),
+            ("tab_s", 4 * KB), ("tab1", 16 * KB), ("first_end", 0), ("wr_s", KB), ("wr", 4 * KB), ("tab2", 8 * KB), ("wa", 2 * KB),
+            ("wm10", 8 * KB), ("wm11", 8 * KB), ("wn0", 8 * KB), ("wn1", 8 * KB), ("gain", 64), ("drift", 64),
+            ("wm_c01", 2 * KB), ("v_w0", 4 * KB), ("late_end", 0),
+            ("tab2_s", 4 * KB), ("wm01", 8 * KB), ("tab0", 16 * KB), ("sine0", 8 * KB), ("sine1", 8 * KB),
+            ("ring_a", 3 * KB), ("wm_bf10", 3 * KB), ("ring_c", 4 * KB), ("ring_b", 4 * KB),
         ):
             at[name] = end
             end = end + size
 
         first = placed([P, at["first_end"]], U8, "first", 0)
-        second = placed([P, at["late_end"] - at["tab2_s"]], U8, "second", at["tab2_s"])
-        tab2_s = second[:, 0:T]
         tab_s = first[:, 0:T]
-        wm_raw = [[placed([P, PACK, KP], F32, "wm_raw%d%d" % (b, a), at["wm%d%d" % (b, a)]) for a in range(2)]
-                  for b in range(2)]
+        tab2_s = placed([P, T], U8, "tab2_s", at["tab2_s"])
+        head = placed([P, at["late_end"] - at["wr_s"]], U8, "head", at["wr_s"])
+        wr_s_raw = head[:, 0:H]
+        zero_in = held([P, 1], F32, "zero_in")
+        zero_src = placed([P, 32], F32, "zero_src", at["tab0"] - 64)
+        zero = placed([P, (at["ring_b"] - at["wm_bf10"]) // 4 + 16], F32, "zero", at["wm_bf10"])[:, 0:1]
+        nc.vector.memset(tab_s.bitcast(I32), 0)
+        nc.vector.memset(tab2_s[:].bitcast(I32), 0)
+        nc.vector.memset(wr_s_raw.bitcast(I32), 0)
+        nc.vector.memset(zero_src[:, 0:1], 0.0)
+        nc.vector.tensor_copy(zero_in[:], zero_src[:, 0:1])
+        zero_late = held([P, 1], F32, "zero_late")
+        nc.vector.memset(zero_late[:], 0.0)
+
+        wm_raw = [[held([P, PACK, KP], F32, "wm_raw00"), placed([P, PACK, KP], F32, "wm_raw01", at["wm01"])],
+                  [placed([P, PACK, KP], F32, "wm_raw1%d" % a, at["wm1%d" % a]) for a in range(2)]]
         tab_w = [placed([P, T], I32, "tab_w%d" % a, at["tab%d" % a]) for a in range(2)]
         tab2_w = placed([P, T // 2], I32, "tab2_w", at["tab2"])
         wn_raw = [placed([P, PACK, N], F32, "wn_raw%d" % b, at["wn%d" % b]) for b in range(2)]
         wr_raw = placed([P, H], I32, "wr_raw", at["wr"])
         wa_w = placed([P, 2, 2 * N], U8, "wa_w", at["wa"])
-        wa_s = placed([P, 2, N], U8, "wa_s", at["wa_s"])
-        gain_sb = held([P, 2, PACK], F32, "gain_sb")
+        gain_sb = placed([P, 2, PACK], F32, "gain_sb", at["gain"])
         drift_sb = placed([P, N // P], F32, "drift_sb", at["drift"])
-        v_plane = [placed([P, S], U8, "v_plane%d" % a, at["planes"] + KB * a) for a in range(2)]
-        v2_plane = placed([P, S], U8, "v2_plane", at["v2_plane"])
-        zero_in = placed([P, 1], F32, "zero_in", at["h_bf01"])
-        zero = placed([P, 1], F32, "zero", at["wm_bf10"])
-
-        wr_s_raw = held([P, H], U8, "wr_s_raw")
-        nc.gpsimd.memset(wr_s_raw[:].bitcast(I32), 0)
-        nc.vector.memset(first[:, 0:T].bitcast(I32), 0)
-        nc.vector.memset(second[:, 0:T].bitcast(I32), 0)
-        nc.vector.memset(zero_in[:], 0.0)
+        stage = held([P, 2 * S + 2 * N + H], U8, "stage")
+        plane_a = held([P, S], U8, "plane_a")
+        plane_b = held([P, 2 * S + 2 * N + H], U8, "plane_b")
+        v_plane = [plane_a[:], plane_b[:, 0:S]]
+        v2_plane = plane_b[:, S : 2 * S]
+        wa_s = [plane_b[:, 2 * S + N * a : 2 * S + N * (a + 1)] for a in range(2)]
+        wr_s = plane_b[:, 2 * S + 2 * N :]
 
         def load_wm(b, a):
             rows = wm[KP * a : KP * (a + 1), KP * b : KP * (b + 1)]
@@ -91,108 +97,103 @@ def tile_list_attitude_propagation_kernel(
             rows = wn[KP * b : KP * (b + 1), :]
             nc.sync.dma_start(wn_raw[b][:], rows.rearrange("(p t) n -> p t n", t=PACK))
 
-        def load_tab(a, lo=0, hi=T):
-            words = tab_words[a].rearrange("p t i -> p (t i)").bitcast(I32)
-            nc.sync.dma_start(tab_w[a][:, lo:hi], words[:, lo:hi])
-
-        def load_wr_scales(q):
-            nc.gpsimd.dma_start(
-                wr_s_raw[32 * q : 32 * q + 4, :].bitcast(I32), wr_scales[0, 4 * q : 4 * q + 4, :].bitcast(I32))
+        def load_tab(a):
+            nc.sync.dma_start(tab_w[a][:], tab_words[a].rearrange("p t i -> p (t i)").bitcast(I32))
 
         nc.sync.dma_start(idx[:], offs)
-        load_wm(0, 0)
         nc.sync.dma_start(idx2[:], offs2)
+        nc.sync.dma_start(
+            stage[64:P:4, 2 * S : 2 * S + 2 * N].bitcast(I32).rearrange("q (a n) -> q a n", a=2),
+            wa_scales.bitcast(I32).rearrange("a q n -> q a n"))
+        load_wm(0, 0)
+        nc.sync.dma_start(
+            first[0:P:4, 0:T].bitcast(I32), tab_scales.rearrange("a q t -> (a q) t").bitcast(I32))
+        nc.sync.dma_start(tab2_s[64:P:4, :].bitcast(I32), tab2_scales[0].bitcast(I32))
+        nc.sync.dma_start(head[64:P:4, 0:H].bitcast(I32), wr_scales[0].bitcast(I32))
+        nc.scalar.activation(zero, zero_in[:], ACT.Sin)
         load_wm(0, 1)
-        nc.scalar.dma_start(
-            tab_s[0:P:4, :].bitcast(I32), tab_scales.rearrange("a q t -> (a q) t").bitcast(I32))
-        nc.scalar.dma_start(tab2_s[0:P:8, :].bitcast(I32), tab2_scales[0].bitcast(I32))
-        nc.scalar.activation(zero[:], zero_in[:], ACT.Sin)
         load_tab(0)
-        for q in range(4):
-            load_wr_scales(q)
-        nc.gpsimd.dma_start(gain_sb[:], gain.rearrange("(b p t) -> p b t", b=2, t=PACK))
 
         v_s = held([P, S], U8, "v_s")
         v2_s = held([P, S], U8, "v2_s")
         nc.vector.tensor_copy(v_s[:], tab_s.indirect(idx[:]))
-        nc.vector.tensor_copy(v2_s[:], tab2_s.indirect(idx2[:]))
+        nc.vector.tensor_copy(v2_s[:], tab2_s[:].indirect(idx2[:]))
+        nc.vector.tensor_copy(stage[:, 0:S].bitcast(I32), v_s[:].bitcast(I32))
+        nc.vector.tensor_copy(stage[:, S : 2 * S].bitcast(I32), v2_s[:].bitcast(I32))
+        nc.vector.tensor_copy(
+            stage[:, 2 * S + 2 * N :].rearrange("p (b t m) -> p b t m", b=2, t=PACK),
+            wr_s_raw.rearrange("p (b m t) -> p b t m", b=2, t=PACK))
 
-        def move_rows(queue, plane, gathered, start, step_r, step_q):
+        def move_rows(plane, spread, first_row):
             for r in range(4):
-                lo = start + step_r * r
-                queue.dma_start(
-                    plane[r:P:32, :].bitcast(I32), gathered[lo : lo + 3 * step_q + 1 : step_q, :].bitcast(I32))
+                lo = first_row + 4 * r
+                nc.sync.dma_start(plane[r:P:32, :].bitcast(I32), spread[lo : lo + 49 : 16, :].bitcast(I32))
+
+        move_rows(plane_a, v_s, 0)
+        load_tab(1)
+        move_rows(plane_b, stage, 64)
+        nc.sync.dma_start(gain_sb[:], gain.rearrange("(b p t) -> p b t", b=2, t=PACK))
+        nc.sync.dma_start(wr_raw[:], wr_words[0].rearrange("p c i -> p (c i)").bitcast(I32))
+        nc.sync.dma_start(tab2_w[:], tab2_words[0].bitcast(I32))
+        nc.sync.dma_start(wa_w[:].bitcast(I32), wa_words.bitcast(I32).rearrange("a p c -> p a c"))
+        load_wm(1, 0)
+        load_wm(1, 1)
+        load_wn(0)
+        load_wn(1)
+        with nc.allow_non_contiguous_dma(reason="one drift value a partition"):
+            nc.sync.dma_start(drift_sb[:], drift.rearrange("(c p) -> p c", p=P))
+
+        v_w0 = placed([P, S], U32, "v_w0", at["v_w0"])
+        v_w1 = [held([P, NT], U32, "v_w1%d" % j) for j in range(2)]
+        wr_c = placed([P, H], I32, "wr_c", at["tab1"])
+        v2_w = [placed([P, 2 * NT], U8, "v2_w%d" % j, at["tab1"] + 4 * KB + KB * j) for j in range(2)]
+        half = NT // 16
 
         wm_bf = [[held([P, KP * PACK], BF16, "wm_bf0%d" % a) for a in range(2)],
                  [placed([P, KP * PACK], BF16, "wm_bf10", at["wm_bf10"]),
-                  placed([P, KP * PACK], BF16, "wm_bf11", at["sine0"] + 2 * KB)]]
+                  placed([P, KP * PACK], BF16, "wm_bf11", at["ring_b"])]]
+        wm_c = [[placed([P, KP], U32, "wm_c00", at["tab2_s"]), placed([P, KP], U32, "wm_c01", at["wm_c01"])],
+                [held([P, KP], U32, "wm_c1%d" % a) for a in range(2)]]
+        wm_s = [[held([P, KP], U8, "wm_s%d%d" % (b, a)) for a in range(2)] for b in range(2)]
+        wn_bf = [placed([P, N * PACK], BF16, "wn_bf0", at["ring_b"]),
+                 placed([P, N * PACK], BF16, "wn_bf1", at["ring_c"])]
+        wn_c = [held([P, N], U32, "wn_c%d" % b) for b in range(2)]
+        wn_s = [placed([P, N], U8, "wn_s%d" % b, at["sine0"] + 6 * KB + N * b) for b in range(2)]
+        h_c = [[held([P, NT], U32, "h_c%d%d" % (b, j)) for j in range(2)] for b in range(2)]
+        h_s = [[held([P, NT], U8, "h_s%d%d" % (b, j)) for j in range(2)] for b in range(2)]
+        planes = [[held([P, PACK, NT], BF16, "h_planes00"), placed([P, PACK, NT], BF16, "h_planes01", at["ring_a"])],
+                  [held([P, PACK, NT], BF16, "h_planes1%d" % j) for j in range(2)]]
+        woven = [[placed([P, NT * PACK], BF16, "h_bf00", at["ring_c"]), placed([P, NT * PACK], BF16, "h_bf01", at["ring_b"])],
+                 [placed([P, NT * PACK], BF16, "h_bf1%d" % j, at["ring_c"]) for j in range(2)]]
+
+        def copy_on_gpsimd(dst, src):
+            nc.gpsimd.tensor_scalar(dst, src, 1.0, 0.0, ALU.mult, ALU.add)
 
         def cast_wm(b, a, copy, lo, hi):
             copy(
                 wm_bf[b][a][:].rearrange("p (t m j) -> p m j t", t=PACK, j=PACK)[:, :, :, lo:hi],
                 wm_raw[b][a][:].rearrange("p j (m t) -> p m j t", t=PACK)[:, :, :, lo:hi])
 
-        cast_wm(0, 0, nc.scalar.copy, 0, PACK)
-
-        move_rows(nc.sync, v_plane[0], v_s, 0, 4, 16)
-        load_tab(1)
-        move_rows(nc.sync, v_plane[1], v_s, 64, 4, 16)
-        nc.sync.dma_start(wr_raw[:], wr_words[0].rearrange("p c i -> p (c i)").bitcast(I32))
-        nc.sync.dma_start(tab2_w[:], tab2_words[0].bitcast(I32))
-        move_rows(nc.gpsimd, v2_plane, v2_s, 0, 8, 32)
-        load_wm(1, 0)
-        load_wm(1, 1)
-        load_wn(0)
-        load_wn(1)
-        nc.sync.dma_start(wa_w[:].bitcast(I32), wa_words.bitcast(I32).rearrange("a p c -> p a c"))
-        for q in range(4):
-            nc.sync.dma_start(
-                wa_s[32 * q : 32 * q + 4, :, :].bitcast(I32),
-                wa_scales[:, 4 * q : 4 * q + 4, :].bitcast(I32).rearrange("a r n -> r a n"))
-        with nc.allow_non_contiguous_dma(reason="one drift value a partition"):
-            nc.sync.dma_start(drift_sb[:], drift.rearrange("(c p) -> p c", p=P))
-
-        v_w0 = held([P, S], U32, "v_w0")
-        v_w1 = [held([P, NT], U32, "v_w1%d" % j) for j in range(2)]
-        v2_w = [held([P, 2 * NT], U8, "v2_w%d" % j) for j in range(2)]
-        half = NT // 16
-
-        wm_c = [[held([P, KP], U32, "wm_c%d%d" % (b, a)) for a in range(2)] for b in range(2)]
-        wm_s = [[held([P, KP], U8, "wm_s%d%d" % (b, a)) for a in range(2)] for b in range(2)]
-        wn_bf = [placed([P, N * PACK], BF16, "wn_bf%d" % b, at["wn_bf"]) for b in range(2)]
-        wn_c = [held([P, N], U32, "wn_c0"), placed([P, N], U32, "wn_c1", at["sine1"] + 6 * KB)]
-        wn_s = [held([P, N], U8, "wn_s%d" % b) for b in range(2)]
-        wr_c = held([P, H], I32, "wr_c")
-        wr_s = placed([P, KP + 2 * P], U8, "wr_s", at["tab2_s"])
-        wr_s_late = placed([P, 2 * P], U8, "wr_s_late", at["sine1"] + 2 * KB)
-        h_c = [[held([P, NT], U32, "h_c%d%d" % (b, j)) for j in range(2)] for b in range(2)]
-        h_s = [[held([P, NT], U8, "h_s%d%d" % (b, j)) for j in range(2)] for b in range(2)]
-        planes = [[held([P, PACK, NT], BF16, "h_planes%d%d" % (b, j)) for j in range(2)] for b in range(2)]
-        woven = [[held([P, NT * PACK], BF16, "h_bf00"), placed([P, NT * PACK], BF16, "h_bf01", at["h_bf01"])],
-                 [placed([P, NT * PACK], BF16, "h_bf1%d" % j, at["h_bf1"]) for j in range(2)]]
-
         def quant_wm(b, a, lo, hi):
             nc.vector.quantize_mx(
                 wm_c[b][a][:, P * lo : P * hi].bitcast(FP8X4), wm_s[b][a][:, P * lo : P * hi],
                 wm_bf[b][a][:, KP * lo : KP * hi])
 
-        def cast_wn(b, copy, lo, hi):
-            for c in range(lo, hi):
-                copy(
-                    wn_bf[b][:, PACK * P * c : PACK * P * (c + 1)].rearrange("p (u i t) -> p u t i", i=4, t=PACK),
-                    wn_raw[b][:, :, P * c : P * (c + 1)].rearrange("p t (u i) -> p u t i", i=4))
+        def interleave(copy, dst, src, lo, hi):
+            copy(
+                dst[:, PACK * lo : PACK * hi].rearrange("p (u i t) -> p u t i", i=4, t=PACK),
+                src[:, :, lo:hi].rearrange("p t (u i) -> p u t i", i=4))
+
+        def interleave_on_gpsimd(dst, src, lo, hi):
+            copy_on_gpsimd(
+                dst[:, PACK * lo : PACK * hi].rearrange("p (n t) -> p n t", t=PACK),
+                src[:, :, lo:hi].rearrange("p t n -> p n t"))
 
         def quant_wn(b):
             nc.vector.quantize_mx(wn_c[b][:].bitcast(FP8X4), wn_s[b][:], wn_bf[b][:])
 
-        def order_wr_scales(dst, b, lo, hi):
-            nc.vector.tensor_copy(
-                dst.rearrange("p (t m) -> p t m", m=P),
-                wr_s_raw[:, KP * b : KP * (b + 1)].rearrange("p (m t) -> p t m", t=PACK)[:, lo:hi, :])
-
-        def gather_v2(j):
-            nc.vector.tensor_copy(
-                v2_w[j][:].bitcast(U16), tab2_w[:].bitcast(U16).indirect(idx2[:, half * j : half * (j + 1)]))
+        def quant_h(b, j):
+            nc.vector.quantize_mx(h_c[b][j][:].bitcast(FP8X4), h_s[b][j][:], woven[b][j][:])
 
         def v_words(a, j):
             return (v_w0[:, NT * j : NT * (j + 1)] if a == 0 else v_w1[j][:]).bitcast(FP8X4)
@@ -219,15 +220,14 @@ def tile_list_attitude_propagation_kernel(
         def kick(b, j, t):
             phase_pass(b, j, t, 1)
             sine = placed([P, NT], F32, "sine%d%d%d" % (b, j, t), at["sine%d" % j] + 2 * KB * t)
-            nc.scalar.activation(sine[:], phases[b, j, t][:], ACT.Sin, bias=(zero, zero_in)[b][:], scale=-1.0)
+            nc.scalar.activation(sine[:], phases[b, j, t][:], ACT.Sin, bias=(zero, zero_late[:])[b], scale=-1.0)
             sines[b, j, t] = sine
 
         def old_rate(b, j, t, n):
             rates[b, j, t] = bank(n, "rate")
+            cols = slice(KP * b + P * t, KP * b + P * (t + 1))
             nc.tensor.matmul_mx(
-                rates[b, j, t][:], lhsT=wr_c[:, KP * b + P * t : KP * b + P * (t + 1)].bitcast(FP8X4),
-                lhsT_scale=(wr_s_late[:, P * (t - 2) : P * (t - 1)] if b == 1 and t >= 2
-                            else wr_s[:, KP * b + P * t : KP * b + P * (t + 1)]),
+                rates[b, j, t][:], lhsT=wr_c[:, cols].bitcast(FP8X4), lhsT_scale=wr_s[:, cols],
                 rhs=v2_w[j][:].bitcast(FP4X4), rhs_scale=v2_plane[:, NT * j : NT * (j + 1)], start=True, stop=True)
 
         def new_rate(b, j, t):
@@ -235,25 +235,12 @@ def tile_list_attitude_propagation_kernel(
                 planes[b][j][:, t, :], sines[b, j, t][:], gain_sb[:, b, t : t + 1], rates[b, j, t][:],
                 ALU.mult, ALU.add)
 
-        def weave(b, j, copy, lo, hi):
-            copy(
-                woven[b][j][:, PACK * lo : PACK * hi].rearrange("p (u i t) -> p u t i", i=4, t=PACK),
-                planes[b][j][:, :, lo:hi].rearrange("p t (u i) -> p u t i", i=4))
-
-        def interleave_on_gpsimd(dst, src, lo, hi):
-            nc.gpsimd.tensor_scalar(
-                dst[:, PACK * lo : PACK * hi].rearrange("p (n t) -> p n t", t=PACK),
-                src[:, :, lo:hi].rearrange("p t n -> p n t"), 1.0, 0.0, ALU.mult, ALU.add)
-
-        def quant_h(b, j):
-            nc.vector.quantize_mx(h_c[b][j][:].bitcast(FP8X4), h_s[b][j][:], woven[b][j][:])
-
         def open_angle(j, c, n):
             acc[j, c] = bank(n, "angle")
             for a in range(2):
                 nc.tensor.matmul_mx(
                     acc[j, c][:], lhsT=wa_w[:, a, 2 * P * c : 2 * P * (c + 1)].bitcast(FP4X4),
-                    lhsT_scale=wa_s[:, a, P * c : P * (c + 1)],
+                    lhsT_scale=wa_s[a][:, P * c : P * (c + 1)],
                     rhs=v_words(a, j), rhs_scale=v_plane[a][:, NT * j : NT * (j + 1)],
                     start=(a == 0), stop=False)
 
@@ -263,41 +250,17 @@ def tile_list_attitude_propagation_kernel(
                 acc[j, c][:], lhsT=wn_c[b][:, cols].bitcast(FP8X4), lhsT_scale=wn_s[b][:, cols],
                 rhs=h_c[b][j][:].bitcast(FP8X4), rhs_scale=h_s[b][j][:], start=False, stop=(b == 1))
 
-        def close_in_halves(j, c, banks):
-            cols = slice(P * c, P * (c + 1))
-            for side, n in enumerate(banks):
-                total = bank(n, "angle")
-                for g in range(2):
-                    lo = P * (2 * side + g)
-                    part = total[:, P * g : P * (g + 1)]
-                    for a in range(2):
-                        nc.tensor.matmul_mx(
-                            part, lhsT=wa_w[:, a, 2 * P * c : 2 * P * (c + 1)].bitcast(FP4X4),
-                            lhsT_scale=wa_s[:, a, cols], rhs=v_words(a, j)[:, lo : lo + P],
-                            rhs_scale=v_plane[a][:, NT * j + lo : NT * j + lo + P], start=(a == 0), stop=False)
-                    for b in range(2):
-                        nc.tensor.matmul_mx(
-                            part, lhsT=wn_c[b][:, cols].bitcast(FP8X4), lhsT_scale=wn_s[b][:, cols],
-                            rhs=h_c[b][j][:, lo : lo + P].bitcast(FP8X4), rhs_scale=h_s[b][j][:, lo : lo + P],
-                            start=False, stop=(b == 1))
-                res = placed([P, 2 * P], F32, "res_half%d" % side, at["tab0"] + 2 * KB * (4 * j + c) + KB * side)
-                nc.vector.tensor_scalar(res[:], total[:, 0 : 2 * P], drift_sb[:, c : c + 1], None, ALU.add)
-                lo = NT * j + 2 * P * side
-                nc.sync.dma_start(out[cols, lo : lo + 2 * P], res[:])
-
-        def finish(j, c, on_vector):
+        def finish(j, c):
             res = placed([P, NT], F32, "res%d%d" % (j, c), at["tab0"] + 2 * KB * (4 * j + c))
-            if on_vector:
+            if j == 1 and c % 2 == 0:
                 nc.vector.tensor_scalar(res[:], acc[j, c][:], drift_sb[:, c : c + 1], None, ALU.add)
             else:
                 nc.scalar.activation(res[:], acc[j, c][:], ACT.Identity, bias=drift_sb[:, c : c + 1])
             nc.sync.dma_start(out[P * c : P * (c + 1), NT * j : NT * (j + 1)], res[:])
 
-        quant_wm(0, 0, 0, PACK)
-        cast_wm(0, 1, nc.scalar.copy, 0, PACK)
-        quant_wm(0, 1, 0, PACK)
-        order_wr_scales(wr_s[:, 0:KP], 0, 0, PACK)
-        order_wr_scales(wr_s[:, KP : KP + 2 * P], 1, 0, 2)
+        for a in range(2):
+            cast_wm(0, a, nc.scalar.copy, 0, PACK)
+            quant_wm(0, a, 0, PACK)
         nc.vector.tensor_copy(v_w0[:], tab_w[0][:].bitcast(U32).indirect(idx[:]))
         for j in range(2):
             nc.vector.tensor_copy(
@@ -305,8 +268,9 @@ def tile_list_attitude_propagation_kernel(
         nc.vector.tensor_copy(
             wr_c[:].rearrange("p (b t u i) -> p b u t i", b=2, t=PACK, i=4),
             wr_raw[:].rearrange("p (b u i t) -> p b u t i", b=2, t=PACK, i=4))
-        gather_v2(0)
-        gather_v2(1)
+        for j in range(2):
+            nc.vector.tensor_copy(
+                v2_w[j][:].bitcast(U16), tab2_w[:].bitcast(U16).indirect(idx2[:, half * j : half * (j + 1)]))
 
         for j in range(2):
             for t in range(PACK):
@@ -317,65 +281,56 @@ def tile_list_attitude_propagation_kernel(
         for t in range(PACK):
             old_rate(0, 0, t, t)
             new_rate(0, 0, t)
+        cast_wm(1, 0, nc.scalar.copy, 0, 2)
+        cast_wm(1, 0, nc.vector.tensor_copy, 2, PACK)
+        quant_wm(1, 0, 0, PACK)
         for t in range(PACK):
             old_rate(0, 1, t, 4 + t)
-        new_rate(0, 1, 0)
-        new_rate(0, 1, 1)
-        order_wr_scales(wr_s_late[:], 1, 2, PACK)
-        cast_wm(1, 0, nc.scalar.copy, 0, PACK)
-        cast_wm(1, 1, nc.vector.tensor_copy, 0, 2)
-        quant_wm(1, 0, 0, PACK)
+            new_rate(0, 1, t)
+        for c in range(4):
+            open_angle(0, c, c)
+        interleave_on_gpsimd(woven[0][0], planes[0][0], 0, H_GPSIMD)
+        cast_wm(1, 1, nc.scalar.copy, 0, 2)
         cast_wm(1, 1, nc.scalar.copy, 2, PACK)
+        interleave(nc.scalar.copy, woven[0][0], planes[0][0], H_GPSIMD, NT)
         quant_wm(1, 1, 0, 2)
-        new_rate(0, 1, 2)
         quant_wm(1, 1, 2, PACK)
-        new_rate(0, 1, 3)
         for t in range(PACK):
-            old_rate(1, 0, t, WAITING[t])
-        for t in range(PACK - 1):
-            open_phase(1, 0, t, TURNING[t])
-        cast_wn(0, nc.scalar.copy, 0, 3)
-        weave(0, 0, nc.vector.tensor_copy, 0, NT)
-        for t in range(PACK - 1):
+            open_phase(1, 0, t, 4 + t)
+        for t in range(PACK):
             kick(1, 0, t)
-        open_phase(1, 0, PACK - 1, TURNING[PACK - 1])
-        kick(1, 0, PACK - 1)
-        cast_wn(0, nc.vector.tensor_copy, 3, 4)
+        interleave(nc.vector.tensor_copy, wn_bf[0], wn_raw[0], 0, N)
         quant_h(0, 0)
-        quant_wn(0)
-        interleave_on_gpsimd(wn_bf[1], wn_raw[1], 0, N)
+        interleave_on_gpsimd(wn_bf[1], wn_raw[1], 0, WN1_GPSIMD)
+        interleave(nc.scalar.copy, wn_bf[1], wn_raw[1], WN1_GPSIMD, N)
         for t in range(PACK):
+            old_rate(1, 0, t, 4 + t)
             new_rate(1, 0, t)
         for t in range(PACK):
-            open_phase(1, 1, t, TURNING[t])
+            open_phase(1, 1, t, 4 + t)
             kick(1, 1, t)
-        interleave_on_gpsimd(woven[1][0], planes[1][0], 0, SPLIT)
-        weave(1, 0, nc.scalar.copy, SPLIT, NT)
-        weave(0, 1, nc.scalar.copy, 0, NT)
+        quant_wn(0)
+        quant_wn(1)
+        interleave_on_gpsimd(woven[1][0], planes[1][0], 0, H_GPSIMD)
+        interleave(nc.scalar.copy, woven[1][0], planes[1][0], H_GPSIMD, NT)
+        interleave(nc.scalar.copy, woven[0][1], planes[0][1], 0, NT)
         for t in range(PACK):
-            old_rate(1, 1, t, TURNING[t])
+            old_rate(1, 1, t, 4 + t)
             new_rate(1, 1, t)
         for c in range(4):
-            open_angle(0, c, WAITING[c])
-        for c in range(4):
             add_h(0, 0, c)
-        quant_wn(1)
         quant_h(1, 0)
-        weave(1, 1, nc.vector.tensor_copy, 0, NT)
+        interleave(nc.vector.tensor_copy, woven[1][1], planes[1][1], 0, NT)
         quant_h(0, 1)
         quant_h(1, 1)
-        open_angle(1, 0, 0)
+        for c in range(2):
+            open_angle(1, c, 4 + c)
         for c in range(4):
             add_h(1, 0, c)
-            finish(0, c, False)
-        open_angle(1, 1, 1)
-        for c in range(2):
+            finish(0, c)
+        for c in range(2, 4):
+            open_angle(1, c, 4 + c)
+        for c in range(4):
             add_h(0, 1, c)
-        for c in range(2):
             add_h(1, 1, c)
-            finish(1, c, True)
-        open_angle(1, 2, TURNING[2])
-        add_h(0, 1, 2)
-        add_h(1, 1, 2)
-        finish(1, 2, True)
-        close_in_halves(1, 3, (TURNING[3], WAITING[0]))
+            finish(1, c)

@@ -21,8 +21,7 @@ PACK = 4
 KP = P * PACK
 NT = 512
 KB = 1024
-WN1_GPSIMD = 256
-H_GPSIMD = 384
+H00_SCALAR = 320
 
 
 def tile_list_attitude_propagation_kernel(
@@ -51,7 +50,7 @@ def tile_list_attitude_propagation_kernel(
             ("wm10", 8 * KB), ("wm11", 8 * KB), ("wn0", 8 * KB), ("wn1", 8 * KB), ("gain", 64), ("drift", 64),
             ("wm_c01", 2 * KB), ("v_w0", 4 * KB), ("late_end", 0),
             ("tab2_s", 4 * KB), ("wm01", 8 * KB), ("tab0", 16 * KB), ("sine0", 8 * KB), ("sine1", 8 * KB),
-            ("ring_a", 3 * KB), ("wm_bf10", 3 * KB), ("ring_c", 4 * KB), ("ring_b", 4 * KB),
+            ("ring_a", 3 * KB), ("wm_bf10", 3 * KB), ("ring_c", 4 * KB), ("ring_b", 4 * KB), ("ring_d", 4 * KB),
         ):
             at[name] = end
             end = end + size
@@ -164,10 +163,7 @@ def tile_list_attitude_propagation_kernel(
         planes = [[held([P, PACK, NT], BF16, "h_planes00"), placed([P, PACK, NT], BF16, "h_planes01", at["ring_a"])],
                   [held([P, PACK, NT], BF16, "h_planes1%d" % j) for j in range(2)]]
         woven = [[placed([P, NT * PACK], BF16, "h_bf00", at["ring_c"]), placed([P, NT * PACK], BF16, "h_bf01", at["ring_b"])],
-                 [placed([P, NT * PACK], BF16, "h_bf1%d" % j, at["ring_c"]) for j in range(2)]]
-
-        def copy_on_gpsimd(dst, src):
-            nc.gpsimd.tensor_scalar(dst, src, 1.0, 0.0, ALU.mult, ALU.add)
+                 [placed([P, NT * PACK], BF16, "h_bf1%d" % j, at["ring_d"]) for j in range(2)]]
 
         def cast_wm(b, a, copy, lo, hi):
             copy(
@@ -183,11 +179,6 @@ def tile_list_attitude_propagation_kernel(
             copy(
                 dst[:, PACK * lo : PACK * hi].rearrange("p (u i t) -> p u t i", i=4, t=PACK),
                 src[:, :, lo:hi].rearrange("p t (u i) -> p u t i", i=4))
-
-        def interleave_on_gpsimd(dst, src, lo, hi):
-            copy_on_gpsimd(
-                dst[:, PACK * lo : PACK * hi].rearrange("p (n t) -> p n t", t=PACK),
-                src[:, :, lo:hi].rearrange("p t n -> p n t"))
 
         def quant_wn(b):
             nc.vector.quantize_mx(wn_c[b][:].bitcast(FP8X4), wn_s[b][:], wn_bf[b][:])
@@ -289,20 +280,19 @@ def tile_list_attitude_propagation_kernel(
             new_rate(0, 1, t)
         for c in range(4):
             open_angle(0, c, c)
-        interleave_on_gpsimd(woven[0][0], planes[0][0], 0, H_GPSIMD)
         cast_wm(1, 1, nc.scalar.copy, 0, 2)
         cast_wm(1, 1, nc.scalar.copy, 2, PACK)
-        interleave(nc.scalar.copy, woven[0][0], planes[0][0], H_GPSIMD, NT)
+        interleave(nc.scalar.copy, woven[0][0], planes[0][0], 0, H00_SCALAR)
         quant_wm(1, 1, 0, 2)
         quant_wm(1, 1, 2, PACK)
         for t in range(PACK):
             open_phase(1, 0, t, 4 + t)
         for t in range(PACK):
             kick(1, 0, t)
+        interleave(nc.vector.tensor_copy, woven[0][0], planes[0][0], H00_SCALAR, NT)
         interleave(nc.vector.tensor_copy, wn_bf[0], wn_raw[0], 0, N)
         quant_h(0, 0)
-        interleave_on_gpsimd(wn_bf[1], wn_raw[1], 0, WN1_GPSIMD)
-        interleave(nc.scalar.copy, wn_bf[1], wn_raw[1], WN1_GPSIMD, N)
+        interleave(nc.scalar.copy, wn_bf[1], wn_raw[1], 0, N // 2)
         for t in range(PACK):
             old_rate(1, 0, t, 4 + t)
             new_rate(1, 0, t)
@@ -310,16 +300,16 @@ def tile_list_attitude_propagation_kernel(
             open_phase(1, 1, t, 4 + t)
             kick(1, 1, t)
         quant_wn(0)
-        quant_wn(1)
-        interleave_on_gpsimd(woven[1][0], planes[1][0], 0, H_GPSIMD)
-        interleave(nc.scalar.copy, woven[1][0], planes[1][0], H_GPSIMD, NT)
+        interleave(nc.vector.tensor_copy, woven[1][0], planes[1][0], 0, NT)
+        quant_h(1, 0)
+        interleave(nc.scalar.copy, wn_bf[1], wn_raw[1], N // 2, N)
         interleave(nc.scalar.copy, woven[0][1], planes[0][1], 0, NT)
         for t in range(PACK):
             old_rate(1, 1, t, 4 + t)
             new_rate(1, 1, t)
         for c in range(4):
             add_h(0, 0, c)
-        quant_h(1, 0)
+        quant_wn(1)
         interleave(nc.vector.tensor_copy, woven[1][1], planes[1][1], 0, NT)
         quant_h(0, 1)
         quant_h(1, 1)

@@ -20,8 +20,10 @@ P = 128
 PACK = 4
 KP = P * PACK
 NT = 512
+NH = NT // 2
 KB = 1024
-H00_SCALAR = 320
+RATE_BANKS = (0, 1, 4, 5)
+PHASE_BANKS = (2, 3, 6, 7)
 
 
 def tile_list_attitude_propagation_kernel(
@@ -47,10 +49,10 @@ def tile_list_attitude_propagation_kernel(
         end = 0
         for name, size in (
             ("tab_s", 4 * KB), ("tab1", 16 * KB), ("first_end", 0), ("wr_s", KB), ("wr", 4 * KB), ("tab2", 8 * KB), ("wa", 2 * KB),
-            ("wm10", 8 * KB), ("wm11", 8 * KB), ("wn0", 8 * KB), ("wn1", 8 * KB), ("gain", 64), ("drift", 64),
-            ("wm_c01", 2 * KB), ("v_w0", 4 * KB), ("late_end", 0),
+            ("wm10", 8 * KB), ("wm11", 8 * KB), ("wn0", 8 * KB), ("wn1", 8 * KB), ("drift", 64),
+            ("wm_c01", 2 * KB), ("v_w0", 4 * KB), ("stage_w", S + N), ("late_end", 0),
             ("tab2_s", 4 * KB), ("wm01", 8 * KB), ("tab0", 16 * KB), ("sine0", 8 * KB), ("sine1", 8 * KB),
-            ("ring_a", 3 * KB), ("wm_bf10", 3 * KB), ("ring_c", 4 * KB), ("ring_b", 4 * KB), ("ring_d", 4 * KB),
+            ("wm_bf10", 4 * KB), ("h_bf00", 4 * KB), ("wn_bf0", 4 * KB), ("wn_bf1", 4 * KB), ("h_bf01", 4 * KB),
         ):
             at[name] = end
             end = end + size
@@ -62,14 +64,14 @@ def tile_list_attitude_propagation_kernel(
         wr_s_raw = head[:, 0:H]
         zero_in = held([P, 1], F32, "zero_in")
         zero_src = placed([P, 32], F32, "zero_src", at["tab0"] - 64)
-        zero = placed([P, (at["ring_b"] - at["wm_bf10"]) // 4 + 16], F32, "zero", at["wm_bf10"])[:, 0:1]
+        zero = placed([P, (at["wn_bf0"] - at["wm_bf10"]) // 4 + 16], F32, "zero", at["wm_bf10"])[:, 0:1]
         nc.vector.memset(tab_s.bitcast(I32), 0)
         nc.vector.memset(tab2_s[:].bitcast(I32), 0)
         nc.vector.memset(wr_s_raw.bitcast(I32), 0)
         nc.vector.memset(zero_src[:, 0:1], 0.0)
         nc.vector.tensor_copy(zero_in[:], zero_src[:, 0:1])
-        zero_late = held([P, 1], F32, "zero_late")
-        nc.vector.memset(zero_late[:], 0.0)
+        zero_late = placed([P, 32], F32, "zero_late", at["h_bf01"] - 64)[:, 0:1]
+        nc.vector.memset(zero_late, 0.0)
 
         wm_raw = [[held([P, PACK, KP], F32, "wm_raw00"), placed([P, PACK, KP], F32, "wm_raw01", at["wm01"])],
                   [placed([P, PACK, KP], F32, "wm_raw1%d" % a, at["wm1%d" % a]) for a in range(2)]]
@@ -78,15 +80,15 @@ def tile_list_attitude_propagation_kernel(
         wn_raw = [placed([P, PACK, N], F32, "wn_raw%d" % b, at["wn%d" % b]) for b in range(2)]
         wr_raw = placed([P, H], I32, "wr_raw", at["wr"])
         wa_w = placed([P, 2, 2 * N], U8, "wa_w", at["wa"])
-        gain_sb = placed([P, 2, PACK], F32, "gain_sb", at["gain"])
+        gain_sb = held([P, 2, PACK], F32, "gain_sb")
         drift_sb = placed([P, N // P], F32, "drift_sb", at["drift"])
-        stage = held([P, 2 * S + 2 * N + H], U8, "stage")
-        plane_a = held([P, S], U8, "plane_a")
-        plane_b = held([P, 2 * S + 2 * N + H], U8, "plane_b")
-        v_plane = [plane_a[:], plane_b[:, 0:S]]
-        v2_plane = plane_b[:, S : 2 * S]
-        wa_s = [plane_b[:, 2 * S + N * a : 2 * S + N * (a + 1)] for a in range(2)]
-        wr_s = plane_b[:, 2 * S + 2 * N :]
+        stage_r = held([P, S + H], U8, "stage_r")
+        stage_w = placed([P, S + N], U8, "stage_w", at["stage_w"])
+        plane_m = [held([P, S], U8, "plane_m%d" % a) for a in range(2)]
+        plane_r = held([P, S + H], U8, "plane_r")
+        plane_w = [held([P, S + N], U8, "plane_w%d" % a) for a in range(2)]
+        v2_plane = plane_r[:, 0:S]
+        wr_s = plane_r[:, S:]
 
         def load_wm(b, a):
             rows = wm[KP * a : KP * (a + 1), KP * b : KP * (b + 1)]
@@ -101,9 +103,7 @@ def tile_list_attitude_propagation_kernel(
 
         nc.sync.dma_start(idx[:], offs)
         nc.sync.dma_start(idx2[:], offs2)
-        nc.sync.dma_start(
-            stage[64:P:4, 2 * S : 2 * S + 2 * N].bitcast(I32).rearrange("q (a n) -> q a n", a=2),
-            wa_scales.bitcast(I32).rearrange("a q n -> q a n"))
+        nc.gpsimd.dma_start(gain_sb[:], gain.rearrange("(b p t) -> p b t", b=2, t=PACK))
         load_wm(0, 0)
         nc.sync.dma_start(
             first[0:P:4, 0:T].bitcast(I32), tab_scales.rearrange("a q t -> (a q) t").bitcast(I32))
@@ -117,63 +117,75 @@ def tile_list_attitude_propagation_kernel(
         v2_s = held([P, S], U8, "v2_s")
         nc.vector.tensor_copy(v_s[:], tab_s.indirect(idx[:]))
         nc.vector.tensor_copy(v2_s[:], tab2_s[:].indirect(idx2[:]))
-        nc.vector.tensor_copy(stage[:, 0:S].bitcast(I32), v_s[:].bitcast(I32))
-        nc.vector.tensor_copy(stage[:, S : 2 * S].bitcast(I32), v2_s[:].bitcast(I32))
+        nc.vector.tensor_copy(stage_r[:, 0:S].bitcast(I32), v2_s[:].bitcast(I32))
         nc.vector.tensor_copy(
-            stage[:, 2 * S + 2 * N :].rearrange("p (b t m) -> p b t m", b=2, t=PACK),
+            stage_r[:, S:].rearrange("p (b t m) -> p b t m", b=2, t=PACK),
             wr_s_raw.rearrange("p (b m t) -> p b t m", b=2, t=PACK))
+        nc.vector.tensor_copy(stage_w[:, 0:S].bitcast(I32), v_s[:].bitcast(I32))
 
-        def move_rows(plane, spread, first_row):
-            for r in range(4):
-                lo = first_row + 4 * r
-                nc.sync.dma_start(plane[r:P:32, :].bitcast(I32), spread[lo : lo + 49 : 16, :].bitcast(I32))
+        def move_rows(plane, plane_row, spread, spread_row, rows=range(4)):
+            for r in rows:
+                lo = spread_row + 4 * r
+                nc.sync.dma_start(
+                    plane[plane_row + r : P : 32, :].bitcast(I32), spread[lo : lo + 49 : 16, :].bitcast(I32))
 
-        move_rows(plane_a, v_s, 0)
+        move_rows(plane_m[0], 4, v_s, 0)
         load_tab(1)
-        move_rows(plane_b, stage, 64)
-        nc.sync.dma_start(gain_sb[:], gain.rearrange("(b p t) -> p b t", b=2, t=PACK))
-        nc.sync.dma_start(wr_raw[:], wr_words[0].rearrange("p c i -> p (c i)").bitcast(I32))
+        move_rows(plane_m[1], 8, v_s, 64)
+        move_rows(plane_r, 0, stage_r, 64, range(2))
         nc.sync.dma_start(tab2_w[:], tab2_words[0].bitcast(I32))
-        nc.sync.dma_start(wa_w[:].bitcast(I32), wa_words.bitcast(I32).rearrange("a p c -> p a c"))
+        move_rows(plane_r, 0, stage_r, 64, range(2, 4))
+        nc.sync.dma_start(wr_raw[:], wr_words[0].rearrange("p c i -> p (c i)").bitcast(I32))
         load_wm(1, 0)
+        nc.sync.dma_start(
+            stage_w[0:P:4, S:].bitcast(I32), wa_scales.rearrange("a q n -> (a q) n").bitcast(I32))
         load_wm(1, 1)
         load_wn(0)
+        nc.sync.dma_start(wa_w[:].bitcast(I32), wa_words.bitcast(I32).rearrange("a p c -> p a c"))
+        move_rows(plane_w[0], 0, stage_w, 0)
         load_wn(1)
+        move_rows(plane_w[1], 0, stage_w, 64)
         with nc.allow_non_contiguous_dma(reason="one drift value a partition"):
             nc.sync.dma_start(drift_sb[:], drift.rearrange("(c p) -> p c", p=P))
 
         v_w0 = placed([P, S], U32, "v_w0", at["v_w0"])
         v_w1 = [held([P, NT], U32, "v_w1%d" % j) for j in range(2)]
         wr_c = placed([P, H], I32, "wr_c", at["tab1"])
-        v2_w = [placed([P, 2 * NT], U8, "v2_w%d" % j, at["tab1"] + 4 * KB + KB * j) for j in range(2)]
+        v2_w = [placed([P, 2 * NT], U8, "v2_w0", at["tab1"] + 4 * KB), placed([P, 2 * NT], U8, "v2_w1", at["wr"])]
         half = NT // 16
 
         wm_bf = [[held([P, KP * PACK], BF16, "wm_bf0%d" % a) for a in range(2)],
-                 [placed([P, KP * PACK], BF16, "wm_bf10", at["wm_bf10"]),
-                  placed([P, KP * PACK], BF16, "wm_bf11", at["ring_b"])]]
+                 [placed([P, KP * PACK], BF16, "wm_bf10", at["wm_bf10"])]]
+        wm_bf11 = [placed([P, KP * 2], BF16, "wm_bf11_0", at["wn_bf0"]),
+                   placed([P, KP * 2], BF16, "wm_bf11_1", at["wm_bf10"])]
         wm_c = [[placed([P, KP], U32, "wm_c00", at["tab2_s"]), placed([P, KP], U32, "wm_c01", at["wm_c01"])],
                 [held([P, KP], U32, "wm_c1%d" % a) for a in range(2)]]
         wm_s = [[held([P, KP], U8, "wm_s%d%d" % (b, a)) for a in range(2)] for b in range(2)]
-        wn_bf = [placed([P, N * PACK], BF16, "wn_bf0", at["ring_b"]),
-                 placed([P, N * PACK], BF16, "wn_bf1", at["ring_c"])]
+        wn_bf = [placed([P, N * PACK], BF16, "wn_bf%d" % b, at["wn_bf%d" % b]) for b in range(2)]
         wn_c = [held([P, N], U32, "wn_c%d" % b) for b in range(2)]
-        wn_s = [placed([P, N], U8, "wn_s%d" % b, at["sine0"] + 6 * KB + N * b) for b in range(2)]
+        wn_s = [held([P, N], U8, "wn_s%d" % b) for b in range(2)]
         h_c = [[held([P, NT], U32, "h_c%d%d" % (b, j)) for j in range(2)] for b in range(2)]
         h_s = [[held([P, NT], U8, "h_s%d%d" % (b, j)) for j in range(2)] for b in range(2)]
-        planes = [[held([P, PACK, NT], BF16, "h_planes00"), placed([P, PACK, NT], BF16, "h_planes01", at["ring_a"])],
-                  [held([P, PACK, NT], BF16, "h_planes1%d" % j) for j in range(2)]]
-        woven = [[placed([P, NT * PACK], BF16, "h_bf00", at["ring_c"]), placed([P, NT * PACK], BF16, "h_bf01", at["ring_b"])],
-                 [placed([P, NT * PACK], BF16, "h_bf1%d" % j, at["ring_d"]) for j in range(2)]]
+        planes = [[held([P, PACK, NT], BF16, "h_planes%d%d" % (b, j)) for j in range(2)] for b in range(2)]
+        woven = [[placed([P, NT * PACK], BF16, "h_bf0%d" % j, at["h_bf0%d" % j]) for j in range(2)],
+                 [held([P, NT * PACK], BF16, "h_bf1%d" % j) for j in range(2)]]
 
-        def cast_wm(b, a, copy, lo, hi):
+        def cast_wm(b, a, copy):
             copy(
-                wm_bf[b][a][:].rearrange("p (t m j) -> p m j t", t=PACK, j=PACK)[:, :, :, lo:hi],
-                wm_raw[b][a][:].rearrange("p j (m t) -> p m j t", t=PACK)[:, :, :, lo:hi])
+                wm_bf[b][a][:].rearrange("p (t m j) -> p m j t", t=PACK, j=PACK),
+                wm_raw[b][a][:].rearrange("p j (m t) -> p m j t", t=PACK))
 
-        def quant_wm(b, a, lo, hi):
-            nc.vector.quantize_mx(
-                wm_c[b][a][:, P * lo : P * hi].bitcast(FP8X4), wm_s[b][a][:, P * lo : P * hi],
-                wm_bf[b][a][:, KP * lo : KP * hi])
+        def quant_wm(b, a):
+            nc.vector.quantize_mx(wm_c[b][a][:].bitcast(FP8X4), wm_s[b][a][:], wm_bf[b][a][:])
+
+        def cast_last_wm(side, copy):
+            copy(
+                wm_bf11[side][:].rearrange("p (t m j) -> p m j t", t=2, j=PACK),
+                wm_raw[1][1][:].rearrange("p j (m t) -> p m j t", t=PACK)[:, :, :, 2 * side : 2 * side + 2])
+
+        def quant_last_wm(side):
+            cols = slice(2 * P * side, 2 * P * (side + 1))
+            nc.vector.quantize_mx(wm_c[1][1][:, cols].bitcast(FP8X4), wm_s[1][1][:, cols], wm_bf11[side][:])
 
         def interleave(copy, dst, src, lo, hi):
             copy(
@@ -201,7 +213,7 @@ def tile_list_attitude_propagation_kernel(
             cols = slice(P * t, P * (t + 1))
             nc.tensor.matmul_mx(
                 phases[b, j, t][:], lhsT=wm_c[b][a][:, cols].bitcast(FP8X4), lhsT_scale=wm_s[b][a][:, cols],
-                rhs=v_words(a, j), rhs_scale=v_plane[a][:, NT * j : NT * (j + 1)],
+                rhs=v_words(a, j), rhs_scale=plane_m[a][4 * a + 4 : P, NT * j : NT * (j + 1)],
                 start=(a == 0), stop=(a == 1))
 
         def open_phase(b, j, t, n):
@@ -211,7 +223,7 @@ def tile_list_attitude_propagation_kernel(
         def kick(b, j, t):
             phase_pass(b, j, t, 1)
             sine = placed([P, NT], F32, "sine%d%d%d" % (b, j, t), at["sine%d" % j] + 2 * KB * t)
-            nc.scalar.activation(sine[:], phases[b, j, t][:], ACT.Sin, bias=(zero, zero_late[:])[b], scale=-1.0)
+            nc.scalar.activation(sine[:], phases[b, j, t][:], ACT.Sin, bias=(zero, zero_late)[b], scale=-1.0)
             sines[b, j, t] = sine
 
         def old_rate(b, j, t, n):
@@ -231,8 +243,8 @@ def tile_list_attitude_propagation_kernel(
             for a in range(2):
                 nc.tensor.matmul_mx(
                     acc[j, c][:], lhsT=wa_w[:, a, 2 * P * c : 2 * P * (c + 1)].bitcast(FP4X4),
-                    lhsT_scale=wa_s[a][:, P * c : P * (c + 1)],
-                    rhs=v_words(a, j), rhs_scale=v_plane[a][:, NT * j : NT * (j + 1)],
+                    lhsT_scale=plane_w[a][:, S + P * c : S + P * (c + 1)],
+                    rhs=v_words(a, j), rhs_scale=plane_w[a][:, NT * j : NT * (j + 1)],
                     start=(a == 0), stop=False)
 
         def add_h(b, j, c):
@@ -249,19 +261,44 @@ def tile_list_attitude_propagation_kernel(
                 nc.scalar.activation(res[:], acc[j, c][:], ACT.Identity, bias=drift_sb[:, c : c + 1])
             nc.sync.dma_start(out[P * c : P * (c + 1), NT * j : NT * (j + 1)], res[:])
 
+        def close_in_halves(j, c, banks):
+            cols = slice(P * c, P * (c + 1))
+            for side, n in enumerate(banks):
+                total = bank(n, "angle")[:, 0:NH]
+                lo = NH * side
+                for a in range(2):
+                    nc.tensor.matmul_mx(
+                        total, lhsT=wa_w[:, a, 2 * P * c : 2 * P * (c + 1)].bitcast(FP4X4),
+                        lhsT_scale=plane_w[a][:, S + P * c : S + P * (c + 1)], rhs=v_words(a, j)[:, lo : lo + NH],
+                        rhs_scale=plane_w[a][:, NT * j + lo : NT * j + lo + NH], start=(a == 0), stop=False)
+                for b in range(2):
+                    nc.tensor.matmul_mx(
+                        total, lhsT=wn_c[b][:, cols].bitcast(FP8X4), lhsT_scale=wn_s[b][:, cols],
+                        rhs=h_c[b][j][:, lo : lo + NH].bitcast(FP8X4), rhs_scale=h_s[b][j][:, lo : lo + NH],
+                        start=False, stop=(b == 1))
+                res = placed([P, NH], F32, "res_half%d" % side, at["tab0"] + 2 * KB * (4 * j + c) + KB * side)
+                if side == 0:
+                    nc.scalar.activation(res[:], total, ACT.Identity, bias=drift_sb[:, c : c + 1])
+                else:
+                    nc.vector.tensor_scalar(res[:], total, drift_sb[:, c : c + 1], None, ALU.add)
+                nc.sync.dma_start(out[cols, NT * j + lo : NT * j + lo + NH], res[:])
+
+        def gather_v2(j):
+            nc.vector.tensor_copy(
+                v2_w[j][:].bitcast(U16), tab2_w[:].bitcast(U16).indirect(idx2[:, half * j : half * (j + 1)]))
+
         for a in range(2):
-            cast_wm(0, a, nc.scalar.copy, 0, PACK)
-            quant_wm(0, a, 0, PACK)
+            cast_wm(0, a, nc.scalar.copy)
+            quant_wm(0, a)
         nc.vector.tensor_copy(v_w0[:], tab_w[0][:].bitcast(U32).indirect(idx[:]))
         for j in range(2):
             nc.vector.tensor_copy(
                 v_w1[j][:], tab_w[1][:].bitcast(U32).indirect(idx[:, half * j : half * (j + 1)]))
+        gather_v2(0)
         nc.vector.tensor_copy(
             wr_c[:].rearrange("p (b t u i) -> p b u t i", b=2, t=PACK, i=4),
             wr_raw[:].rearrange("p (b u i t) -> p b u t i", b=2, t=PACK, i=4))
-        for j in range(2):
-            nc.vector.tensor_copy(
-                v2_w[j][:].bitcast(U16), tab2_w[:].bitcast(U16).indirect(idx2[:, half * j : half * (j + 1)]))
+        gather_v2(1)
 
         for j in range(2):
             for t in range(PACK):
@@ -269,58 +306,54 @@ def tile_list_attitude_propagation_kernel(
         for j in range(2):
             for t in range(PACK):
                 kick(0, j, t)
+        for j in range(2):
+            for t in range(PACK):
+                old_rate(0, j, t, 4 * j + t)
+                new_rate(0, j, t)
         for t in range(PACK):
-            old_rate(0, 0, t, t)
-            new_rate(0, 0, t)
-        cast_wm(1, 0, nc.scalar.copy, 0, 2)
-        cast_wm(1, 0, nc.vector.tensor_copy, 2, PACK)
-        quant_wm(1, 0, 0, PACK)
+            old_rate(1, 0, t, RATE_BANKS[t])
+        cast_wm(1, 0, nc.scalar.copy)
+        quant_wm(1, 0)
+        cast_last_wm(0, nc.scalar.copy)
+        quant_last_wm(0)
+        cast_last_wm(1, nc.vector.tensor_copy)
+        quant_last_wm(1)
+        interleave(nc.scalar.copy, woven[0][0], planes[0][0], 0, NT)
+        interleave(nc.vector.tensor_copy, wn_bf[0], wn_raw[0], 0, N)
         for t in range(PACK):
-            old_rate(0, 1, t, 4 + t)
-            new_rate(0, 1, t)
-        for c in range(4):
-            open_angle(0, c, c)
-        cast_wm(1, 1, nc.scalar.copy, 0, 2)
-        cast_wm(1, 1, nc.scalar.copy, 2, PACK)
-        interleave(nc.scalar.copy, woven[0][0], planes[0][0], 0, H00_SCALAR)
-        quant_wm(1, 1, 0, 2)
-        quant_wm(1, 1, 2, PACK)
-        for t in range(PACK):
-            open_phase(1, 0, t, 4 + t)
+            open_phase(1, 0, t, PHASE_BANKS[t])
         for t in range(PACK):
             kick(1, 0, t)
-        interleave(nc.vector.tensor_copy, woven[0][0], planes[0][0], H00_SCALAR, NT)
-        interleave(nc.vector.tensor_copy, wn_bf[0], wn_raw[0], 0, N)
-        quant_h(0, 0)
-        interleave(nc.scalar.copy, wn_bf[1], wn_raw[1], 0, N // 2)
         for t in range(PACK):
-            old_rate(1, 0, t, 4 + t)
             new_rate(1, 0, t)
         for t in range(PACK):
-            open_phase(1, 1, t, 4 + t)
+            open_phase(1, 1, t, PHASE_BANKS[t])
             kick(1, 1, t)
+        quant_h(0, 0)
         quant_wn(0)
-        interleave(nc.vector.tensor_copy, woven[1][0], planes[1][0], 0, NT)
-        quant_h(1, 0)
-        interleave(nc.scalar.copy, wn_bf[1], wn_raw[1], N // 2, N)
-        interleave(nc.scalar.copy, woven[0][1], planes[0][1], 0, NT)
         for t in range(PACK):
-            old_rate(1, 1, t, 4 + t)
+            old_rate(1, 1, t, RATE_BANKS[t])
             new_rate(1, 1, t)
-        for c in range(4):
-            add_h(0, 0, c)
+        interleave(nc.scalar.copy, wn_bf[1], wn_raw[1], 0, N)
+        interleave(nc.scalar.copy, woven[0][1], planes[0][1], 0, NT)
+        interleave(nc.vector.tensor_copy, woven[1][0], planes[1][0], 0, NT)
         quant_wn(1)
+        quant_h(1, 0)
         interleave(nc.vector.tensor_copy, woven[1][1], planes[1][1], 0, NT)
         quant_h(0, 1)
         quant_h(1, 1)
-        for c in range(2):
-            open_angle(1, c, 4 + c)
+        for c in range(4):
+            open_angle(0, c, PHASE_BANKS[c])
+        for c in range(4):
+            add_h(0, 0, c)
+        for c in range(3):
+            open_angle(1, c, RATE_BANKS[c])
         for c in range(4):
             add_h(1, 0, c)
             finish(0, c)
-        for c in range(2, 4):
-            open_angle(1, c, 4 + c)
-        for c in range(4):
+        for c in range(3):
             add_h(0, 1, c)
+        for c in range(3):
             add_h(1, 1, c)
             finish(1, c)
+        close_in_halves(1, 3, (RATE_BANKS[3], PHASE_BANKS[0]))

@@ -48,32 +48,30 @@ def tile_list_attitude_propagation_kernel(
         at = {}
         end = 0
         for name, size in (
-            ("tab_s", 4 * KB), ("tab1", 16 * KB), ("first_end", 0), ("wr_s", KB), ("wr", 4 * KB), ("tab2", 8 * KB), ("wa", 2 * KB),
-            ("wm10", 8 * KB), ("wm11", 8 * KB), ("wn0", 8 * KB), ("wn1", 8 * KB), ("drift", 64),
-            ("wm_c01", 2 * KB), ("v_w0", 4 * KB), ("stage_w", S + N), ("late_end", 0),
-            ("tab2_s", 4 * KB), ("wm01", 8 * KB), ("tab0", 16 * KB), ("sine0", 8 * KB), ("sine1", 8 * KB),
+            ("tab0", 16 * KB), ("tab1", 16 * KB), ("tab2", 8 * KB), ("wr", 4 * KB), ("early_end", 0),
+            ("wm_bf01", 4 * KB), ("wm10", 8 * KB), ("wm11", 8 * KB), ("wn0", 8 * KB), ("wa", 2 * KB),
+            ("plane_w", S + 2 * N), ("wn1", 8 * KB), ("drift", 64), ("late_end", 0),
+            ("tab_s", 4 * KB), ("tab2_s", 4 * KB), ("wr_s", 4 * KB), ("sine0", 8 * KB), ("sine1", 8 * KB),
             ("wm_bf10", 4 * KB), ("h_bf00", 4 * KB), ("wn_bf0", 4 * KB), ("wn_bf1", 4 * KB), ("h_bf01", 4 * KB),
         ):
             at[name] = end
             end = end + size
 
-        first = placed([P, at["first_end"]], U8, "first", 0)
-        tab_s = first[:, 0:T]
+        tab_s = placed([P, T], U8, "tab_s", at["tab_s"])
         tab2_s = placed([P, T], U8, "tab2_s", at["tab2_s"])
-        head = placed([P, at["late_end"] - at["wr_s"]], U8, "head", at["wr_s"])
-        wr_s_raw = head[:, 0:H]
+        wr_s_raw = placed([P, H], U8, "wr_s_raw", at["wr_s"])
+        zero_src = placed([P, at["early_end"] // 4], F32, "zero_src", 0)[:, 0:1]
         zero_in = held([P, 1], F32, "zero_in")
-        zero_src = placed([P, 32], F32, "zero_src", at["tab0"] - 64)
         zero = placed([P, (at["wn_bf0"] - at["wm_bf10"]) // 4 + 16], F32, "zero", at["wm_bf10"])[:, 0:1]
-        nc.vector.memset(tab_s.bitcast(I32), 0)
-        nc.vector.memset(tab2_s[:].bitcast(I32), 0)
-        nc.vector.memset(wr_s_raw.bitcast(I32), 0)
-        nc.vector.memset(zero_src[:, 0:1], 0.0)
-        nc.vector.tensor_copy(zero_in[:], zero_src[:, 0:1])
         zero_late = placed([P, 32], F32, "zero_late", at["h_bf01"] - 64)[:, 0:1]
+        nc.gpsimd.memset(wr_s_raw[:].bitcast(I32), 0)
+        nc.vector.memset(tab_s[:].bitcast(I32), 0)
+        nc.vector.memset(tab2_s[:].bitcast(I32), 0)
+        nc.vector.memset(zero_src, 0.0)
+        nc.vector.tensor_copy(zero_in[:], zero_src)
         nc.vector.memset(zero_late, 0.0)
 
-        wm_raw = [[held([P, PACK, KP], F32, "wm_raw00"), placed([P, PACK, KP], F32, "wm_raw01", at["wm01"])],
+        wm_raw = [[held([P, PACK, KP], F32, "wm_raw0%d" % a) for a in range(2)],
                   [placed([P, PACK, KP], F32, "wm_raw1%d" % a, at["wm1%d" % a]) for a in range(2)]]
         tab_w = [placed([P, T], I32, "tab_w%d" % a, at["tab%d" % a]) for a in range(2)]
         tab2_w = placed([P, T // 2], I32, "tab2_w", at["tab2"])
@@ -83,10 +81,11 @@ def tile_list_attitude_propagation_kernel(
         gain_sb = held([P, 2, PACK], F32, "gain_sb")
         drift_sb = placed([P, N // P], F32, "drift_sb", at["drift"])
         stage_r = held([P, S + H], U8, "stage_r")
-        stage_w = placed([P, S + N], U8, "stage_w", at["stage_w"])
-        plane_m = [held([P, S], U8, "plane_m%d" % a) for a in range(2)]
+        plane_m = held([P, S], U8, "plane_m")
         plane_r = held([P, S + H], U8, "plane_r")
-        plane_w = [held([P, S + N], U8, "plane_w%d" % a) for a in range(2)]
+        plane_w = placed([P, S], U8, "plane_w", at["plane_w"])
+        wa_s = placed([P, 2, N], U8, "wa_s", at["plane_w"] + S)
+        wa_plane = [plane_m, plane_w]
         v2_plane = plane_r[:, 0:S]
         wr_s = plane_r[:, S:]
 
@@ -103,62 +102,48 @@ def tile_list_attitude_propagation_kernel(
 
         nc.sync.dma_start(idx[:], offs)
         nc.sync.dma_start(idx2[:], offs2)
-        nc.gpsimd.dma_start(gain_sb[:], gain.rearrange("(b p t) -> p b t", b=2, t=PACK))
         load_wm(0, 0)
-        nc.sync.dma_start(
-            first[0:P:4, 0:T].bitcast(I32), tab_scales.rearrange("a q t -> (a q) t").bitcast(I32))
-        nc.sync.dma_start(tab2_s[64:P:4, :].bitcast(I32), tab2_scales[0].bitcast(I32))
-        nc.sync.dma_start(head[64:P:4, 0:H].bitcast(I32), wr_scales[0].bitcast(I32))
-        nc.scalar.activation(zero, zero_in[:], ACT.Sin)
         load_wm(0, 1)
+        for q in range(4):
+            nc.scalar.dma_start(
+                tab_s[32 * q : 32 * (q + 1) : 4, :].bitcast(I32), tab_scales[:, 4 * q : 4 * (q + 1), :].bitcast(I32))
+        nc.scalar.dma_start(tab2_s[64:P:4, :].bitcast(I32), tab2_scales[0].bitcast(I32))
+        nc.scalar.activation(zero, zero_in[:], ACT.Sin)
+        nc.gpsimd.dma_start(wr_s_raw[64:P:4, :].bitcast(I32), wr_scales[0].bitcast(I32))
+        nc.gpsimd.dma_start(gain_sb[:], gain.rearrange("(b p t) -> p b t", b=2, t=PACK))
         load_tab(0)
+        load_tab(1)
+        nc.sync.dma_start(tab2_w[:], tab2_words[0].bitcast(I32))
+        nc.sync.dma_start(wr_raw[:], wr_words[0].rearrange("p c i -> p (c i)").bitcast(I32))
 
         v_s = held([P, S], U8, "v_s")
         v2_s = held([P, S], U8, "v2_s")
-        nc.vector.tensor_copy(v_s[:], tab_s.indirect(idx[:]))
+        nc.vector.tensor_copy(v_s[:], tab_s[:].indirect(idx[:]))
         nc.vector.tensor_copy(v2_s[:], tab2_s[:].indirect(idx2[:]))
         nc.vector.tensor_copy(stage_r[:, 0:S].bitcast(I32), v2_s[:].bitcast(I32))
         nc.vector.tensor_copy(
             stage_r[:, S:].rearrange("p (b t m) -> p b t m", b=2, t=PACK),
-            wr_s_raw.rearrange("p (b m t) -> p b t m", b=2, t=PACK))
-        nc.vector.tensor_copy(stage_w[:, 0:S].bitcast(I32), v_s[:].bitcast(I32))
+            wr_s_raw[:].rearrange("p (b m t) -> p b t m", b=2, t=PACK))
 
-        def move_rows(plane, plane_row, spread, spread_row, rows=range(4)):
-            for r in rows:
-                lo = spread_row + 4 * r
-                nc.sync.dma_start(
-                    plane[plane_row + r : P : 32, :].bitcast(I32), spread[lo : lo + 49 : 16, :].bitcast(I32))
+        for q in range(4):
+            nc.scalar.dma_start(
+                plane_m[32 * q : 32 * q + 8, :].bitcast(I32), v_s[32 * q : 32 * (q + 1) : 4, :].bitcast(I32))
+        for r in range(4):
+            nc.gpsimd.dma_start(
+                plane_r[r:P:32, :].bitcast(I32), stage_r[64 + 4 * r : 64 + 4 * r + 49 : 16, :].bitcast(I32))
 
-        move_rows(plane_m[0], 4, v_s, 0)
-        load_tab(1)
-        move_rows(plane_m[1], 8, v_s, 64)
-        move_rows(plane_r, 0, stage_r, 64, range(2))
-        nc.sync.dma_start(tab2_w[:], tab2_words[0].bitcast(I32))
-        move_rows(plane_r, 0, stage_r, 64, range(2, 4))
-        nc.sync.dma_start(wr_raw[:], wr_words[0].rearrange("p c i -> p (c i)").bitcast(I32))
-        load_wm(1, 0)
-        nc.sync.dma_start(
-            stage_w[0:P:4, S:].bitcast(I32), wa_scales.rearrange("a q n -> (a q) n").bitcast(I32))
-        load_wm(1, 1)
-        load_wn(0)
-        nc.sync.dma_start(wa_w[:].bitcast(I32), wa_words.bitcast(I32).rearrange("a p c -> p a c"))
-        move_rows(plane_w[0], 0, stage_w, 0)
-        load_wn(1)
-        move_rows(plane_w[1], 0, stage_w, 64)
-        with nc.allow_non_contiguous_dma(reason="one drift value a partition"):
-            nc.sync.dma_start(drift_sb[:], drift.rearrange("(c p) -> p c", p=P))
-
-        v_w0 = placed([P, S], U32, "v_w0", at["v_w0"])
+        v_w0 = placed([P, S], U32, "v_w0", at["wr_s"])
         v_w1 = [held([P, NT], U32, "v_w1%d" % j) for j in range(2)]
         wr_c = placed([P, H], I32, "wr_c", at["tab1"])
         v2_w = [placed([P, 2 * NT], U8, "v2_w0", at["tab1"] + 4 * KB), placed([P, 2 * NT], U8, "v2_w1", at["wr"])]
         half = NT // 16
 
-        wm_bf = [[held([P, KP * PACK], BF16, "wm_bf0%d" % a) for a in range(2)],
-                 [placed([P, KP * PACK], BF16, "wm_bf10", at["wm_bf10"])]]
+        wm_bf = [[held([P, KP * PACK], BF16, "wm_bf00")[:],
+                  placed([P, (at["late_end"] - at["wm_bf01"]) // 2], BF16, "wm_bf01", at["wm_bf01"])[:, 0 : KP * PACK]],
+                 [placed([P, KP * PACK], BF16, "wm_bf10", at["wm_bf10"])[:]]]
         wm_bf11 = [placed([P, KP * 2], BF16, "wm_bf11_0", at["wn_bf0"]),
                    placed([P, KP * 2], BF16, "wm_bf11_1", at["wm_bf10"])]
-        wm_c = [[placed([P, KP], U32, "wm_c00", at["tab2_s"]), placed([P, KP], U32, "wm_c01", at["wm_c01"])],
+        wm_c = [[placed([P, KP], U32, "wm_c00", at["tab2_s"]), placed([P, KP], U32, "wm_c01", at["tab2_s"] + 2 * KB)],
                 [held([P, KP], U32, "wm_c1%d" % a) for a in range(2)]]
         wm_s = [[held([P, KP], U8, "wm_s%d%d" % (b, a)) for a in range(2)] for b in range(2)]
         wn_bf = [placed([P, N * PACK], BF16, "wn_bf%d" % b, at["wn_bf%d" % b]) for b in range(2)]
@@ -172,11 +157,11 @@ def tile_list_attitude_propagation_kernel(
 
         def cast_wm(b, a, copy):
             copy(
-                wm_bf[b][a][:].rearrange("p (t m j) -> p m j t", t=PACK, j=PACK),
+                wm_bf[b][a].rearrange("p (t m j) -> p m j t", t=PACK, j=PACK),
                 wm_raw[b][a][:].rearrange("p j (m t) -> p m j t", t=PACK))
 
         def quant_wm(b, a):
-            nc.vector.quantize_mx(wm_c[b][a][:].bitcast(FP8X4), wm_s[b][a][:], wm_bf[b][a][:])
+            nc.vector.quantize_mx(wm_c[b][a][:].bitcast(FP8X4), wm_s[b][a][:], wm_bf[b][a])
 
         def cast_last_wm(side, copy):
             copy(
@@ -213,7 +198,7 @@ def tile_list_attitude_propagation_kernel(
             cols = slice(P * t, P * (t + 1))
             nc.tensor.matmul_mx(
                 phases[b, j, t][:], lhsT=wm_c[b][a][:, cols].bitcast(FP8X4), lhsT_scale=wm_s[b][a][:, cols],
-                rhs=v_words(a, j), rhs_scale=plane_m[a][4 * a + 4 : P, NT * j : NT * (j + 1)],
+                rhs=v_words(a, j), rhs_scale=plane_m[4 * a : P, NT * j : NT * (j + 1)],
                 start=(a == 0), stop=(a == 1))
 
         def open_phase(b, j, t, n):
@@ -243,8 +228,8 @@ def tile_list_attitude_propagation_kernel(
             for a in range(2):
                 nc.tensor.matmul_mx(
                     acc[j, c][:], lhsT=wa_w[:, a, 2 * P * c : 2 * P * (c + 1)].bitcast(FP4X4),
-                    lhsT_scale=plane_w[a][:, S + P * c : S + P * (c + 1)],
-                    rhs=v_words(a, j), rhs_scale=plane_w[a][:, NT * j : NT * (j + 1)],
+                    lhsT_scale=wa_s[:, a, P * c : P * (c + 1)],
+                    rhs=v_words(a, j), rhs_scale=wa_plane[a][:, NT * j : NT * (j + 1)],
                     start=(a == 0), stop=False)
 
         def add_h(b, j, c):
@@ -269,8 +254,8 @@ def tile_list_attitude_propagation_kernel(
                 for a in range(2):
                     nc.tensor.matmul_mx(
                         total, lhsT=wa_w[:, a, 2 * P * c : 2 * P * (c + 1)].bitcast(FP4X4),
-                        lhsT_scale=plane_w[a][:, S + P * c : S + P * (c + 1)], rhs=v_words(a, j)[:, lo : lo + NH],
-                        rhs_scale=plane_w[a][:, NT * j + lo : NT * j + lo + NH], start=(a == 0), stop=False)
+                        lhsT_scale=wa_s[:, a, P * c : P * (c + 1)], rhs=v_words(a, j)[:, lo : lo + NH],
+                        rhs_scale=wa_plane[a][:, NT * j + lo : NT * j + lo + NH], start=(a == 0), stop=False)
                 for b in range(2):
                     nc.tensor.matmul_mx(
                         total, lhsT=wn_c[b][:, cols].bitcast(FP8X4), lhsT_scale=wn_s[b][:, cols],
@@ -289,8 +274,22 @@ def tile_list_attitude_propagation_kernel(
 
         for a in range(2):
             cast_wm(0, a, nc.scalar.copy)
+        for a in range(2):
             quant_wm(0, a)
         nc.vector.tensor_copy(v_w0[:], tab_w[0][:].bitcast(U32).indirect(idx[:]))
+        load_wm(1, 0)
+        load_wm(1, 1)
+        load_wn(0)
+        nc.sync.dma_start(wa_w[:].bitcast(I32), wa_words.bitcast(I32).rearrange("a p c -> p a c"))
+        for r in range(4):
+            nc.sync.dma_start(plane_w[r:P:32, :].bitcast(I32), v_s[16 + 4 * r : P : 32, :].bitcast(I32))
+        load_wn(1)
+        for q in range(4):
+            nc.sync.dma_start(
+                wa_s[32 * q : 32 * q + 4, :, :].bitcast(I32),
+                wa_scales[:, 4 * q : 4 * q + 4, :].bitcast(I32).rearrange("a r n -> r a n"))
+        with nc.allow_non_contiguous_dma(reason="one drift value a partition"):
+            nc.sync.dma_start(drift_sb[:], drift.rearrange("(c p) -> p c", p=P))
         for j in range(2):
             nc.vector.tensor_copy(
                 v_w1[j][:], tab_w[1][:].bitcast(U32).indirect(idx[:, half * j : half * (j + 1)]))

@@ -48,27 +48,27 @@ def tile_list_attitude_propagation_kernel(
         at = {}
         end = 0
         for name, size in (
-            ("tab0", 16 * KB), ("tab1", 16 * KB), ("tab2", 8 * KB), ("wr", 4 * KB), ("early_end", 0),
-            ("wm_bf01", 4 * KB), ("wm10", 8 * KB), ("wm11", 8 * KB), ("wn0", 8 * KB), ("wa", 2 * KB),
-            ("plane_w", S + 2 * N), ("wn1", 8 * KB), ("drift", 64), ("late_end", 0),
-            ("tab_s", 4 * KB), ("tab2_s", 4 * KB), ("wr_s", 4 * KB), ("sine0", 8 * KB), ("sine1", 8 * KB),
+            ("tab_s", 4 * KB), ("tab1", 16 * KB), ("first_end", 0),
+            ("tab2_s", 4 * KB), ("tab2", 8 * KB), ("wr", 4 * KB), ("wm10", 8 * KB), ("wm11", 8 * KB),
+            ("wn0", 8 * KB), ("wa", 2 * KB), ("wa_s", 2 * N), ("wn1", 8 * KB), ("drift", 64), ("late_end", 0),
+            ("tab0", 16 * KB), ("wr_s", KB), ("wm_bf01", 4 * KB), ("sine0", 8 * KB), ("sine1", 8 * KB),
             ("wm_bf10", 4 * KB), ("h_bf00", 4 * KB), ("wn_bf0", 4 * KB), ("wn_bf1", 4 * KB), ("h_bf01", 4 * KB),
         ):
             at[name] = end
             end = end + size
 
-        tab_s = placed([P, T], U8, "tab_s", at["tab_s"])
-        tab2_s = placed([P, T], U8, "tab2_s", at["tab2_s"])
+        first = placed([P, at["first_end"]], U8, "first", 0)
+        second = placed([P, at["late_end"] - at["tab2_s"]], U8, "second", at["tab2_s"])
+        tab_s = first[:, 0:T]
+        tab2_s = second[:, 0:T]
         wr_s_raw = placed([P, H], U8, "wr_s_raw", at["wr_s"])
-        zero_src = placed([P, at["early_end"] // 4], F32, "zero_src", 0)[:, 0:1]
         zero_in = held([P, 1], F32, "zero_in")
         zero = placed([P, (at["wn_bf0"] - at["wm_bf10"]) // 4 + 16], F32, "zero", at["wm_bf10"])[:, 0:1]
         zero_late = placed([P, 32], F32, "zero_late", at["h_bf01"] - 64)[:, 0:1]
         nc.gpsimd.memset(wr_s_raw[:].bitcast(I32), 0)
-        nc.vector.memset(tab_s[:].bitcast(I32), 0)
-        nc.vector.memset(tab2_s[:].bitcast(I32), 0)
-        nc.vector.memset(zero_src, 0.0)
-        nc.vector.tensor_copy(zero_in[:], zero_src)
+        nc.vector.memset(tab_s.bitcast(I32), 0)
+        nc.vector.memset(tab2_s.bitcast(I32), 0)
+        nc.vector.memset(zero_in[:], 0.0)
         nc.vector.memset(zero_late, 0.0)
 
         wm_raw = [[held([P, PACK, KP], F32, "wm_raw0%d" % a) for a in range(2)],
@@ -81,11 +81,9 @@ def tile_list_attitude_propagation_kernel(
         gain_sb = held([P, 2, PACK], F32, "gain_sb")
         drift_sb = placed([P, N // P], F32, "drift_sb", at["drift"])
         stage_r = held([P, S + H], U8, "stage_r")
-        plane_m = held([P, S], U8, "plane_m")
+        v_plane = [held([P, S], U8, "v_plane%d" % a) for a in range(2)]
         plane_r = held([P, S + H], U8, "plane_r")
-        plane_w = placed([P, S], U8, "plane_w", at["plane_w"])
-        wa_s = placed([P, 2, N], U8, "wa_s", at["plane_w"] + S)
-        wa_plane = [plane_m, plane_w]
+        wa_s = placed([P, 2, N], U8, "wa_s", at["wa_s"])
         v2_plane = plane_r[:, 0:S]
         wr_s = plane_r[:, S:]
 
@@ -101,51 +99,63 @@ def tile_list_attitude_propagation_kernel(
             nc.sync.dma_start(tab_w[a][:], tab_words[a].rearrange("p t i -> p (t i)").bitcast(I32))
 
         nc.sync.dma_start(idx[:], offs)
-        nc.sync.dma_start(idx2[:], offs2)
         load_wm(0, 0)
+        nc.sync.dma_start(idx2[:], offs2)
         load_wm(0, 1)
-        for q in range(4):
-            nc.scalar.dma_start(
-                tab_s[32 * q : 32 * (q + 1) : 4, :].bitcast(I32), tab_scales[:, 4 * q : 4 * (q + 1), :].bitcast(I32))
-        nc.scalar.dma_start(tab2_s[64:P:4, :].bitcast(I32), tab2_scales[0].bitcast(I32))
+        nc.scalar.dma_start(
+            first[0:P:4, 0:T].bitcast(I32), tab_scales.rearrange("a q t -> (a q) t").bitcast(I32))
+        nc.scalar.dma_start(second[64:P:4, 0:T].bitcast(I32), tab2_scales[0].bitcast(I32))
         nc.scalar.activation(zero, zero_in[:], ACT.Sin)
+        load_tab(0)
         nc.gpsimd.dma_start(wr_s_raw[64:P:4, :].bitcast(I32), wr_scales[0].bitcast(I32))
         nc.gpsimd.dma_start(gain_sb[:], gain.rearrange("(b p t) -> p b t", b=2, t=PACK))
-        load_tab(0)
-        load_tab(1)
-        nc.sync.dma_start(tab2_w[:], tab2_words[0].bitcast(I32))
-        nc.sync.dma_start(wr_raw[:], wr_words[0].rearrange("p c i -> p (c i)").bitcast(I32))
 
         v_s = held([P, S], U8, "v_s")
         v2_s = held([P, S], U8, "v2_s")
-        nc.vector.tensor_copy(v_s[:], tab_s[:].indirect(idx[:]))
-        nc.vector.tensor_copy(v2_s[:], tab2_s[:].indirect(idx2[:]))
+        nc.vector.tensor_copy(v_s[:], tab_s.indirect(idx[:]))
+        nc.vector.tensor_copy(v2_s[:], tab2_s.indirect(idx2[:]))
         nc.vector.tensor_copy(stage_r[:, 0:S].bitcast(I32), v2_s[:].bitcast(I32))
         nc.vector.tensor_copy(
             stage_r[:, S:].rearrange("p (b t m) -> p b t m", b=2, t=PACK),
             wr_s_raw[:].rearrange("p (b m t) -> p b t m", b=2, t=PACK))
 
-        for q in range(4):
-            nc.scalar.dma_start(
-                plane_m[32 * q : 32 * q + 8, :].bitcast(I32), v_s[32 * q : 32 * (q + 1) : 4, :].bitcast(I32))
-        for r in range(4):
-            nc.gpsimd.dma_start(
-                plane_r[r:P:32, :].bitcast(I32), stage_r[64 + 4 * r : 64 + 4 * r + 49 : 16, :].bitcast(I32))
+        def move_rows(queue, plane, spread, first_row):
+            for r in range(4):
+                lo = first_row + 4 * r
+                queue.dma_start(plane[r:P:32, :].bitcast(I32), spread[lo : lo + 49 : 16, :].bitcast(I32))
 
-        v_w0 = placed([P, S], U32, "v_w0", at["wr_s"])
-        v_w1 = [held([P, NT], U32, "v_w1%d" % j) for j in range(2)]
+        move_rows(nc.sync, v_plane[0], v_s, 0)
+        load_tab(1)
+        move_rows(nc.sync, v_plane[1], v_s, 64)
+        move_rows(nc.gpsimd, plane_r, stage_r, 64)
+        nc.sync.dma_start(tab2_w[:], tab2_words[0].bitcast(I32))
+        nc.sync.dma_start(wr_raw[:], wr_words[0].rearrange("p c i -> p (c i)").bitcast(I32))
+        load_wm(1, 0)
+        load_wm(1, 1)
+        load_wn(0)
+        nc.sync.dma_start(wa_w[:].bitcast(I32), wa_words.bitcast(I32).rearrange("a p c -> p a c"))
+        load_wn(1)
+        for q in range(4):
+            nc.sync.dma_start(
+                wa_s[32 * q : 32 * q + 4, :, :].bitcast(I32),
+                wa_scales[:, 4 * q : 4 * q + 4, :].bitcast(I32).rearrange("a r n -> r a n"))
+        with nc.allow_non_contiguous_dma(reason="one drift value a partition"):
+            nc.sync.dma_start(drift_sb[:], drift.rearrange("(c p) -> p c", p=P))
+
+        v_w0 = placed([P, S], U32, "v_w0", at["wm_bf01"])
+        v_w1 = [placed([P, NT], U32, "v_w1%d" % j, at["tab0"] + 2 * KB * j) for j in range(2)]
         wr_c = placed([P, H], I32, "wr_c", at["tab1"])
         v2_w = [placed([P, 2 * NT], U8, "v2_w0", at["tab1"] + 4 * KB), placed([P, 2 * NT], U8, "v2_w1", at["wr"])]
         half = NT // 16
 
-        wm_bf = [[held([P, KP * PACK], BF16, "wm_bf00")[:],
-                  placed([P, (at["late_end"] - at["wm_bf01"]) // 2], BF16, "wm_bf01", at["wm_bf01"])[:, 0 : KP * PACK]],
+        wm_bf = [[held([P, KP * PACK], BF16, "wm_bf00")[:], placed([P, KP * PACK], BF16, "wm_bf01", at["wm_bf01"])[:]],
                  [placed([P, KP * PACK], BF16, "wm_bf10", at["wm_bf10"])[:]]]
         wm_bf11 = [placed([P, KP * 2], BF16, "wm_bf11_0", at["wn_bf0"]),
                    placed([P, KP * 2], BF16, "wm_bf11_1", at["wm_bf10"])]
         wm_c = [[placed([P, KP], U32, "wm_c00", at["tab2_s"]), placed([P, KP], U32, "wm_c01", at["tab2_s"] + 2 * KB)],
                 [held([P, KP], U32, "wm_c1%d" % a) for a in range(2)]]
-        wm_s = [[held([P, KP], U8, "wm_s%d%d" % (b, a)) for a in range(2)] for b in range(2)]
+        wm_s = [[placed([P, KP], U8, "wm_s0%d" % a, at["wr_s"] + KP * a) for a in range(2)],
+                [held([P, KP], U8, "wm_s1%d" % a) for a in range(2)]]
         wn_bf = [placed([P, N * PACK], BF16, "wn_bf%d" % b, at["wn_bf%d" % b]) for b in range(2)]
         wn_c = [held([P, N], U32, "wn_c%d" % b) for b in range(2)]
         wn_s = [held([P, N], U8, "wn_s%d" % b) for b in range(2)]
@@ -198,7 +208,7 @@ def tile_list_attitude_propagation_kernel(
             cols = slice(P * t, P * (t + 1))
             nc.tensor.matmul_mx(
                 phases[b, j, t][:], lhsT=wm_c[b][a][:, cols].bitcast(FP8X4), lhsT_scale=wm_s[b][a][:, cols],
-                rhs=v_words(a, j), rhs_scale=plane_m[4 * a : P, NT * j : NT * (j + 1)],
+                rhs=v_words(a, j), rhs_scale=v_plane[a][:, NT * j : NT * (j + 1)],
                 start=(a == 0), stop=(a == 1))
 
         def open_phase(b, j, t, n):
@@ -229,7 +239,7 @@ def tile_list_attitude_propagation_kernel(
                 nc.tensor.matmul_mx(
                     acc[j, c][:], lhsT=wa_w[:, a, 2 * P * c : 2 * P * (c + 1)].bitcast(FP4X4),
                     lhsT_scale=wa_s[:, a, P * c : P * (c + 1)],
-                    rhs=v_words(a, j), rhs_scale=wa_plane[a][:, NT * j : NT * (j + 1)],
+                    rhs=v_words(a, j), rhs_scale=v_plane[a][:, NT * j : NT * (j + 1)],
                     start=(a == 0), stop=False)
 
         def add_h(b, j, c):
@@ -239,7 +249,7 @@ def tile_list_attitude_propagation_kernel(
                 rhs=h_c[b][j][:].bitcast(FP8X4), rhs_scale=h_s[b][j][:], start=False, stop=(b == 1))
 
         def finish(j, c):
-            res = placed([P, NT], F32, "res%d%d" % (j, c), at["tab0"] + 2 * KB * (4 * j + c))
+            res = placed([P, NT], F32, "res%d%d" % (j, c), at["wm10"] + 2 * KB * (4 * j + c))
             if j == 1 and c % 2 == 0:
                 nc.vector.tensor_scalar(res[:], acc[j, c][:], drift_sb[:, c : c + 1], None, ALU.add)
             else:
@@ -255,13 +265,13 @@ def tile_list_attitude_propagation_kernel(
                     nc.tensor.matmul_mx(
                         total, lhsT=wa_w[:, a, 2 * P * c : 2 * P * (c + 1)].bitcast(FP4X4),
                         lhsT_scale=wa_s[:, a, P * c : P * (c + 1)], rhs=v_words(a, j)[:, lo : lo + NH],
-                        rhs_scale=wa_plane[a][:, NT * j + lo : NT * j + lo + NH], start=(a == 0), stop=False)
+                        rhs_scale=v_plane[a][:, NT * j + lo : NT * j + lo + NH], start=(a == 0), stop=False)
                 for b in range(2):
                     nc.tensor.matmul_mx(
                         total, lhsT=wn_c[b][:, cols].bitcast(FP8X4), lhsT_scale=wn_s[b][:, cols],
                         rhs=h_c[b][j][:, lo : lo + NH].bitcast(FP8X4), rhs_scale=h_s[b][j][:, lo : lo + NH],
                         start=False, stop=(b == 1))
-                res = placed([P, NH], F32, "res_half%d" % side, at["tab0"] + 2 * KB * (4 * j + c) + KB * side)
+                res = placed([P, NH], F32, "res_half%d" % side, at["wm10"] + 2 * KB * (4 * j + c) + KB * side)
                 if side == 0:
                     nc.scalar.activation(res[:], total, ACT.Identity, bias=drift_sb[:, c : c + 1])
                 else:
@@ -277,19 +287,6 @@ def tile_list_attitude_propagation_kernel(
         for a in range(2):
             quant_wm(0, a)
         nc.vector.tensor_copy(v_w0[:], tab_w[0][:].bitcast(U32).indirect(idx[:]))
-        load_wm(1, 0)
-        load_wm(1, 1)
-        load_wn(0)
-        nc.sync.dma_start(wa_w[:].bitcast(I32), wa_words.bitcast(I32).rearrange("a p c -> p a c"))
-        for r in range(4):
-            nc.sync.dma_start(plane_w[r:P:32, :].bitcast(I32), v_s[16 + 4 * r : P : 32, :].bitcast(I32))
-        load_wn(1)
-        for q in range(4):
-            nc.sync.dma_start(
-                wa_s[32 * q : 32 * q + 4, :, :].bitcast(I32),
-                wa_scales[:, 4 * q : 4 * q + 4, :].bitcast(I32).rearrange("a r n -> r a n"))
-        with nc.allow_non_contiguous_dma(reason="one drift value a partition"):
-            nc.sync.dma_start(drift_sb[:], drift.rearrange("(c p) -> p c", p=P))
         for j in range(2):
             nc.vector.tensor_copy(
                 v_w1[j][:], tab_w[1][:].bitcast(U32).indirect(idx[:, half * j : half * (j + 1)]))

@@ -49,29 +49,31 @@ def tile_list_attitude_propagation_kernel(
         end = 0
         for name, size in (
             ("tab_s", 4 * KB), ("tab1", 16 * KB), ("first_end", 0),
-            ("tab2_s", 4 * KB), ("tab2", 8 * KB), ("wr", 4 * KB), ("wm10", 8 * KB), ("wm11", 8 * KB),
+            ("wr_s", KB), ("tab2", 8 * KB), ("wr", 4 * KB), ("wm10", 8 * KB), ("wm11", 8 * KB),
             ("wn0", 8 * KB), ("wa", 2 * KB), ("wa_s", 2 * N), ("wn1", 8 * KB), ("drift", 64), ("late_end", 0),
-            ("tab0", 16 * KB), ("wr_s", KB), ("wm_bf01", 4 * KB), ("sine0", 8 * KB), ("sine1", 8 * KB),
-            ("wm_bf10", 4 * KB), ("h_bf00", 4 * KB), ("wn_bf0", 4 * KB), ("wn_bf1", 4 * KB), ("h_bf01", 4 * KB),
+            ("wm01", 8 * KB), ("tab0", 16 * KB), ("tab2_s", 4 * KB), ("wm_bf01", 4 * KB), ("sine0", 8 * KB), ("sine1", 8 * KB),
+            ("wm_bf10", 4 * KB), ("h_bf00", 4 * KB), ("wn_bf0", 4 * KB), ("wn_bf1", 4 * KB),
         ):
             at[name] = end
             end = end + size
 
         first = placed([P, at["first_end"]], U8, "first", 0)
-        second = placed([P, at["late_end"] - at["tab2_s"]], U8, "second", at["tab2_s"])
+        second = placed([P, at["late_end"] - at["wr_s"]], U8, "second", at["wr_s"])
         tab_s = first[:, 0:T]
-        tab2_s = second[:, 0:T]
-        wr_s_raw = placed([P, H], U8, "wr_s_raw", at["wr_s"])
+        tab2_s = placed([P, T], U8, "tab2_s", at["tab2_s"])[:]
+        wr_s_raw = second[:, 0:H]
         zero_in = held([P, 1], F32, "zero_in")
         zero = placed([P, (at["wn_bf0"] - at["wm_bf10"]) // 4 + 16], F32, "zero", at["wm_bf10"])[:, 0:1]
-        zero_late = placed([P, 32], F32, "zero_late", at["h_bf01"] - 64)[:, 0:1]
-        nc.gpsimd.memset(wr_s_raw[:].bitcast(I32), 0)
+        zero_late = placed([P, 1], F32, "zero_late", at["wn_bf1"])[:]
+        nc.gpsimd.memset(wr_s_raw.bitcast(I32), 0)
         nc.vector.memset(tab_s.bitcast(I32), 0)
         nc.vector.memset(tab2_s.bitcast(I32), 0)
-        nc.vector.memset(zero_in[:], 0.0)
+        zero_src = placed([P, 32], F32, "zero_src", at["tab0"] - 64)
+        nc.vector.memset(zero_src[:, 0:1], 0.0)
+        nc.vector.tensor_copy(zero_in[:], zero_src[:, 0:1])
         nc.vector.memset(zero_late, 0.0)
 
-        wm_raw = [[held([P, PACK, KP], F32, "wm_raw0%d" % a) for a in range(2)],
+        wm_raw = [[held([P, PACK, KP], F32, "wm_raw00"), placed([P, PACK, KP], F32, "wm_raw01", at["wm01"])],
                   [placed([P, PACK, KP], F32, "wm_raw1%d" % a, at["wm1%d" % a]) for a in range(2)]]
         tab_w = [placed([P, T], I32, "tab_w%d" % a, at["tab%d" % a]) for a in range(2)]
         tab2_w = placed([P, T // 2], I32, "tab2_w", at["tab2"])
@@ -80,12 +82,13 @@ def tile_list_attitude_propagation_kernel(
         wa_w = placed([P, 2, 2 * N], U8, "wa_w", at["wa"])
         gain_sb = held([P, 2, PACK], F32, "gain_sb")
         drift_sb = placed([P, N // P], F32, "drift_sb", at["drift"])
-        stage_r = held([P, S + H], U8, "stage_r")
-        v_plane = [held([P, S], U8, "v_plane%d" % a) for a in range(2)]
-        plane_r = held([P, S + H], U8, "plane_r")
+        stage = held([P, 2 * S + H], U8, "stage")
+        plane_a = held([P, S], U8, "plane_a")
+        plane_b = held([P, 2 * S + H], U8, "plane_b")
+        v_plane = [plane_a[:], plane_b[:, 0:S]]
         wa_s = placed([P, 2, N], U8, "wa_s", at["wa_s"])
-        v2_plane = plane_r[:, 0:S]
-        wr_s = plane_r[:, S:]
+        v2_plane = plane_b[:, S : 2 * S]
+        wr_s = plane_b[:, 2 * S :]
 
         def load_wm(b, a):
             rows = wm[KP * a : KP * (a + 1), KP * b : KP * (b + 1)]
@@ -101,33 +104,33 @@ def tile_list_attitude_propagation_kernel(
         nc.sync.dma_start(idx[:], offs)
         load_wm(0, 0)
         nc.sync.dma_start(idx2[:], offs2)
-        load_wm(0, 1)
-        nc.scalar.dma_start(
+        nc.sync.dma_start(
             first[0:P:4, 0:T].bitcast(I32), tab_scales.rearrange("a q t -> (a q) t").bitcast(I32))
-        nc.scalar.dma_start(second[64:P:4, 0:T].bitcast(I32), tab2_scales[0].bitcast(I32))
+        nc.sync.dma_start(tab2_s[64:P:4, :].bitcast(I32), tab2_scales[0].bitcast(I32))
         nc.scalar.activation(zero, zero_in[:], ACT.Sin)
-        load_tab(0)
-        nc.gpsimd.dma_start(wr_s_raw[64:P:4, :].bitcast(I32), wr_scales[0].bitcast(I32))
+        nc.sync.dma_start(second[64:P:4, 0:H].bitcast(I32), wr_scales[0].bitcast(I32))
         nc.gpsimd.dma_start(gain_sb[:], gain.rearrange("(b p t) -> p b t", b=2, t=PACK))
 
+        load_wm(0, 1)
+        load_tab(0)
         v_s = held([P, S], U8, "v_s")
         v2_s = held([P, S], U8, "v2_s")
         nc.vector.tensor_copy(v_s[:], tab_s.indirect(idx[:]))
         nc.vector.tensor_copy(v2_s[:], tab2_s.indirect(idx2[:]))
-        nc.vector.tensor_copy(stage_r[:, 0:S].bitcast(I32), v2_s[:].bitcast(I32))
+        nc.vector.tensor_copy(stage[:, 0:S].bitcast(I32), v_s[:].bitcast(I32))
+        nc.vector.tensor_copy(stage[:, S : 2 * S].bitcast(I32), v2_s[:].bitcast(I32))
         nc.vector.tensor_copy(
-            stage_r[:, S:].rearrange("p (b t m) -> p b t m", b=2, t=PACK),
-            wr_s_raw[:].rearrange("p (b m t) -> p b t m", b=2, t=PACK))
+            stage[:, 2 * S :].rearrange("p (b t m) -> p b t m", b=2, t=PACK),
+            wr_s_raw.rearrange("p (b m t) -> p b t m", b=2, t=PACK))
 
-        def move_rows(queue, plane, spread, first_row):
+        def move_rows(plane, spread, first_row):
             for r in range(4):
                 lo = first_row + 4 * r
-                queue.dma_start(plane[r:P:32, :].bitcast(I32), spread[lo : lo + 49 : 16, :].bitcast(I32))
+                nc.sync.dma_start(plane[r:P:32, :].bitcast(I32), spread[lo : lo + 49 : 16, :].bitcast(I32))
 
-        move_rows(nc.sync, v_plane[0], v_s, 0)
+        move_rows(plane_a, v_s, 0)
         load_tab(1)
-        move_rows(nc.sync, v_plane[1], v_s, 64)
-        move_rows(nc.gpsimd, plane_r, stage_r, 64)
+        move_rows(plane_b, stage, 64)
         nc.sync.dma_start(tab2_w[:], tab2_words[0].bitcast(I32))
         nc.sync.dma_start(wr_raw[:], wr_words[0].rearrange("p c i -> p (c i)").bitcast(I32))
         load_wm(1, 0)
@@ -142,7 +145,7 @@ def tile_list_attitude_propagation_kernel(
         with nc.allow_non_contiguous_dma(reason="one drift value a partition"):
             nc.sync.dma_start(drift_sb[:], drift.rearrange("(c p) -> p c", p=P))
 
-        v_w0 = placed([P, S], U32, "v_w0", at["wm_bf01"])
+        v_w0 = [placed([P, NT], U32, "v_w0%d" % j, at["wm_bf01"] + 2 * KB * j) for j in range(2)]
         v_w1 = [placed([P, NT], U32, "v_w1%d" % j, at["tab0"] + 2 * KB * j) for j in range(2)]
         wr_c = placed([P, H], I32, "wr_c", at["tab1"])
         v2_w = [placed([P, 2 * NT], U8, "v2_w0", at["tab1"] + 4 * KB), placed([P, 2 * NT], U8, "v2_w1", at["wr"])]
@@ -162,7 +165,7 @@ def tile_list_attitude_propagation_kernel(
         h_c = [[held([P, NT], U32, "h_c%d%d" % (b, j)) for j in range(2)] for b in range(2)]
         h_s = [[held([P, NT], U8, "h_s%d%d" % (b, j)) for j in range(2)] for b in range(2)]
         planes = [[held([P, PACK, NT], BF16, "h_planes%d%d" % (b, j)) for j in range(2)] for b in range(2)]
-        woven = [[placed([P, NT * PACK], BF16, "h_bf0%d" % j, at["h_bf0%d" % j]) for j in range(2)],
+        woven = [[placed([P, NT * PACK], BF16, "h_bf00", at["h_bf00"]), placed([P, NT * PACK], BF16, "h_bf01", at["wn1"])],
                  [held([P, NT * PACK], BF16, "h_bf1%d" % j) for j in range(2)]]
 
         def cast_wm(b, a, copy):
@@ -194,7 +197,7 @@ def tile_list_attitude_propagation_kernel(
             nc.vector.quantize_mx(h_c[b][j][:].bitcast(FP8X4), h_s[b][j][:], woven[b][j][:])
 
         def v_words(a, j):
-            return (v_w0[:, NT * j : NT * (j + 1)] if a == 0 else v_w1[j][:]).bitcast(FP8X4)
+            return (v_w0, v_w1)[a][j][:].bitcast(FP8X4)
 
         def bank(n, name):
             return psum.tile([P, NT], F32, name=name, tag="bank%d" % n)
@@ -286,10 +289,10 @@ def tile_list_attitude_propagation_kernel(
             cast_wm(0, a, nc.scalar.copy)
         for a in range(2):
             quant_wm(0, a)
-        nc.vector.tensor_copy(v_w0[:], tab_w[0][:].bitcast(U32).indirect(idx[:]))
-        for j in range(2):
-            nc.vector.tensor_copy(
-                v_w1[j][:], tab_w[1][:].bitcast(U32).indirect(idx[:, half * j : half * (j + 1)]))
+        for a in range(2):
+            for j in range(2):
+                nc.vector.tensor_copy(
+                    (v_w0, v_w1)[a][j][:], tab_w[a][:].bitcast(U32).indirect(idx[:, half * j : half * (j + 1)]))
         gather_v2(0)
         nc.vector.tensor_copy(
             wr_c[:].rearrange("p (b t u i) -> p b u t i", b=2, t=PACK, i=4),

@@ -22,8 +22,10 @@ KP = P * PACK
 NT = 512
 NH = NT // 2
 KB = 1024
-RATE_BANKS = (0, 1, 4, 5)
-PHASE_BANKS = (2, 3, 6, 7)
+GPSIMD_FIRST = 320
+GPSIMD_SHARE = 384
+RATE_BANKS = (0, 4, 5, 6)
+PHASE_BANKS = (1, 2, 3, 7)
 
 
 def tile_list_attitude_propagation_kernel(
@@ -163,10 +165,11 @@ def tile_list_attitude_propagation_kernel(
         wn_c = [held([P, N], U32, "wn_c%d" % b) for b in range(2)]
         wn_s = [held([P, N], U8, "wn_s%d" % b) for b in range(2)]
         h_c = [[held([P, NT], U32, "h_c%d%d" % (b, j)) for j in range(2)] for b in range(2)]
-        h_s = [[held([P, NT], U8, "h_s%d%d" % (b, j)) for j in range(2)] for b in range(2)]
+        h_s = [[placed([P, NT], U8, "h_s00", at["wm_bf10"]), held([P, NT], U8, "h_s01")],
+               [held([P, NT], U8, "h_s1%d" % j) for j in range(2)]]
         planes = [[held([P, PACK, NT], BF16, "h_planes%d%d" % (b, j)) for j in range(2)] for b in range(2)]
         woven = [[placed([P, NT * PACK], BF16, "h_bf00", at["h_bf00"]), placed([P, NT * PACK], BF16, "h_bf01", at["wn1"])],
-                 [held([P, NT * PACK], BF16, "h_bf1%d" % j) for j in range(2)]]
+                 [placed([P, NT * PACK], BF16, "h_bf10", at["wn_bf0"]), held([P, NT * PACK], BF16, "h_bf11")]]
 
         def cast_wm(b, a, copy):
             copy(
@@ -189,6 +192,11 @@ def tile_list_attitude_propagation_kernel(
             copy(
                 dst[:, PACK * lo : PACK * hi].rearrange("p (u i t) -> p u t i", i=4, t=PACK),
                 src[:, :, lo:hi].rearrange("p t (u i) -> p u t i", i=4))
+
+        def interleave_on_gpsimd(dst, src, lo, hi):
+            nc.gpsimd.tensor_scalar(
+                dst[:, PACK * lo : PACK * hi].rearrange("p (n t) -> p n t", t=PACK),
+                src[:, :, lo:hi].rearrange("p t n -> p n t"), 1.0, 0.0, ALU.mult, ALU.add)
 
         def quant_wn(b):
             nc.vector.quantize_mx(wn_c[b][:].bitcast(FP8X4), wn_s[b][:], wn_bf[b][:])
@@ -317,7 +325,8 @@ def tile_list_attitude_propagation_kernel(
         quant_last_wm(0)
         cast_last_wm(1, nc.vector.tensor_copy)
         quant_last_wm(1)
-        interleave(nc.scalar.copy, woven[0][0], planes[0][0], 0, NT)
+        interleave_on_gpsimd(woven[0][0], planes[0][0], 0, GPSIMD_FIRST)
+        interleave(nc.scalar.copy, woven[0][0], planes[0][0], GPSIMD_FIRST, NT)
         interleave(nc.vector.tensor_copy, wn_bf[0], wn_raw[0], 0, N)
         for t in range(PACK):
             open_phase(1, 0, t, PHASE_BANKS[t])
@@ -333,9 +342,10 @@ def tile_list_attitude_propagation_kernel(
         for t in range(PACK):
             old_rate(1, 1, t, RATE_BANKS[t])
             new_rate(1, 1, t)
+        interleave_on_gpsimd(woven[1][0], planes[1][0], 0, GPSIMD_SHARE)
         interleave(nc.scalar.copy, wn_bf[1], wn_raw[1], 0, N)
+        interleave(nc.scalar.copy, woven[1][0], planes[1][0], GPSIMD_SHARE, NT)
         interleave(nc.scalar.copy, woven[0][1], planes[0][1], 0, NT)
-        interleave(nc.vector.tensor_copy, woven[1][0], planes[1][0], 0, NT)
         quant_wn(1)
         quant_h(1, 0)
         interleave(nc.vector.tensor_copy, woven[1][1], planes[1][1], 0, NT)

@@ -84,13 +84,12 @@ def tile_list_attitude_propagation_kernel(
         wa_w = placed([P, 2, 2 * N], U8, "wa_w", at["wa"])
         gain_sb = held([P, 2, PACK], F32, "gain_sb")
         drift_sb = placed([P, N // P], F32, "drift_sb", at["drift"])
-        stage = held([P, 2 * S + H], U8, "stage")
-        plane_a = held([P, S], U8, "plane_a")
-        plane_b = held([P, 2 * S + H], U8, "plane_b")
-        v_plane = [plane_a[:], plane_b[:, 0:S]]
+        stage = held([P, S + H], U8, "stage")
+        v_plane = [held([P, S], U8, "v_plane%d" % a) for a in range(2)]
+        plane_r = held([P, S + H], U8, "plane_r")
         wa_s = placed([P, 2, N], U8, "wa_s", at["wa_s"])
-        v2_plane = plane_b[:, S : 2 * S]
-        wr_s = plane_b[:, 2 * S :]
+        v2_plane = plane_r[:, 0:S]
+        wr_s = plane_r[:, S:]
 
         def load_wm(b, a):
             rows = wm[KP * a : KP * (a + 1), KP * b : KP * (b + 1)]
@@ -103,8 +102,8 @@ def tile_list_attitude_propagation_kernel(
         def load_tab(a):
             nc.sync.dma_start(tab_w[a][:], tab_words[a].rearrange("p t i -> p (t i)").bitcast(I32))
 
-        nc.sync.dma_start(idx[:], offs)
         load_wm(0, 0)
+        nc.sync.dma_start(idx[:], offs)
         nc.sync.dma_start(idx2[:], offs2)
         nc.sync.dma_start(
             first[0:P:4, 0:T].bitcast(I32), tab_scales.rearrange("a q t -> (a q) t").bitcast(I32))
@@ -119,10 +118,9 @@ def tile_list_attitude_propagation_kernel(
         v2_s = held([P, S], U8, "v2_s")
         nc.vector.tensor_copy(v_s[:], tab_s.indirect(idx[:]))
         nc.vector.tensor_copy(v2_s[:], tab2_s.indirect(idx2[:]))
-        nc.vector.tensor_copy(stage[:, 0:S].bitcast(I32), v_s[:].bitcast(I32))
-        nc.vector.tensor_copy(stage[:, S : 2 * S].bitcast(I32), v2_s[:].bitcast(I32))
+        nc.vector.tensor_copy(stage[:, 0:S].bitcast(I32), v2_s[:].bitcast(I32))
         nc.vector.tensor_copy(
-            stage[:, 2 * S :].rearrange("p (b t m) -> p b t m", b=2, t=PACK),
+            stage[:, S:].rearrange("p (b t m) -> p b t m", b=2, t=PACK),
             wr_s_raw.rearrange("p (b m t) -> p b t m", b=2, t=PACK))
 
         def move_rows(plane, spread, first_row):
@@ -130,11 +128,12 @@ def tile_list_attitude_propagation_kernel(
                 lo = first_row + 4 * r
                 nc.sync.dma_start(plane[r:P:32, :].bitcast(I32), spread[lo : lo + 49 : 16, :].bitcast(I32))
 
-        move_rows(plane_a, v_s, 0)
+        move_rows(v_plane[0], v_s, 0)
         load_tab(1)
-        move_rows(plane_b, stage, 64)
+        move_rows(v_plane[1], v_s, 64)
         nc.sync.dma_start(tab2_w[:], tab2_words[0].bitcast(I32))
         nc.sync.dma_start(wr_raw[:], wr_words[0].rearrange("p c i -> p (c i)").bitcast(I32))
+        move_rows(plane_r, stage, 64)
         load_wm(1, 0)
         load_wm(1, 1)
         load_wn(0)

@@ -164,11 +164,14 @@ def tile_list_attitude_propagation_kernel(
         wn_c = [held([P, N], U32, "wn_c%d" % b) for b in range(2)]
         wn_s = [held([P, N], U8, "wn_s%d" % b) for b in range(2)]
         h_c = [[held([P, NT], U32, "h_c%d%d" % (b, j)) for j in range(2)] for b in range(2)]
-        h_s = [[placed([P, NT], U8, "h_s00", at["wm_bf10"]), held([P, NT], U8, "h_s01")],
+        h_s = [[placed([P, NT], U8, "h_s00", at["wm_bf10"]), placed([P, NT], U8, "h_s01", at["sine1"] + 6 * KB)],
                [held([P, NT], U8, "h_s1%d" % j) for j in range(2)]]
         planes = [[held([P, PACK, NT], BF16, "h_planes%d%d" % (b, j)) for j in range(2)] for b in range(2)]
-        woven = [[placed([P, NT * PACK], BF16, "h_bf00", at["h_bf00"]), placed([P, NT * PACK], BF16, "h_bf01", at["wn1"])],
+        woven = [[placed([P, NT * PACK], BF16, "h_bf00", at["h_bf00"]), None],
                  [placed([P, NT * PACK], BF16, "h_bf10", at["wn_bf0"]), held([P, NT * PACK], BF16, "h_bf11")]]
+
+        woven01 = [placed([P, GPSIMD_SHARE * PACK], BF16, "h_bf01_0", at["wn0"]),
+                   placed([P, (NT - GPSIMD_SHARE) * PACK], BF16, "h_bf01_1", at["wn1"])]
 
         def cast_wm(b, a, copy):
             copy(
@@ -196,6 +199,9 @@ def tile_list_attitude_propagation_kernel(
             nc.gpsimd.tensor_scalar(
                 dst[:, PACK * lo : PACK * hi].rearrange("p (n t) -> p n t", t=PACK),
                 src[:, :, lo:hi].rearrange("p t n -> p n t"), 1.0, 0.0, ALU.mult, ALU.add)
+
+        def quant_h_part(b, j, part, lo, hi):
+            nc.vector.quantize_mx(h_c[b][j][:, lo:hi].bitcast(FP8X4), h_s[b][j][:, lo:hi], part[:])
 
         def quant_wn(b):
             nc.vector.quantize_mx(wn_c[b][:].bitcast(FP8X4), wn_s[b][:], wn_bf[b][:])
@@ -327,6 +333,7 @@ def tile_list_attitude_propagation_kernel(
         interleave_on_gpsimd(woven[0][0], planes[0][0], 0, GPSIMD_FIRST)
         interleave(nc.scalar.copy, woven[0][0], planes[0][0], GPSIMD_FIRST, NT)
         interleave(nc.vector.tensor_copy, wn_bf[0], wn_raw[0], 0, N)
+        interleave_on_gpsimd(woven01[0], planes[0][1], 0, GPSIMD_SHARE)
         for t in range(PACK):
             open_phase(1, 0, t, PHASE_BANKS[t])
         for t in range(PACK):
@@ -344,23 +351,26 @@ def tile_list_attitude_propagation_kernel(
         interleave_on_gpsimd(woven[1][0], planes[1][0], 0, GPSIMD_SHARE)
         interleave(nc.scalar.copy, wn_bf[1], wn_raw[1], 0, N)
         interleave(nc.scalar.copy, woven[1][0], planes[1][0], GPSIMD_SHARE, NT)
-        interleave(nc.scalar.copy, woven[0][1], planes[0][1], 0, NT)
+        interleave(nc.scalar.copy, woven01[1], planes[0][1][:, :, GPSIMD_SHARE:NT], 0, NT - GPSIMD_SHARE)
         quant_wn(1)
         quant_h(1, 0)
+        quant_h_part(0, 1, woven01[0], 0, GPSIMD_SHARE)
+        quant_h_part(0, 1, woven01[1], GPSIMD_SHARE, NT)
         interleave(nc.vector.tensor_copy, woven[1][1], planes[1][1], 0, NT)
-        quant_h(0, 1)
         quant_h(1, 1)
         for c in range(4):
             open_angle(0, c, PHASE_BANKS[c])
         for c in range(4):
             add_h(0, 0, c)
-        for c in range(3):
-            open_angle(1, c, RATE_BANKS[c])
+        open_angle(1, 0, RATE_BANKS[0])
         for c in range(4):
             add_h(1, 0, c)
             finish(0, c)
-        for c in range(3):
+        open_angle(1, 1, RATE_BANKS[1])
+        for c in range(2):
             add_h(0, 1, c)
+        open_angle(1, 2, RATE_BANKS[2])
+        add_h(0, 1, 2)
         for c in range(3):
             add_h(1, 1, c)
             finish(1, c)

@@ -80,7 +80,7 @@ def tile_list_attitude_propagation_kernel(
         tab_w = [placed([P, T], I32, "tab_w%d" % a, at["tab%d" % a]) for a in range(2)]
         tab2_w = placed([P, T // 2], I32, "tab2_w", at["tab2"])
         wn_raw = [placed([P, PACK, N], F32, "wn_raw%d" % b, at["wn%d" % b]) for b in range(2)]
-        wr_raw = placed([P, H], I32, "wr_raw", at["wr"])
+        wr_raw = [placed([P, KP], I32, "wr_raw%d" % b, at["wr"] + 2 * KB * b)[:] for b in range(2)]
         wa_w = placed([P, 2, 2 * N], U8, "wa_w", at["wa"])
         gain_sb = held([P, 2, PACK], F32, "gain_sb")
         drift_sb = placed([P, N // P], F32, "drift_sb", at["drift"])
@@ -98,6 +98,10 @@ def tile_list_attitude_propagation_kernel(
         def load_wn(b):
             rows = wn[KP * b : KP * (b + 1), :]
             nc.sync.dma_start(wn_raw[b][:], rows.rearrange("(p t) n -> p t n", t=PACK))
+
+        def load_wr(b):
+            words = wr_words[0][:, KP * b : KP * (b + 1), :]
+            nc.sync.dma_start(wr_raw[b], words.rearrange("p c i -> p (c i)").bitcast(I32))
 
         def load_tab(a):
             nc.sync.dma_start(tab_w[a][:], tab_words[a].rearrange("p t i -> p (t i)").bitcast(I32))
@@ -132,8 +136,9 @@ def tile_list_attitude_propagation_kernel(
         load_tab(1)
         move_rows(v_plane[1], v_s, 64)
         nc.sync.dma_start(tab2_w[:], tab2_words[0].bitcast(I32))
-        nc.sync.dma_start(wr_raw[:], wr_words[0].rearrange("p c i -> p (c i)").bitcast(I32))
         move_rows(plane_r, stage, 64)
+        load_wr(0)
+        load_wr(1)
         load_wm(1, 0)
         load_wm(1, 1)
         load_wn(0)
@@ -148,7 +153,7 @@ def tile_list_attitude_propagation_kernel(
 
         v_w0 = [placed([P, NT], U32, "v_w0%d" % j, at["wm_bf01"] + 2 * KB * j) for j in range(2)]
         v_w1 = [placed([P, NT], U32, "v_w1%d" % j, at["tab0"] + 2 * KB * j) for j in range(2)]
-        wr_c = placed([P, H], I32, "wr_c", at["tab1"])
+        wr_c = [placed([P, KP], I32, "wr_c0", at["tab1"]), placed([P, KP], I32, "wr_c1", at["tab2"])]
         v2_w = [placed([P, 2 * NT], U8, "v2_w0", at["tab1"] + 4 * KB), placed([P, 2 * NT], U8, "v2_w1", at["wr"])]
         half = NT // 16
 
@@ -241,7 +246,7 @@ def tile_list_attitude_propagation_kernel(
             rates[b, j, t] = bank(n, "rate")
             cols = slice(KP * b + P * t, KP * b + P * (t + 1))
             nc.tensor.matmul_mx(
-                rates[b, j, t][:], lhsT=wr_c[:, cols].bitcast(FP8X4), lhsT_scale=wr_s[:, cols],
+                rates[b, j, t][:], lhsT=wr_c[b][:, P * t : P * (t + 1)].bitcast(FP8X4), lhsT_scale=wr_s[:, cols],
                 rhs=v2_w[j][:].bitcast(FP4X4), rhs_scale=v2_plane[:, NT * j : NT * (j + 1)], start=True, stop=True)
 
         def new_rate(b, j, t):
@@ -308,9 +313,11 @@ def tile_list_attitude_propagation_kernel(
                     (v_w0, v_w1)[a][j][:], tab_w[a][:].bitcast(U32).indirect(idx[:, half * j : half * (j + 1)]))
         gather_v2(0)
         nc.vector.tensor_copy(
-            wr_c[:].rearrange("p (b t u i) -> p b u t i", b=2, t=PACK, i=4),
-            wr_raw[:].rearrange("p (b u i t) -> p b u t i", b=2, t=PACK, i=4))
+            wr_c[0][:].rearrange("p (t u i) -> p u t i", t=PACK, i=4),
+            wr_raw[0].rearrange("p (u i t) -> p u t i", t=PACK, i=4))
         gather_v2(1)
+        nc.gpsimd.tensor_copy(
+            wr_c[1][:].rearrange("p (t m) -> p t m", t=PACK), wr_raw[1].rearrange("p (m t) -> p t m", t=PACK))
 
         for j in range(2):
             for t in range(PACK):

@@ -359,11 +359,12 @@ def tile_list_attitude_propagation_kernel(
         interleave(nc.scalar.copy, wn_bf[1], wn_raw[1], 0, N)
         interleave(nc.scalar.copy, woven[1][0], planes[1][0], GPSIMD_SHARE, NT)
         interleave(nc.scalar.copy, woven01[1], planes[0][1][:, :, GPSIMD_SHARE:NT], 0, NT - GPSIMD_SHARE)
+        interleave(nc.scalar.copy, woven[1][1], planes[1][1], GPSIMD_SHARE, NT)
         quant_wn(1)
         quant_h(1, 0)
         quant_h_part(0, 1, woven01[0], 0, GPSIMD_SHARE)
         quant_h_part(0, 1, woven01[1], GPSIMD_SHARE, NT)
-        interleave(nc.vector.tensor_copy, woven[1][1], planes[1][1], 0, NT)
+        interleave(nc.vector.tensor_copy, woven[1][1], planes[1][1], 0, GPSIMD_SHARE)
         quant_h(1, 1)
         for c in range(4):
             open_angle(0, c, PHASE_BANKS[c])
@@ -373,12 +374,10 @@ def tile_list_attitude_propagation_kernel(
         for c in range(4):
             add_h(1, 0, c)
             finish(0, c)
-        open_angle(1, 1, RATE_BANKS[1])
-        for c in range(2):
-            add_h(0, 1, c)
-        open_angle(1, 2, RATE_BANKS[2])
-        add_h(0, 1, 2)
+        for c in range(1, 3):
+            open_angle(1, c, RATE_BANKS[c])
         for c in range(3):
+            add_h(0, 1, c)
             add_h(1, 1, c)
             finish(1, c)
         close_in_halves(1, 3, (RATE_BANKS[3], PHASE_BANKS[0]))

@@ -22,7 +22,7 @@ KP = P * PACK
 NT = 512
 NH = NT // 2
 KB = 1024
-GPSIMD_FIRST = 320
+GPSIMD_FIRST = 384
 GPSIMD_SHARE = 384
 RATE_BANKS = (0, 4, 5, 6)
 PHASE_BANKS = (1, 2, 3, 7)
@@ -51,9 +51,9 @@ def tile_list_attitude_propagation_kernel(
         end = 0
         for name, size in (
             ("tab_s", 4 * KB), ("tab1", 16 * KB), ("first_end", 0),
-            ("wr_s", KB), ("tab2", 8 * KB), ("wr", 4 * KB), ("wm10", 8 * KB), ("wm11", 8 * KB),
+            ("wr_s", KB), ("tab2", 8 * KB), ("sine1", 8 * KB), ("wr1", 2 * KB), ("wm10", 8 * KB), ("wm11", 8 * KB),
             ("wn0", 8 * KB), ("wa", 2 * KB), ("wa_s", 2 * N), ("wn1", 8 * KB), ("drift", 64), ("late_end", 0),
-            ("wm01", 8 * KB), ("tab0", 16 * KB), ("tab2_s", 4 * KB), ("wm_bf01", 4 * KB), ("sine0", 8 * KB), ("sine1", 8 * KB),
+            ("wm01", 8 * KB), ("tab0", 16 * KB), ("tab2_s", 4 * KB), ("wm_bf01", 4 * KB), ("sine0", 8 * KB),
             ("wm_bf10", 4 * KB), ("h_bf00", 4 * KB), ("wn_bf0", 4 * KB), ("wn_bf1", 4 * KB),
         ):
             at[name] = end
@@ -80,7 +80,7 @@ def tile_list_attitude_propagation_kernel(
         tab_w = [placed([P, T], I32, "tab_w%d" % a, at["tab%d" % a]) for a in range(2)]
         tab2_w = placed([P, T // 2], I32, "tab2_w", at["tab2"])
         wn_raw = [placed([P, PACK, N], F32, "wn_raw%d" % b, at["wn%d" % b]) for b in range(2)]
-        wr_raw = [placed([P, KP], I32, "wr_raw%d" % b, at["wr"] + 2 * KB * b)[:] for b in range(2)]
+        wr_raw = [placed([P, PACK * KP], I32, "wr_raw0", at["sine1"])[:, 0:KP], placed([P, KP], I32, "wr_raw1", at["wr1"])[:]]
         wa_w = placed([P, 2, 2 * N], U8, "wa_w", at["wa"])
         gain_sb = held([P, 2, PACK], F32, "gain_sb")
         drift_sb = placed([P, N // P], F32, "drift_sb", at["drift"])
@@ -153,8 +153,8 @@ def tile_list_attitude_propagation_kernel(
 
         v_w0 = [placed([P, NT], U32, "v_w0%d" % j, at["wm_bf01"] + 2 * KB * j) for j in range(2)]
         v_w1 = [placed([P, NT], U32, "v_w1%d" % j, at["tab0"] + 2 * KB * j) for j in range(2)]
-        wr_c = [placed([P, KP], I32, "wr_c0", at["tab1"]), placed([P, KP], I32, "wr_c1", at["tab2"])]
-        v2_w = [placed([P, 2 * NT], U8, "v2_w0", at["tab1"] + 4 * KB), placed([P, 2 * NT], U8, "v2_w1", at["wr"])]
+        wr_c = [held([P, KP], I32, "wr_c0"), placed([P, KP], I32, "wr_c1", at["tab2"])]
+        v2_w = [placed([P, 2 * NT], U8, "v2_w0", at["tab1"] + 4 * KB), placed([P, 2 * NT], U8, "v2_w1", at["tab1"] + 5 * KB)]
         half = NT // 16
 
         wm_bf = [[held([P, KP * PACK], BF16, "wm_bf00")[:], placed([P, KP * PACK], BF16, "wm_bf01", at["wm_bf01"])[:]],
@@ -312,10 +312,10 @@ def tile_list_attitude_propagation_kernel(
                 nc.vector.tensor_copy(
                     (v_w0, v_w1)[a][j][:], tab_w[a][:].bitcast(U32).indirect(idx[:, half * j : half * (j + 1)]))
         gather_v2(0)
-        nc.vector.tensor_copy(
-            wr_c[0][:].rearrange("p (t u i) -> p u t i", t=PACK, i=4),
-            wr_raw[0].rearrange("p (u i t) -> p u t i", t=PACK, i=4))
         gather_v2(1)
+        nc.scalar.copy(
+            wr_c[0][:].bitcast(U32).rearrange("p (t m) -> p m t", t=PACK),
+            wr_raw[0].bitcast(U32).rearrange("p (m t) -> p m t", t=PACK))
         nc.gpsimd.tensor_copy(
             wr_c[1][:].rearrange("p (t m) -> p t m", t=PACK), wr_raw[1].rearrange("p (m t) -> p t m", t=PACK))
 
@@ -334,8 +334,8 @@ def tile_list_attitude_propagation_kernel(
         cast_wm(1, 0, nc.scalar.copy)
         quant_wm(1, 0)
         cast_last_wm(0, nc.scalar.copy)
-        quant_last_wm(0)
         cast_last_wm(1, nc.vector.tensor_copy)
+        quant_last_wm(0)
         quant_last_wm(1)
         interleave_on_gpsimd(woven[0][0], planes[0][0], 0, GPSIMD_FIRST)
         interleave(nc.scalar.copy, woven[0][0], planes[0][0], GPSIMD_FIRST, NT)

@@ -66,7 +66,7 @@ def tile_list_attitude_propagation_kernel(
         wr_s_raw = second[:, 0:H]
         zero_in = held([P, 1], F32, "zero_in")
         zero = placed([P, (at["wn_bf0"] - at["wm_bf10"]) // 4 + 16], F32, "zero", at["wm_bf10"])[:, 0:1]
-        zero_late = placed([P, 1], F32, "zero_late", at["wn_bf1"])[:]
+        zero_late = placed([P, KB], F32, "zero_late", at["wn_bf1"])[:, 0:1]
         nc.gpsimd.memset(wr_s_raw.bitcast(I32), 0)
         nc.vector.memset(tab_s.bitcast(I32), 0)
         nc.vector.memset(tab2_s.bitcast(I32), 0)
@@ -165,7 +165,8 @@ def tile_list_attitude_propagation_kernel(
                 [held([P, KP], U32, "wm_c1%d" % a) for a in range(2)]]
         wm_s = [[placed([P, KP], U8, "wm_s0%d" % a, at["wr_s"] + KP * a) for a in range(2)],
                 [held([P, KP], U8, "wm_s1%d" % a) for a in range(2)]]
-        wn_bf = [placed([P, N * PACK], BF16, "wn_bf%d" % b, at["wn_bf%d" % b]) for b in range(2)]
+        wn_bf0 = placed([P, N * PACK], BF16, "wn_bf0", at["wn_bf0"])
+        wn_bf1 = [placed([P, NH * PACK], BF16, "wn_bf1_%d" % side, at["wn_bf1"] + 2 * KB * side) for side in range(2)]
         wn_c = [held([P, N], U32, "wn_c%d" % b) for b in range(2)]
         wn_s = [held([P, N], U8, "wn_s%d" % b) for b in range(2)]
         h_c = [[held([P, NT], U32, "h_c%d%d" % (b, j)) for j in range(2)] for b in range(2)]
@@ -208,8 +209,8 @@ def tile_list_attitude_propagation_kernel(
         def quant_h_part(b, j, part, lo, hi):
             nc.vector.quantize_mx(h_c[b][j][:, lo:hi].bitcast(FP8X4), h_s[b][j][:, lo:hi], part[:])
 
-        def quant_wn(b):
-            nc.vector.quantize_mx(wn_c[b][:].bitcast(FP8X4), wn_s[b][:], wn_bf[b][:])
+        def quant_wn(b, part, lo, hi):
+            nc.vector.quantize_mx(wn_c[b][:, lo:hi].bitcast(FP8X4), wn_s[b][:, lo:hi], part[:])
 
         def quant_h(b, j):
             nc.vector.quantize_mx(h_c[b][j][:].bitcast(FP8X4), h_s[b][j][:], woven[b][j][:])
@@ -339,7 +340,7 @@ def tile_list_attitude_propagation_kernel(
         quant_last_wm(1)
         interleave_on_gpsimd(woven[0][0], planes[0][0], 0, GPSIMD_FIRST)
         interleave(nc.scalar.copy, woven[0][0], planes[0][0], GPSIMD_FIRST, NT)
-        interleave(nc.vector.tensor_copy, wn_bf[0], wn_raw[0], 0, N)
+        interleave(nc.vector.tensor_copy, wn_bf0, wn_raw[0], 0, N)
         interleave_on_gpsimd(woven01[0], planes[0][1], 0, GPSIMD_SHARE)
         for t in range(PACK):
             open_phase(1, 0, t, PHASE_BANKS[t])
@@ -351,17 +352,19 @@ def tile_list_attitude_propagation_kernel(
             open_phase(1, 1, t, PHASE_BANKS[t])
             kick(1, 1, t)
         quant_h(0, 0)
-        quant_wn(0)
+        quant_wn(0, wn_bf0, 0, N)
         for t in range(PACK):
             old_rate(1, 1, t, RATE_BANKS[t])
             new_rate(1, 1, t)
         interleave_on_gpsimd(woven[1][0], planes[1][0], 0, GPSIMD_SHARE)
-        interleave(nc.scalar.copy, wn_bf[1], wn_raw[1], 0, N)
+        interleave(nc.scalar.copy, wn_bf1[0], wn_raw[1], 0, NH)
         interleave(nc.scalar.copy, woven[1][0], planes[1][0], GPSIMD_SHARE, NT)
+        interleave(nc.scalar.copy, wn_bf1[1], wn_raw[1][:, :, NH:N], 0, NH)
         interleave(nc.scalar.copy, woven01[1], planes[0][1][:, :, GPSIMD_SHARE:NT], 0, NT - GPSIMD_SHARE)
         interleave(nc.scalar.copy, woven[1][1], planes[1][1], GPSIMD_SHARE, NT)
-        quant_wn(1)
+        quant_wn(1, wn_bf1[0], 0, NH)
         quant_h(1, 0)
+        quant_wn(1, wn_bf1[1], NH, N)
         quant_h_part(0, 1, woven01[0], 0, GPSIMD_SHARE)
         quant_h_part(0, 1, woven01[1], GPSIMD_SHARE, NT)
         interleave(nc.vector.tensor_copy, woven[1][1], planes[1][1], 0, GPSIMD_SHARE)

@@ -143,11 +143,11 @@ def tile_list_attitude_propagation_kernel(
         load_wm(1, 1)
         load_wn(0)
         nc.sync.dma_start(wa_w[:].bitcast(I32), wa_words.bitcast(I32).rearrange("a p c -> p a c"))
-        load_wn(1)
         for q in range(4):
             nc.sync.dma_start(
                 wa_s[32 * q : 32 * q + 4, :, :].bitcast(I32),
                 wa_scales[:, 4 * q : 4 * q + 4, :].bitcast(I32).rearrange("a r n -> r a n"))
+        load_wn(1)
         with nc.allow_non_contiguous_dma(reason="one drift value a partition"):
             nc.sync.dma_start(drift_sb[:], drift.rearrange("(c p) -> p c", p=P))
 

from contextlib import ExitStack

import concourse.mybir as mybir

K, K2, T, S, H, N = 1024, 512, 4096, 1024, 1024, 512
FLOPS = 2 * S * (K * H + K2 * H + K * N + H * N)

F32 = mybir.dt.float32
BF16 = mybir.dt.bfloat16
I32 = mybir.dt.int32
U32 = mybir.dt.uint32
U16 = mybir.dt.uint16
U8 = mybir.dt.uint8
FP8X4 = mybir.dt.float8_e4m3fn_x4
FP4X4 = mybir.dt.float4_e2m1fn_x4
ACT = mybir.ActivationFunctionType
ALU = mybir.AluOpType

P = 128
PACK = 4
KP = P * PACK
NT = 512
NH = NT // 2
KB = 1024
GPSIMD_FIRST = 384
GPSIMD_SHARE = 384
RATE_BANKS = (0, 4, 5, 6)
PHASE_BANKS = (1, 2, 3, 7)


def tile_list_attitude_propagation_kernel(
    tc, tab_words, tab_scales, tab2_words, tab2_scales, offs, offs2,
    wa_words, wa_scales, wr_words, wr_scales, wm, wn, gain, drift, out,
):
    nc = tc.nc
    with ExitStack() as ctx:
        keep = ctx.enter_context(tc.tile_pool(name="keep", bufs=1))
        arena = ctx.enter_context(tc.tile_pool(name="arena", bufs=1))
        psum = ctx.enter_context(tc.psum_pool(name="psum", bufs=1))

        def held(shape, dtype, name):
            return keep.tile(shape, dtype, name=name, align_bytes=64)

        def placed(shape, dtype, name, at):
            return arena.tile(shape, dtype, name=name, align_bytes=64, offset=at)

        idx = keep.tile([P, S // 16], U16, name="idx")
        idx2 = keep.tile([P, S // 16], U16, name="idx2")

        at = {}
        end = 0
        for name, size in (
            ("tab_s", 4 * KB), ("tab1", 16 * KB), ("first_end", 0),
            ("wr_s", KB), ("tab2", 8 * KB), ("sine1", 8 * KB), ("wr1", 2 * KB), ("wm10", 8 * KB), ("wm11", 8 * KB),
            ("wn0", 8 * KB), ("wa", 2 * KB), ("wa_s", 2 * N), ("wn1", 8 * KB), ("drift", 64), ("late_end", 0),
            ("wm01", 8 * KB), ("tab0", 16 * KB), ("tab2_s", 4 * KB), ("wm_bf01", 4 * KB), ("sine0", 8 * KB),
            ("wm_bf10", 4 * KB), ("h_bf00", 4 * KB), ("wn_bf0", 4 * KB), ("wn_bf1", 4 * KB),
        ):
            at[name] = end
            end = end + size

        first = placed([P, at["first_end"]], U8, "first", 0)
        second = placed([P, at["late_end"] - at["wr_s"]], U8, "second", at["wr_s"])
        tab_s = first[:, 0:T]
        tab2_s = placed([P, T], U8, "tab2_s", at["tab2_s"])[:]
        wr_s_raw = second[:, 0:H]
        zero_in = held([P, 1], F32, "zero_in")
        zero = placed([P, (at["wn_bf0"] - at["wm_bf10"]) // 4 + 16], F32, "zero", at["wm_bf10"])[:, 0:1]
        zero_late = placed([P, KB], F32, "zero_late", at["wn_bf1"])[:, 0:1]
        nc.gpsimd.memset(wr_s_raw.bitcast(I32), 0)
        nc.vector.memset(tab_s.bitcast(I32), 0)
        nc.vector.memset(tab2_s.bitcast(I32), 0)
        zero_src = placed([P, 32], F32, "zero_src", at["tab0"] - 64)
        nc.vector.memset(zero_src[:, 0:1], 0.0)
        nc.vector.tensor_copy(zero_in[:], zero_src[:, 0:1])
        nc.vector.memset(zero_late, 0.0)

        wm_raw = [[held([P, PACK, KP], F32, "wm_raw00"), placed([P, PACK, KP], F32, "wm_raw01", at["wm01"])],
                  [placed([P, PACK, KP], F32, "wm_raw1%d" % a, at["wm1%d" % a]) for a in range(2)]]
        tab_w = [placed([P, T], I32, "tab_w%d" % a, at["tab%d" % a]) for a in range(2)]
        tab2_w = placed([P, T // 2], I32, "tab2_w", at["tab2"])
        wn_raw = [placed([P, PACK, N], F32, "wn_raw%d" % b, at["wn%d" % b]) for b in range(2)]
        wr_raw = [placed([P, PACK * KP], I32, "wr_raw0", at["sine1"])[:, 0:KP], placed([P, KP], I32, "wr_raw1", at["wr1"])[:]]
        wa_w = placed([P, 2, 2 * N], U8, "wa_w", at["wa"])
        gain_sb = held([P, 2, PACK], F32, "gain_sb")
        drift_sb = placed([P, N // P], F32, "drift_sb", at["drift"])
        stage = held([P, S + H], U8, "stage")
        v_plane = [held([P, S], U8, "v_plane%d" % a) for a in range(2)]
        plane_r = held([P, S + H], U8, "plane_r")
        wa_s = placed([P, 2, N], U8, "wa_s", at["wa_s"])
        v2_plane = plane_r[:, 0:S]
        wr_s = plane_r[:, S:]

        def load_wm(b, a):
            rows = wm[KP * a : KP * (a + 1), KP * b : KP * (b + 1)]
            nc.sync.dma_start(wm_raw[b][a][:], rows.rearrange("(p j) c -> p j c", j=PACK))

        def load_wn(b):
            rows = wn[KP * b : KP * (b + 1), :]
            nc.sync.dma_start(wn_raw[b][:], rows.rearrange("(p t) n -> p t n", t=PACK))

        def load_wr(b):
            words = wr_words[0][:, KP * b : KP * (b + 1), :]
            nc.sync.dma_start(wr_raw[b], words.rearrange("p c i -> p (c i)").bitcast(I32))

        def load_tab(a):
            nc.sync.dma_start(tab_w[a][:], tab_words[a].rearrange("p t i -> p (t i)").bitcast(I32))

        load_wm(0, 0)
        nc.sync.dma_start(idx[:], offs)
        nc.sync.dma_start(idx2[:], offs2)
        nc.sync.dma_start(
            first[0:P:4, 0:T].bitcast(I32), tab_scales.rearrange("a q t -> (a q) t").bitcast(I32))
        nc.sync.dma_start(tab2_s[64:P:4, :].bitcast(I32), tab2_scales[0].bitcast(I32))
        nc.scalar.activation(zero, zero_in[:], ACT.Sin)
        nc.sync.dma_start(second[64:P:4, 0:H].bitcast(I32), wr_scales[0].bitcast(I32))
        nc.gpsimd.dma_start(gain_sb[:], gain.rearrange("(b p t) -> p b t", b=2, t=PACK))

        load_wm(0, 1)
        load_tab(0)
        v_s = held([P, S], U8, "v_s")
        v2_s = held([P, S], U8, "v2_s")
        nc.vector.tensor_copy(v_s[:], tab_s.indirect(idx[:]))
        nc.vector.tensor_copy(v2_s[:], tab2_s.indirect(idx2[:]))
        nc.vector.tensor_copy(stage[:, 0:S].bitcast(I32), v2_s[:].bitcast(I32))
        nc.vector.tensor_copy(
            stage[:, S:].rearrange("p (b t m) -> p b t m", b=2, t=PACK),
            wr_s_raw.rearrange("p (b m t) -> p b t m", b=2, t=PACK))

        def move_rows(plane, spread, first_row):
            for r in range(4):
                lo = first_row + 4 * r
                nc.sync.dma_start(plane[r:P:32, :].bitcast(I32), spread[lo : lo + 49 : 16, :].bitcast(I32))

        move_rows(v_plane[0], v_s, 0)
        load_tab(1)
        move_rows(v_plane[1], v_s, 64)
        nc.sync.dma_start(tab2_w[:], tab2_words[0].bitcast(I32))
        move_rows(plane_r, stage, 64)
        load_wr(0)
        load_wr(1)
        load_wm(1, 0)
        load_wm(1, 1)
        load_wn(0)
        nc.sync.dma_start(wa_w[:].bitcast(I32), wa_words.bitcast(I32).rearrange("a p c -> p a c"))
        for q in range(4):
            nc.sync.dma_start(
                wa_s[32 * q : 32 * q + 4, :, :].bitcast(I32),
                wa_scales[:, 4 * q : 4 * q + 4, :].bitcast(I32).rearrange("a r n -> r a n"))
        load_wn(1)
        with nc.allow_non_contiguous_dma(reason="one drift value a partition"):
            nc.sync.dma_start(drift_sb[:], drift.rearrange("(c p) -> p c", p=P))

        v_w0 = [placed([P, NT], U32, "v_w0%d" % j, at["wm_bf01"] + 2 * KB * j) for j in range(2)]
        v_w1 = [placed([P, NT], U32, "v_w1%d" % j, at["tab0"] + 2 * KB * j) for j in range(2)]
        wr_c = [held([P, KP], I32, "wr_c0"), placed([P, KP], I32, "wr_c1", at["tab2"])]
        v2_w = [placed([P, 2 * NT], U8, "v2_w0", at["tab1"] + 4 * KB), placed([P, 2 * NT], U8, "v2_w1", at["tab1"] + 5 * KB)]
        half = NT // 16

        wm_bf = [[held([P, KP * PACK], BF16, "wm_bf00")[:], placed([P, KP * PACK], BF16, "wm_bf01", at["wm_bf01"])[:]],
                 [placed([P, KP * PACK], BF16, "wm_bf10", at["wm_bf10"])[:]]]
        wm_bf11 = [placed([P, KP * 2], BF16, "wm_bf11_0", at["wn_bf0"]),
                   placed([P, KP * 2], BF16, "wm_bf11_1", at["wm_bf10"])]
        wm_c = [[placed([P, KP], U32, "wm_c00", at["tab2_s"]), placed([P, KP], U32, "wm_c01", at["tab2_s"] + 2 * KB)],
                [held([P, KP], U32, "wm_c1%d" % a) for a in range(2)]]
        wm_s = [[placed([P, KP], U8, "wm_s0%d" % a, at["wr_s"] + KP * a) for a in range(2)],
                [held([P, KP], U8, "wm_s1%d" % a) for a in range(2)]]
        wn_bf0 = placed([P, N * PACK], BF16, "wn_bf0", at["wn_bf0"])
        wn_bf1 = [placed([P, NH * PACK], BF16, "wn_bf1_%d" % side, at["wn_bf1"] + 2 * KB * side) for side in range(2)]
        wn_c = [held([P, N], U32, "wn_c%d" % b) for b in range(2)]
        wn_s = [held([P, N], U8, "wn_s%d" % b) for b in range(2)]
        h_c = [[held([P, NT], U32, "h_c%d%d" % (b, j)) for j in range(2)] for b in range(2)]
        h_s = [[placed([P, NT], U8, "h_s00", at["wm_bf10"]), placed([P, NT], U8, "h_s01", at["sine1"] + 6 * KB)],
               [held([P, NT], U8, "h_s1%d" % j) for j in range(2)]]
        planes = [[held([P, PACK, NT], BF16, "h_planes%d%d" % (b, j)) for j in range(2)] for b in range(2)]
        woven = [[placed([P, NT * PACK], BF16, "h_bf00", at["h_bf00"]), None],
                 [placed([P, NT * PACK], BF16, "h_bf10", at["wn_bf0"]), held([P, NT * PACK], BF16, "h_bf11")]]

        woven01 = [placed([P, GPSIMD_SHARE * PACK], BF16, "h_bf01_0", at["wn0"]),
                   placed([P, (NT - GPSIMD_SHARE) * PACK], BF16, "h_bf01_1", at["wn1"])]

        def cast_wm(b, a, copy):
            copy(
                wm_bf[b][a].rearrange("p (t m j) -> p m j t", t=PACK, j=PACK),
                wm_raw[b][a][:].rearrange("p j (m t) -> p m j t", t=PACK))

        def quant_wm(b, a):
            nc.vector.quantize_mx(wm_c[b][a][:].bitcast(FP8X4), wm_s[b][a][:], wm_bf[b][a])

        def cast_last_wm(side, copy):
            copy(
                wm_bf11[side][:].rearrange("p (t m j) -> p m j t", t=2, j=PACK),
                wm_raw[1][1][:].rearrange("p j (m t) -> p m j t", t=PACK)[:, :, :, 2 * side : 2 * side + 2])

        def quant_last_wm(side):
            cols = slice(2 * P * side, 2 * P * (side + 1))
            nc.vector.quantize_mx(wm_c[1][1][:, cols].bitcast(FP8X4), wm_s[1][1][:, cols], wm_bf11[side][:])

        def interleave(copy, dst, src, lo, hi):
            copy(
                dst[:, PACK * lo : PACK * hi].rearrange("p (u i t) -> p u t i", i=4, t=PACK),
                src[:, :, lo:hi].rearrange("p t (u i) -> p u t i", i=4))

        def interleave_on_gpsimd(dst, src, lo, hi):
            nc.gpsimd.tensor_scalar(
                dst[:, PACK * lo : PACK * hi].rearrange("p (n t) -> p n t", t=PACK),
                src[:, :, lo:hi].rearrange("p t n -> p n t"), 1.0, 0.0, ALU.mult, ALU.add)

        def quant_h_part(b, j, part, lo, hi):
            nc.vector.quantize_mx(h_c[b][j][:, lo:hi].bitcast(FP8X4), h_s[b][j][:, lo:hi], part[:])

        def quant_wn(b, part, lo, hi):
            nc.vector.quantize_mx(wn_c[b][:, lo:hi].bitcast(FP8X4), wn_s[b][:, lo:hi], part[:])

        def quant_h(b, j):
            nc.vector.quantize_mx(h_c[b][j][:].bitcast(FP8X4), h_s[b][j][:], woven[b][j][:])

        def v_words(a, j):
            return (v_w0, v_w1)[a][j][:].bitcast(FP8X4)

        def bank(n, name):
            return psum.tile([P, NT], F32, name=name, tag="bank%d" % n)

        phases = {}
        sines = {}
        rates = {}
        acc = {}

        def phase_pass(b, j, t, a):
            cols = slice(P * t, P * (t + 1))
            nc.tensor.matmul_mx(
                phases[b, j, t][:], lhsT=wm_c[b][a][:, cols].bitcast(FP8X4), lhsT_scale=wm_s[b][a][:, cols],
                rhs=v_words(a, j), rhs_scale=v_plane[a][:, NT * j : NT * (j + 1)],
                start=(a == 0), stop=(a == 1))

        def open_phase(b, j, t, n):
            phases[b, j, t] = bank(n, "phase")
            phase_pass(b, j, t, 0)

        def kick(b, j, t):
            phase_pass(b, j, t, 1)
            sine = placed([P, NT], F32, "sine%d%d%d" % (b, j, t), at["sine%d" % j] + 2 * KB * t)
            nc.scalar.activation(sine[:], phases[b, j, t][:], ACT.Sin, bias=(zero, zero_late)[b], scale=-1.0)
            sines[b, j, t] = sine

        def old_rate(b, j, t, n):
            rates[b, j, t] = bank(n, "rate")
            cols = slice(KP * b + P * t, KP * b + P * (t + 1))
            nc.tensor.matmul_mx(
                rates[b, j, t][:], lhsT=wr_c[b][:, P * t : P * (t + 1)].bitcast(FP8X4), lhsT_scale=wr_s[:, cols],
                rhs=v2_w[j][:].bitcast(FP4X4), rhs_scale=v2_plane[:, NT * j : NT * (j + 1)], start=True, stop=True)

        def new_rate(b, j, t):
            nc.vector.scalar_tensor_tensor(
                planes[b][j][:, t, :], sines[b, j, t][:], gain_sb[:, b, t : t + 1], rates[b, j, t][:],
                ALU.mult, ALU.add)

        def open_angle(j, c, n):
            acc[j, c] = bank(n, "angle")
            for a in range(2):
                nc.tensor.matmul_mx(
                    acc[j, c][:], lhsT=wa_w[:, a, 2 * P * c : 2 * P * (c + 1)].bitcast(FP4X4),
                    lhsT_scale=wa_s[:, a, P * c : P * (c + 1)],
                    rhs=v_words(a, j), rhs_scale=v_plane[a][:, NT * j : NT * (j + 1)],
                    start=(a == 0), stop=False)

        def add_h(b, j, c):
            cols = slice(P * c, P * (c + 1))
            nc.tensor.matmul_mx(
                acc[j, c][:], lhsT=wn_c[b][:, cols].bitcast(FP8X4), lhsT_scale=wn_s[b][:, cols],
                rhs=h_c[b][j][:].bitcast(FP8X4), rhs_scale=h_s[b][j][:], start=False, stop=(b == 1))

        def finish(j, c):
            res = placed([P, NT], F32, "res%d%d" % (j, c), at["wm10"] + 2 * KB * (4 * j + c))
            if j == 1 and c % 2 == 0:
                nc.vector.tensor_scalar(res[:], acc[j, c][:], drift_sb[:, c : c + 1], None, ALU.add)
            else:
                nc.scalar.activation(res[:], acc[j, c][:], ACT.Identity, bias=drift_sb[:, c : c + 1])
            nc.sync.dma_start(out[P * c : P * (c + 1), NT * j : NT * (j + 1)], res[:])

        def close_in_halves(j, c, banks):
            cols = slice(P * c, P * (c + 1))
            for side, n in enumerate(banks):
                total = bank(n, "angle")[:, 0:NH]
                lo = NH * side
                for a in range(2):
                    nc.tensor.matmul_mx(
                        total, lhsT=wa_w[:, a, 2 * P * c : 2 * P * (c + 1)].bitcast(FP4X4),
                        lhsT_scale=wa_s[:, a, P * c : P * (c + 1)], rhs=v_words(a, j)[:, lo : lo + NH],
                        rhs_scale=v_plane[a][:, NT * j + lo : NT * j + lo + NH], start=(a == 0), stop=False)
                for b in range(2):
                    nc.tensor.matmul_mx(
                        total, lhsT=wn_c[b][:, cols].bitcast(FP8X4), lhsT_scale=wn_s[b][:, cols],
                        rhs=h_c[b][j][:, lo : lo + NH].bitcast(FP8X4), rhs_scale=h_s[b][j][:, lo : lo + NH],
                        start=False, stop=(b == 1))
                res = placed([P, NH], F32, "res_half%d" % side, at["wm10"] + 2 * KB * (4 * j + c) + KB * side)
                if side == 0:
                    nc.scalar.activation(res[:], total, ACT.Identity, bias=drift_sb[:, c : c + 1])
                else:
                    nc.vector.tensor_scalar(res[:], total, drift_sb[:, c : c + 1], None, ALU.add)
                nc.sync.dma_start(out[cols, NT * j + lo : NT * j + lo + NH], res[:])

        def gather_v2(j):
            nc.vector.tensor_copy(
                v2_w[j][:].bitcast(U16), tab2_w[:].bitcast(U16).indirect(idx2[:, half * j : half * (j + 1)]))

        for a in range(2):
            cast_wm(0, a, nc.scalar.copy)
        for a in range(2):
            quant_wm(0, a)
        for a in range(2):
            for j in range(2):
                nc.vector.tensor_copy(
                    (v_w0, v_w1)[a][j][:], tab_w[a][:].bitcast(U32).indirect(idx[:, half * j : half * (j + 1)]))
        gather_v2(0)
        gather_v2(1)
        nc.scalar.copy(
            wr_c[0][:].bitcast(U32).rearrange("p (t m) -> p m t", t=PACK),
            wr_raw[0].bitcast(U32).rearrange("p (m t) -> p m t", t=PACK))
        nc.gpsimd.tensor_copy(
            wr_c[1][:].rearrange("p (t m) -> p t m", t=PACK), wr_raw[1].rearrange("p (m t) -> p t m", t=PACK))

        for j in range(2):
            for t in range(PACK):
                open_phase(0, j, t, 4 * j + t)
        for j in range(2):
            for t in range(PACK):
                kick(0, j, t)
        for j in range(2):
            for t in range(PACK):
                old_rate(0, j, t, 4 * j + t)
                new_rate(0, j, t)
        for t in range(PACK):
            old_rate(1, 0, t, RATE_BANKS[t])
        cast_wm(1, 0, nc.scalar.copy)
        quant_wm(1, 0)
        cast_last_wm(0, nc.scalar.copy)
        cast_last_wm(1, nc.vector.tensor_copy)
        quant_last_wm(0)
        quant_last_wm(1)
        interleave_on_gpsimd(woven[0][0], planes[0][0], 0, GPSIMD_FIRST)
        interleave(nc.scalar.copy, woven[0][0], planes[0][0], GPSIMD_FIRST, NT)
        interleave(nc.vector.tensor_copy, wn_bf0, wn_raw[0], 0, N)
        interleave_on_gpsimd(woven01[0], planes[0][1], 0, GPSIMD_SHARE)
        for t in range(PACK):
            open_phase(1, 0, t, PHASE_BANKS[t])
        for t in range(PACK):
            kick(1, 0, t)
        for t in range(PACK):
            new_rate(1, 0, t)
        for t in range(PACK):
            open_phase(1, 1, t, PHASE_BANKS[t])
            kick(1, 1, t)
        quant_h(0, 0)
        quant_wn(0, wn_bf0, 0, N)
        for t in range(PACK):
            old_rate(1, 1, t, RATE_BANKS[t])
            new_rate(1, 1, t)
        interleave_on_gpsimd(woven[1][0], planes[1][0], 0, GPSIMD_SHARE)
        interleave(nc.scalar.copy, wn_bf1[0], wn_raw[1], 0, NH)
        interleave(nc.scalar.copy, woven[1][0], planes[1][0], GPSIMD_SHARE, NT)
        interleave(nc.scalar.copy, wn_bf1[1], wn_raw[1][:, :, NH:N], 0, NH)
        interleave(nc.scalar.copy, woven01[1], planes[0][1][:, :, GPSIMD_SHARE:NT], 0, NT - GPSIMD_SHARE)
        interleave(nc.scalar.copy, woven[1][1], planes[1][1], GPSIMD_SHARE, NT)
        quant_wn(1, wn_bf1[0], 0, NH)
        quant_h(1, 0)
        quant_wn(1, wn_bf1[1], NH, N)
        quant_h_part(0, 1, woven01[0], 0, GPSIMD_SHARE)
        quant_h_part(0, 1, woven01[1], GPSIMD_SHARE, NT)
        interleave(nc.vector.tensor_copy, woven[1][1], planes[1][1], 0, GPSIMD_SHARE)
        quant_h(1, 1)
        for c in range(4):
            open_angle(0, c, PHASE_BANKS[c])
        for c in range(4):
            add_h(0, 0, c)
        open_angle(1, 0, RATE_BANKS[0])
        for c in range(4):
            add_h(1, 0, c)
            finish(0, c)
        for c in range(1, 3):
            open_angle(1, c, RATE_BANKS[c])
        for c in range(3):
            add_h(0, 1, c)
            add_h(1, 1, c)
            finish(1, c)
        close_in_halves(1, 3, (RATE_BANKS[3], PHASE_BANKS[0]))
